import numpy as np, ml_dtypes
CORES = [66,74,82,90,194,202,210,218]
N = 8
import mx_ref
BF = ml_dtypes.bfloat16
def entries(a):
    return np.ascontiguousarray(a.T).reshape(-1)
def table(e):
    return np.ascontiguousarray(np.reshape(e, (-1, 16)).T).astype(np.int32)
def pick(q, e):
    c = np.concatenate([q[0].reshape(128, -1, 4), np.zeros((128, 1, 4), np.uint8)], axis=1); s = np.concatenate([q[1], np.ones((16, 1), np.uint8)], axis=1)
    return (np.ascontiguousarray(c[:, e].reshape(128, -1)), np.ascontiguousarray(s[:, e]))
def join(*qs):
    return (np.concatenate([q[0] for q in qs], axis=1), np.concatenate([q[1] for q in qs], axis=1))
def put(q, e, v):
    c, s = q[0].reshape(128, -1, 4).copy(), q[1].copy(); c[:, e] = v[0].reshape(128, -1, 4); s[:, e] = v[1]
    return (c.reshape(128, -1), s)
def pk(c, s):
    return (np.ascontiguousarray(c), mx_ref.live(s))
def emit(q):
    return q[0], q[1]
def cut(t, i, w=512):
    return t[:, w * i:w * i + w]
def f(rng, *shape):
    return mx_ref.flush((rng.standard_normal(shape, dtype=np.float32) * np.exp2(rng.integers(-2, 3, shape[:-1] + (1,)))).astype(BF))
def wide(rng, *shape, cols=0):
    v = rng.standard_normal(shape, dtype=np.float32) * np.exp2(rng.integers(-12, 13, shape)).astype(np.float32)
    if cols: v *= np.repeat(np.exp2(rng.integers(-cols, cols + 1, shape[:-2] + (1, shape[-1] // 4))) * (rng.random(shape[:-2] + (1, shape[-1] // 4)) > 0.0625), 4, axis=-1).astype(np.float32)
    return mx_ref.flush(v.astype(BF))
P, K, R, LC = 128, 16, 3, 24
def near(nb):
    return np.stack([entries(nb[r]).reshape(P, 3) for r in range(N)]).astype(np.int64)
def play(x, bb, nb, u, v, a):
    n = near(nb)
    X = join(*[mx_ref.quantize(np.ascontiguousarray(x[r])) for r in range(N)])
    qu, qv = mx_ref.quantize(np.ascontiguousarray(u[0])), mx_ref.quantize(np.ascontiguousarray(v[0]))
    qa = [[mx_ref.quantize(np.ascontiguousarray(cut(a[r], i))) for i in range(4)] for r in range(N)]
    fixed = [mx_ref.matmul(qv, mx_ref.quantize(np.ascontiguousarray(bb[r])))[0] for r in range(N)]
    b = bb.astype(np.float32).reshape(N, 128, P, 4)
    done, res, made = np.zeros((N, R, K), np.int64), [], []
    for t in range(R):
        e = mx_ref.matmul(qu, X)[0]
        new = []
        for r in range(N):
            z = ((e[n[r, :, 0]] + e[n[r, :, 1]]) + e[n[r, :, 2]]) - fixed[r]
            j = np.argsort(-np.abs(z), kind="stable")[:K]
            nbs = pick(X, n[r, j].T.reshape(-1))
            s = []
            for i in range(4):
                m = mx_ref.matmul(qa[r][i], nbs)
                s.append((m[:, :K] + m[:, K:2 * K]) + m[:, 2 * K:])
            g = np.float32(0.05) * np.stack(s, axis=2) + b[r][:, j]
            new.append(mx_ref.quantize(np.ascontiguousarray(g.reshape(128, -1).astype(BF))))
            done[r, t] = j
            res.append(z)
            made.append(g)
        X = put(X, np.concatenate([P * r + done[r, t] for r in range(N)]), join(*new))
    return X, done, np.stack(res), np.stack(made)
def fit(z, g):
    top = np.abs(g.astype(BF).astype(np.float32)).reshape(-1, 16, 8, K, 4).max(axis=(2, 4))
    g = np.abs(g)
    return bool(np.isfinite(z).all() and np.isfinite(g).all() and ((g == 0) | (g >= 2.0 ** -60) & (g <= 2.0 ** 60)).all() and ((top == 0) | (top >= 2.0 ** -30) & (top <= 2.0 ** 30)).all())
def bf(v):
    return mx_ref.flush(np.asarray(v, np.float32).astype(BF))
def lone(c):
    t = np.zeros((N, 128, 512), BF)
    t[:, :, :4] = c
    return t
def few(rng, q, n, free, most):
    p = rng.permutation(free)[:most]
    return q * P + rng.permutation(np.concatenate([p, p[rng.integers(0, p.size, P)]])[:n])
def graph(rng, src=None, free=None, most=LC):
    n = np.zeros((N, P, 3), np.int64)
    if free is None: free = [np.arange(P)] * N
    for r in range(N):
        n[r, :, :2] = r * P + rng.choice(free[r], (P, 2))
        s = (r + rng.integers(1, N, P)) % N if src is None else np.full(P, src[r])
        for q in range(N):
            i = np.flatnonzero(s == q)
            n[r, i, 2] = few(rng, q, i.size, free[q], most)
    return n
def stored(n):
    return np.stack([table(n[r].reshape(-1)) for r in range(N)])
def setup_inputs(rng):
    return {"x": f(rng, N, 128, 4 * P), "bb": f(rng, N, 128, 4 * P), "nb": stored(graph(rng)), "u": lone(f(rng, 128, 4)), "v": lone(f(rng, 128, 4)),
            "a": bf(f(rng, N, 128, 2048).astype(np.float32) * np.float32(2.0 ** -4)), "w": f(rng, N, 128, 512)}
def signs(rng):
    return 1.0 - 2.0 * rng.integers(0, 2, (128, 4))
def signed(rng, sg, size):
    return bf(((1 + rng.random((N, 128, P, 4))) * size[:, None, :, None] * sg[:, None, :] + 0.0).reshape(N, 128, 4 * P))
def single(rng, sg, size):
    return lone(bf((1 + rng.random((128, 4))) * sg * size))
def setup_inputs_again(rng):
    d, sg, size, m = setup_inputs(rng), signs(rng), np.zeros((N, P)), K // 8
    o = np.stack([rng.permutation(P) for r in range(N)])
    rest = np.sort(o[:, 7 * m:], axis=1)
    hold = np.stack([rng.permutation(rest[r, -5:]) for r in range(N)])
    n = graph(rng, free=rest[:, :-5], most=LC - 2)
    large, small = (1 + rng.random((128, 4))) * sg * 2.0 ** 20, (1 + rng.random((128, 4))) * sg * 2.0 ** -8
    top = np.arange(128)[:, None] < 64
    five = np.stack([large * top, large * ~top, -large, large, small], axis=1) + 0.0
    x = np.zeros((N, 128, P, 4))
    for r in range(N):
        x[r][:, hold[r]] = five
        h, left, both, alone = o[r, :4 * m], o[r, 4 * m:5 * m], o[r, 5 * m:6 * m], o[r, 6 * m:7 * m]
        size[r, h] = 64
        size[r, left] = 64
        n[r, h, 0] = r * P + rng.permutation(h)
        n[r, left, 0], n[r, left, 1] = r * P + hold[r, 0], r * P + hold[r, 1]
        n[r, both, 0], n[r, both, 1] = r * P + hold[r, 3], r * P + hold[r, 2]
        for i, k in ((left, 2), (both, 4), (alone, 4)):
            q = n[r, i, 2] // P
            n[r, i, 2] = q * P + hold[q, k]
    bb = signed(rng, sg, size).reshape(N, 128, P, 4)
    for r in range(N): bb[r][8:, o[r, 4 * m:5 * m]] = 0
    d.update(x=bf(x.reshape(N, 128, 4 * P)), bb=bb.reshape(N, 128, 4 * P), nb=stored(n), u=single(rng, sg, 1.0), v=single(rng, sg, 4.0))
    return d
def setup_inputs_far(rng):
    h = int(rng.integers(0, N))
    src = np.full(N, h)
    src[h] = (h + int(rng.integers(1, N))) % N
    d, n, sg, size = setup_inputs(rng), graph(rng, src), signs(rng), np.full((N, P), 2.0 ** 20)
    for r in range(N):
        first = np.unique(n[r, :, 2], return_index=True)[1]
        size[r, rng.permutation(first)[:K]] = 2.0 ** 26
    d.update(x=signed(rng, sg, np.full((N, P), 2.0 ** 20)), bb=signed(rng, sg, size), nb=stored(n), u=single(rng, sg, 2.0 ** 23), v=single(rng, sg, 2.0 ** 29))
    return d
def setup_inputs_moved(rng):
    d, n, sg, size = setup_inputs(rng), np.zeros((N, P, 3), np.int64), signs(rng), np.full((N, P), 2.0 ** -4)
    o = [rng.permutation(P) for r in range(N)]
    for r in range(N):
        size[r, o[r][:K]] = 64
        n[r, :, :2] = r * P + rng.choice(o[r][K:], (P, 2))
        m = np.zeros(P, bool)
        m[rng.permutation(P)[:K + K // 2]] = True
        s = (r + rng.integers(1, N, P)) % N
        for q in range(N):
            hot, cold = rng.permutation(o[q][:K])[:LC // 2], rng.permutation(o[q][K:])[:LC - LC // 2]
            i, k = np.flatnonzero((s == q) & m), np.flatnonzero((s == q) & ~m)
            n[r, i, 2] = q * P + rng.choice(hot, i.size)
            n[r, k, 2] = q * P + rng.choice(cold, k.size)
    d.update(x=signed(rng, sg, np.full((N, P), 2.0 ** -6)), bb=signed(rng, sg, size), nb=stored(n), u=single(rng, sg, 16.0), v=single(rng, sg, 1.0))
    return d
def setup_inputs_spread(rng):
    d = setup_inputs(rng)
    d["x"] = wide(rng, N, 128, 4 * P, cols=4)
    d["bb"] = wide(rng, N, 128, 4 * P, cols=4)
    return d
def setup_inputs_ties(rng):
    d, n = setup_inputs(rng), np.zeros((N, P, 3), np.int64)
    kind = np.stack([rng.permutation(np.arange(P) % 4) for r in range(N)])
    for k in ("x", "bb"):
        c = f(rng, 128, 8).astype(np.float32).reshape(128, 2, 4)
        d[k] = np.stack([bf((c[:, kind[r] >> 1] * (1 - 2 * (kind[r] & 1))[None, :, None]).reshape(128, -1)) for r in range(N)])
    for r in range(N):
        s = (r + rng.integers(1, N, P)) % N
        for k in range(4):
            i = np.flatnonzero(kind[r] == k)
            n[r, i, 0] = r * P + rng.choice(i, i.size)
            n[r, i, 1] = r * P + rng.choice(np.flatnonzero(kind[r] == (k ^ 2)), i.size)
            for q in range(N):
                j = i[s[i] == q]
                n[r, j, 2] = q * P + rng.choice(rng.permutation(np.flatnonzero(kind[q] == k))[:LC // 4], j.size)
    d["nb"] = stored(n)
    return d
def check_inputs(d):
    b = []
    for k in ("x", "bb", "u", "v", "a", "w"):
        t = np.abs(d[k].astype(np.float32))
        if not (np.isfinite(t).all() and ((t == 0) | (t >= 2.0 ** -30) & (t <= 2.0 ** 30)).all()): b.append("a value of " + k)
    for k in ("u", "v"):
        t = d[k].astype(np.float32)
        if (t[:, :, 4:] != 0).any(): b.append(k + " has numbers behind its column 0")
        if (t != t[:1]).any(): b.append(k + " isn't the same on all ranks")
    n = near(d["nb"])
    at, own = n // P, np.arange(N)[:, None, None]
    if n.min() < 0 or n.max() >= N * P or (at[:, :, :2] != own).any() or (at[:, :, 2] == own[:, :, 0]).any(): b.append("nb")
    elif any(np.unique(n[r, :, 2][at[r, :, 2] == q]).size > LC for r in range(N) for q in range(N)): b.append("nb names too many columns of one rank")
    if not b:
        try:
            with np.errstate(all="ignore"):
                X, done, z, g = play(d["x"], d["bb"], d["nb"], d["u"], d["v"], d["a"])
                good = fit(z, g)
        except Exception:
            good = False
        if not good: b.append("a number that the rounds make")
    return b
def reference(x, bb, nb, u, v, a, w):
    X, done, z, g = play(x, bb, nb, u, v, a)
    oc, osc, y = np.zeros((N, 128, 4 * P), np.uint8), np.zeros((N, 16, P), np.uint8), np.zeros((N, 128, P), np.float32)
    for r in range(N):
        q = pick(X, np.arange(P * r, P * r + P))
        oc[r], osc[r] = emit(q)
        y[r] = mx_ref.matmul(mx_ref.quantize(np.ascontiguousarray(w[r])), q)
    return {"oc": oc, "osc": osc, "nd": done.astype(np.float32), "y": y}

@@ -1,0 +1,563 @@
+import numpy as np
+from concourse.bass import DstId, RemoteDMATransfer
+from concourse.mybir import dt, AluOpType, AxisListType, ActivationFunctionType
+
+F32, I32, U16, B16, Q8, U8 = "float32", "int32", "uint16", "bfloat16", "float8_e4m3fn_x4", "uint8"
+P, K, R, LC = 128, 16, 3, 24
+SCRATCH = {}
+ALIAS = {}
+
+
+def _sb(kind, **names):
+    for k in names:
+        SCRATCH[k] = ("sbuf", [128, names[k]], kind)
+
+
+def _pack(kind, big, **names):
+    at = 0
+    for k in names:
+        ALIAS[k] = (big, at, names[k])
+        at += (names[k] + 7) // 8 * 8
+    SCRATCH[big] = ("sbuf", [128, at], kind)
+
+
+_pack(I32, "KI", PID=1, PM16i=1, PM32i=1, W1=1, W2=1, II=32, IO16=32, MJ=16, MJ2=16, MJ3=16, MJ4=16, MJ5=16, CNB=32, MJB=16)
+_pack(F32, "KF", PM16=1, PM32=1, PMR=3, MH=3, CI=8, CI128=8, NCI=8, FA=8, FB=8, FC=8, FD0=8, FO=8, GO=8, NGO=8, RS=8, RV=8,
+      G8=1, TSH=3, NTAU=8, NPM=1, BASE=8, PC=11, PVC=8, R3=1, LA1=1, LA2=1, LAB=4, CT=4, IX=1, LD=8, PMH=1, BC=4, NVC=4, OFFC=8,
+      KJ=32, CKA=32, CKB=32, CK=32, OXF=64, VAL=32)
+_pack(U16, "KU", FOU=8, RU=8, PU=24, NBU=24, CN=32, CIO=16, LN=16, NLD=32, FLD=16, LF=8, IDD=16, OFF8=8, PL=4, BO=8, JU=2, OX=64,
+      LFIN=8, JL=2)
+_sb(I32, NB=24, SF=144, SFL=144, AB=136, VL=256)
+_sb(F32, JT=1024, PLK=128, FRF=128, GR=128, JKA=768, JKB=896, CMR=256, NEQ=128, ABF=128, KAP=128, CMP=512, RLD=352, RLT=352, LABT=1024,
+    LBI=128, PIO=128, NBR=384, D3=256, POS=1024, PT=512, FT=256, UGT=256, NP=128, UPD=2048, UG=256, LT=256,
+    ETR=128, EXP=1024, ETAB=1024, E3=384, E01=128, E2=128, ZS=128,
+    NZ=128, RW=128, TR=128, SP=128, CM=512, JK4=512, MM=128, MT=128, GP=128, GPT=128, CC=128, T1=64, T2=64, T3=64,
+    NDB=48, FPD=256, FPT=256, YS=128)
+_sb(F32, ET=32)
+_sb(U16, RQ=12, RQIN=14, GL0=2, GL1=2, RI0=8, RI1=8)
+_sb(B16, xb=512, bbb=512, ub=16, vb=16, ab=2048, wb=512, UT=512, VT=512, XT=512, BG=64)
+for _n, _w in (("XQ", 128), ("NW", 512), ("BBQ", 128), ("UQ", 128), ("VQ", 128), ("AQ", 512), ("WQ", 128), ("SL", 224), ("FW", 1280),
+               ("PZ", 384), ("PX", 256), ("FIN", 128)):
+    SCRATCH[_n] = ("sbuf", [128, _w], Q8)
+    SCRATCH[_n + "S"] = ("sbuf", [128, _w], U8)
+BANKS = ("Z", "S0", "S1", "S2", "S3", "Y", "EB", "FB0")
+for _n in BANKS:
+    SCRATCH[_n] = ("psum", [128, 512], F32)
+SEMAPHORES = ["cv", "cs", "ct", "cp", "ln0", "ln1", "lx", "lb", "lu", "lv", "la", "lw", "ee", "rq", "rc", "rs", "loc",
+              "li0", "li1", "cd0", "cd1", "sc0", "sc1", "on", "oc", "os", "oy"]
+
+
+def rank_program(g, core, T, topo):
+    me = T.rank_of(core)
+    if me is None:
+        return
+    n = len(T.cores)
+    OP, FN, AX = AluOpType, ActivationFunctionType, AxisListType.X
+    E = {"v": g.vector, "s": g.scalar, "t": g.tensor, "p": g, "y": g.sync}
+    SEM = {"v": "cv", "s": "cs", "t": "ct", "p": "cp"}
+    clock = {e: {} for e in E}
+    total, recs = {}, {}
+
+    def norm(x):
+        return (x[0], 0, 512, 1) if x[0] in BANKS else x
+
+    def meet(a, b):
+        if a[1] >= b[2] or b[1] >= a[2]:
+            return False
+        return not (a[3] == b[3] and a[3] > 1 and (a[1] - b[1]) % a[3])
+
+    def sync(e, reads, writes):
+        toks = []
+        for kind, xs in (("r", reads), ("w", writes)):
+            for x in xs:
+                x = norm(x)
+                bank = x[0] in BANKS
+                for (y, k, tok, by) in recs.get(x[0], []):
+                    if bank and by == e == "t":
+                        continue
+                    if (kind == "w" or k == "w" or (bank and by != e)) and meet(x, y):
+                        toks.append(tok)
+        best = {}
+        for t in toks:
+            if clock[e].get(t[0], 0) < t[1] and best.get(t[0], (0, 0))[1] < t[1]:
+                best[t[0]] = t
+        for s in sorted(best):
+            t = best[s]
+            if any(o != s and best[o][2].get(s, 0) >= t[1] for o in best):
+                continue
+            E[e].wait_ge(T.sem[s], t[1])
+        for s in best:
+            for k in best[s][2]:
+                clock[e][k] = max(clock[e].get(k, 0), best[s][2][k])
+            clock[e][s] = max(clock[e].get(s, 0), best[s][1])
+
+    def note(e, tok, reads, writes):
+        for x in writes:
+            x = norm(x)
+            old = recs.setdefault(x[0], [])
+            if x[3] == 1 and x[0] not in BANKS:
+                old[:] = [r for r in old if not (x[1] <= r[0][1] and r[0][2] <= x[2])]
+            old.append((x, "w", tok, e))
+        for x in reads:
+            x = norm(x)
+            recs.setdefault(x[0], []).append((x, "r", tok, e))
+
+    def emit(e, fn, reads, writes):
+        reads = [x for x in reads if isinstance(x, tuple)]
+        sync(e, reads, writes)
+        s = SEM[e]
+        total[s] = total.get(s, 0) + 1
+        fn().then_inc(T.sem[s], 1)
+        snap = dict(clock[e])
+        snap[s] = total[s]
+        note(e, (s, total[s], snap), reads, writes)
+
+    def dma(q, s, pairs, reads, writes):
+        sync(q, reads, writes)
+        for o, i in pairs:
+            E[q].dma_start(o, i).then_inc(T.sem[s], 16)
+        total[s] = 16 * len(pairs)
+        snap = dict(clock[q])
+        snap[s] = total[s]
+        note("d", (s, total[s], snap), reads, writes)
+
+    def arrive(s, val, writes):
+        total[s] = val
+        note("r", (s, val, {s: val}), [], writes)
+
+    def X(name, lo=0, hi=None, st=1):
+        if name in ALIAS:
+            big, at, w = ALIAS[name]
+            return (big, at + lo, at + (w if hi is None else hi), st)
+        return (name, lo, SCRATCH[name][1][1] if hi is None else hi, st)
+
+    def ap(x):
+        if not isinstance(x, tuple):
+            return x
+        return T[x[0]][:, x[1]:x[2]] if x[3] == 1 else T[x[0]][:, x[1]:x[2]:x[3]]
+
+    def sc(x):
+        return (x[0] + "S", x[1], x[2], x[3])
+
+    def tt(o, a, b, op):
+        emit("v", lambda: g.vector.tensor_tensor(ap(o), ap(a), ap(b), op), [a, b], [o])
+
+    def ts(o, a, s1, op0, s2=None, op1=None):
+        if op1 is None:
+            emit("v", lambda: g.vector.tensor_scalar(ap(o), ap(a), ap(s1), None, op0), [a, s1], [o])
+        else:
+            emit("v", lambda: g.vector.tensor_scalar(ap(o), ap(a), ap(s1), ap(s2), op0, op1), [a, s1, s2], [o])
+
+    def tc(o, a):
+        emit("v", lambda: g.vector.tensor_copy(ap(o), ap(a)), [a], [o])
+
+    def tr(o, a):
+        emit("v", lambda: g.vector.transpose(ap(o), ap(a)), [a], [o])
+
+    def red(o, a):
+        emit("v", lambda: g.vector.tensor_reduce(ap(o), ap(a), AX, OP.add), [a], [o])
+
+    def fill(o, c):
+        emit("v", lambda: g.vector.memset(ap(o), c), [], [o])
+
+    def gat(o, win, off):
+        emit("v", lambda: g.vector.tensor_copy(ap(o), ap(win).indirect(ap(off))), [win, off], [o])
+
+    def sct(win, off, a):
+        emit("v", lambda: g.vector.tensor_copy(ap(win).indirect(ap(off)), ap(a)), [a, off], [win])
+
+    def act(o, a, f, bias=None, scale=None, acc=None, off=None):
+        kw = {}
+        if bias is not None:
+            kw["bias"] = ap(bias)
+        if scale is not None:
+            kw["scale"] = ap(scale)
+        if acc is not None:
+            kw["accum_out"] = ap(acc)
+
+        def go():
+            return g.scalar.activation(ap(o), ap(a) if off is None else ap(a).indirect(ap(off)), f, **kw)
+        emit("s", go, [a, bias, scale, off], [o] + ([acc] if acc is not None else []))
+
+    def quant(o, tile):
+        emit("v", lambda: g.vector.quantize_mx(ap(o), ap(sc(o)), ap(tile)), [tile], [o, sc(o)])
+
+    def pick(o, win, off):
+        emit("v", lambda: g.vector.tensor_copy(ap(o).bitcast(dt.uint32), ap(win).bitcast(dt.uint32).indirect(ap(off))),
+             [win, off], [o])
+        emit("s", lambda: g.scalar.activation(ap(sc(o)), ap(sc(win)).indirect(ap(off)), FN.Copy), [sc(win), off], [sc(o)])
+
+    def mm(bank, a, b, start=True, stop=True):
+        o = (bank, 0, b[2] - b[1], 1)
+        emit("t", lambda: g.tensor.matmul_mx(ap(o), ap(a), ap(sc(a)), ap(b), ap(sc(b)), start, stop),
+             [a, sc(a), b, sc(b)], [o])
+
+    def iota(o, pattern, cm=0, base=0):
+        emit("p", lambda: g.iota(ap(o), pattern, base, cm), [], [o])
+
+    def fiota(o, pattern, base=0):
+        emit("p", lambda: g.iota(ap(o), pattern, base, 0, allow_small_or_imprecise_dtypes=True), [], [o])
+
+    peers = [(me + 1 + i) % n for i in range(n - 1)]
+
+    def slot_at(s):
+        return (me - s - 1) % n
+
+    def dst(s):
+        rid, pid = topo.addr(T.cores[s], core)
+        return DstId(rid=rid, pnc=pid)
+
+    shared = topo.mask(core, T.cores[peers[0]])
+    for s in peers:
+        shared &= topo.mask(core, T.cores[s])
+
+    def bits(m):
+        return bin(m).count("1")
+
+    def each(plan, srcs, dsts, sem, reads):
+        sync("p", reads, [])
+        for call in plan:
+            trs = []
+            for i, es in call:
+                have = topo.engines(core, T.cores[peers[i]])
+                m = 0
+                for k in es:
+                    m |= 1 << have[k]
+                trs.append(RemoteDMATransfer(dst_ids=[dst(peers[i])], dma_engine_mask=m, remote_sem=T.sem[sem], src=srcs[i], dst=dsts[i]))
+                total["loc"] = total.get("loc", 0) + len(es)
+            g.remote_dma_fused(trs, local_sem=T.sem.loc)
+
+    def spread(src, dsts, sem, reads):
+        sync("p", reads, [])
+        total["loc"] = total.get("loc", 0) + bits(shared)
+        g.remote_dma_fused([RemoteDMATransfer(dst_ids=[dst(s) for s in peers], dma_engine_mask=shared, remote_sem=T.sem[sem],
+                                              srcs=[src], dsts=dsts)], local_sem=T.sem.loc)
+
+    ONE = [[(i, [i]) for i in range(7)]]
+    FOUR = [(i, [2 * i, 2 * i + 1]) for i in range(4)]
+    CODES = [FOUR, [(4, [0, 1]), (5, [2, 3]), (6, [4, 5, 6, 7])]]
+    SCALES = [FOUR, [(4, [4, 5]), (5, [6, 7]), (6, [0, 1, 2, 3])]]
+    u8 = dt.uint8
+
+    for q, s, lo in (("y", "ln0", 0), ("s", "ln1", 4)):
+        for k in range(lo, lo + 4):
+            E[q].dma_start(T.NB[16 * k:16 * k + 16, :], T.nb[:]).then_inc(T.sem[s], 16)
+        total[s] = 64
+    recs["NB"] = [(X("NB"), "w", (s, 64, {s: 64}), "d") for s in ("ln0", "ln1")]
+    dma("s", "lu", [(T.ub[:], T.u[:, 0:16])], [], [X("ub")])
+    dma("y", "lx", [(T.xb[:], T.x[:])], [], [X("xb")])
+    dma("s", "lv", [(T.vb[:], T.v[:, 0:16])], [], [X("vb")])
+    dma("y", "lb", [(T.bbb[:], T.bb[:])], [], [X("bbb")])
+    dma("y", "la", [(T.ab[:], T.a[:])], [], [X("ab")])
+    dma("y", "lw", [(T.wb[:], T.w[:])], [], [X("wb")])
+
+    iota(X("PID"), [[0, 1]], 1)
+    fiota(X("JT", 0, 256), [[1, 256]])
+    iota(X("II"), [[1, 32]])
+    fiota(X("OXF"), [[1, 32], [0, 2]])
+    wrap = n - 1 - me
+    for lo, hi, base in ((0, wrap, -P * (me + 1)), (wrap, 8, 0)):
+        if lo < hi and lo % 2:
+            fiota(X("BASE", lo, lo + 1), [[0, 1]], base - 8)
+            lo, base = lo + 1, base - P
+        if hi - lo > 1:
+            fiota(X("BASE", lo, hi - hi % 2), [[-2 * P, (hi - lo) // 2], [-P - 8, 2]], base)
+        if hi % 2 and lo < hi:
+            fiota(X("BASE", hi - 1, hi), [[0, 1]], base - P * (hi - 1 - lo))
+    iota(X("CNB"), [[1, 2], [48, 8], [0, 2]])
+    iota(X("MJB"), [[48, 8], [0, 2]], 0, 2)
+    fiota(X("OFFC"), [[256, 4], [0, 2]])
+    fiota(X("KJ"), [[1, 32]])
+    fill(X("SF", 0, 8), -1)
+    fill(X("SF", 8, 144), 0)
+    ts(X("PM16i"), X("PID"), 15, OP.bitwise_and)
+    ts(X("PM32i"), X("PID"), 31, OP.bitwise_and)
+    ts(X("W1"), X("PM16i"), 11, OP.mult)
+    tc(X("PM16"), X("PM16i"))
+    for h in range(3):
+        ts(X("PMR", h, h + 1), X("PM16i"), float(h - 2), OP.add)
+    ts(X("W2"), X("W1"), 5, OP.arith_shift_right)
+    ts(X("G8"), X("PM16"), 7.5, OP.is_gt)
+    for h in range(3):
+        ts(X("MH", h, h + 1), X("W2"), 3.0, OP.mult, X("PMR", h, h + 1), OP.is_equal)
+    ts(X("JT", 256, 512), X("JT", 0, 256), 256.0, OP.add)
+    ts(X("CI"), X("JT", 0, 128, 16), X("PM16"), OP.add)
+    ts(X("PLK"), X("JT", 0, 128), 1.0 / P, OP.mult)
+    ts(X("CI128"), X("CI"), 1.0 / P, OP.mult)
+    ts(X("NCI"), X("CI"), -1.0 / P, OP.mult)
+    ts(X("JT", 512, 1024), X("JT", 0, 512), 512.0, OP.add)
+    for b in range(4):
+        act(X("UT", b, 512, 4), X("JT", 0, 128), FN.Identity, bias=X("ub", b, b + 1), scale=0.0)
+
+    def shared_column(m):
+        ts(X("TSH", m, m + 1), X("G8"), float(P * (peers[2 * m + 1] - peers[2 * m]) - LC), OP.mult, X("PM16"), OP.add)
+
+    for h, o in enumerate(("FA", "FB", "FC")):
+        ts(X(o), X("NB", h, 24, 3), X("MH", h, h + 1), OP.mult)
+    tt(X("FD0"), X("FA"), X("FB"), OP.add)
+    shared_column(0)
+    tt(X("FO"), X("FD0"), X("FC"), OP.add)
+    shared_column(1)
+    tc(X("FOU"), X("FO"))
+    tt(X("GO"), X("FO"), X("CI128"), OP.add)
+    tt(X("NGO"), X("NCI"), X("FO"), OP.subtract)
+    emit("v", lambda: g.vector.tensor_tensor(ap(X("GR")), ap(X("JT")).indirect(ap(X("FOU"))), ap(X("PLK")), OP.add),
+         [X("JT"), X("FOU"), X("PLK")], [X("GR")])
+    act(X("FRF"), X("JT"), FN.Copy, off=X("FOU"))
+    NS = 6
+    for t in range(NS):
+        act(X("JKA", 128 * t, 128 * t + 128), X("GR"), FN.Sign, bias=X("NGO", t, t + 1), acc=X("RS", t, t + 1))
+    quant(X("XQ"), X("xb"))
+    quant(X("UQ"), X("UT"))
+    mm("EB", X("UQ"), X("XQ"))
+    for t in range(NS, 8):
+        ts(X("CMR", 128 * (t - NS), 128 * (t - NS) + 128), X("GR"), X("GO", t, t + 1), OP.is_lt)
+    tr(X("ETR"), X("EB", 0, 128))
+    for t in range(NS, 8):
+        red(X("RV", t, t + 1), X("CMR", 128 * (t - NS), 128 * (t - NS) + 128))
+    own = X("ET", 4 * me, 4 * me + 4)
+    tc(own, X("ETR", 0, 128, 32))
+    spread(ap(own), [ap(own) for s in peers], "ee", [own])
+    for lo, hi in ((0, 4 * me), (4 * me + 4, 32)):
+        if lo < hi:
+            arrive("ee", (n - 1) * bits(shared), [X("ET", lo, hi)])
+    fiota(X("LABT"), [[32, 64], [1, 16]])
+    fiota(X("POS", 768, 1024), [[64, 8], [0, 2], [4, 16]])
+    tc(X("RU", NS, 8), X("RV", NS, 8))
+    ts(X("RU", 0, NS), X("RS", 0, NS), -0.5, OP.mult, 63.5, OP.add)
+    ts(X("NPM"), X("PM16"), -1.0, OP.mult, 0.5, OP.add)
+    sct(X("SF", 8, 136), X("RU"), X("FRF"))
+    ts(X("NTAU"), X("BASE"), X("NPM"), OP.add)
+    ts(X("AB"), X("SF", 8, 144), 896, OP.bitwise_and)
+    tt(X("NEQ"), X("SF", 8, 136), X("SF", 7, 135), OP.not_equal)
+    tc(X("ABF"), X("AB", 0, 128))
+    shared_column(2)
+    emit("v", lambda: g.vector.tensor_tensor_scan(ap(X("KAP")), ap(X("NEQ")), ap(X("ABF")), -1.0, OP.add, OP.max),
+         [X("NEQ"), X("ABF")], [X("KAP")])
+    for i in range(n - 1):
+        c = 3 * (i // 2) + 2 * (i % 2)
+        act(X("JKB", 128 * i, 128 * i + 128), X("KAP"), FN.Sign, bias=X("NTAU", i, i + 1), acc=X("PC", c, c + 1))
+    for m in range(4):
+        than = X("TSH", m, m + 1) if m < 3 else X("PM16")
+        ts(X("CMP", 128 * m, 128 * m + 128), X("KAP"), P * peers[2 * m] + 16.0, OP.subtract, than, OP.is_lt)
+    for m in range(4):
+        red(X("PVC", m, m + 1), X("CMP", 128 * m, 128 * m + 128))
+    ts(X("SFL", 8, 144), X("SF", 8, 144), 127, OP.bitwise_and)
+    ts(X("PC", 1, 11, 3), X("PVC", 0, 4), -2.0, OP.mult, float(P), OP.add)
+    for d in range(2):
+        ts(X("PU", d, 22, 2), X("PC"), -0.5, OP.mult, 64.0, OP.add)
+    gat(X("RLD"), X("SFL", 8, 144), X("PU", 0, 22))
+    tr(X("RLT"), X("RLD"))
+    tc(X("RQ", 0, 11), X("RLT", 0, 352, 32))
+    first = [3 * (i // 2) + i % 2 for i in range(n - 1)]
+    each(ONE, [T.RQ[:, c:c + 2] for c in first],
+         [T.RQIN[:, 2 * slot_at(s):2 * slot_at(s) + 2] for s in peers], "rq", [X("RQ")])
+    fiota(X("UPD"), [[0, 2048]])
+    iota(X("VL"), [[1, 256]], 0, 1024)
+
+    tc(X("NBU"), X("NB"))
+    tc(X("OX"), X("OXF"))
+    ts(X("R3"), X("PM16"), 3.0, OP.mult)
+    for i, c in enumerate((2.0 ** -25, 1.0, float(-P * me))):
+        fill(X("BC", i, i + 1), c)
+    ts(X("CN"), X("CNB"), X("R3"), OP.add)
+    ts(X("NVC"), X("vb", 0, 4), -1.0, OP.mult)
+    for b in range(4):
+        act(X("VT", b, 512, 4), X("JT", 0, 128), FN.Identity, bias=X("NVC", b, b + 1), scale=0.0)
+    gat(X("NBR"), X("JT"), X("NBU"))
+    act(X("POS", 0, 512), X("NBR"), FN.Identity, bias=X("BC", 2, 3), off=X("CN"))
+    ts(X("MJ"), X("MJB"), X("R3"), OP.add)
+    quant(X("NW", 0, 128), X("xb"))
+    ts(X("MJ2"), X("MJ"), 4, OP.arith_shift_right)
+    quant(X("VQ"), X("VT"))
+    ts(X("MJ3"), X("MJ2"), 171, OP.mult)
+    quant(X("BBQ"), X("bbb"))
+    mm("FB0", X("VQ"), X("BBQ"))
+    ts(X("MJ4"), X("MJ3"), 9, OP.arith_shift_right)
+    ts(X("MJ2"), X("MJ"), 15, OP.bitwise_and)
+    ts(X("MJ5"), X("MJ4"), 16, OP.mult)
+    tt(X("MJ3"), X("MJ2"), X("MJ5"), OP.add)
+    tc(X("CIO"), X("MJ3"))
+    act(X("PIO"), X("KAP"), FN.Copy, off=X("RU"))
+    act(X("POS", 512, 768), X("PIO"), FN.Copy, off=X("CIO"))
+    tc(X("PM32"), X("PM32i"))
+    ts(X("PMH"), X("PM32"), -0.5, OP.add)
+    act(X("CKA"), X("KJ"), FN.Sign, bias=X("PMH"), scale=-1.0)
+    act(X("CKB"), X("CKA"), FN.Identity, bias=X("BC", 0, 1), scale=2.0 ** -25)
+    act(X("CK"), X("CKB"), FN.Identity, bias=X("BC", 1, 2), scale=-1.0)
+    ts(X("LA1"), X("PM32"), 16.0, OP.is_ge, 16.0, OP.mult)
+    ts(X("IO16"), X("II"), 15, OP.bitwise_and)
+    tt(X("LA2"), X("LA1"), X("PM32"), OP.add)
+    for b in range(4):
+        quant(X("AQ", 128 * b, 128 * b + 128), X("ab", 512 * b, 512 * b + 512))
+    ts(X("LAB"), X("JT", 0, 256, 64), X("LA2"), OP.add)
+    for b in range(2):
+        quant(X("PX", 128 * b, 128 * b + 128), X("xb"))
+    fill(X("XT"), 0.0)
+    tc(X("NP"), X("JT", 0, 128))
+
+    for h in range(2):
+        act(X("EXP", 512 * h, 512 * h + 512), X("ET"), FN.Copy, off=X("OX", 32 * h, 32 * h + 32))
+        tr(X("ETAB", 512 * h, 512 * h + 512), X("EXP", 512 * h, 512 * h + 512))
+
+    arrive("rq", n - 1, [X("RQIN")])
+    pick(X("SL"), X("XQ"), X("RQIN"))
+    blocks = []
+    for i in range(n - 1):
+        skip = 8 if slot_at(peers[i]) % 2 else 0
+        blocks.append((32 * i + skip, 32 * i + skip + LC))
+    land = (P * me, P * me + LC)
+    each(CODES, [T.SL[:, a:b].bitcast(u8) for a, b in blocks], [T.FW[:, land[0]:land[1]].bitcast(u8) for s in peers], "rc", [X("SL")])
+    each(SCALES, [T.SLS[:, a:b] for a, b in blocks], [T.FWS[:, land[0]:land[1]] for s in peers], "rs", [X("SLS")])
+    for s, w in (("rc", "FW"), ("rs", "FWS")):
+        arrive(s, sum(len(es) for call in CODES for i, es in call), [X(w, 0, 1024)])
+
+    gat(X("E3"), X("ETAB"), X("NBU"))
+    tt(X("E01"), X("E3", 0, 384, 3), X("E3", 1, 384, 3), OP.add)
+    tt(X("E2"), X("E01"), X("E3", 2, 384, 3), OP.add)
+    tt(X("ZS"), X("E2"), X("FB0", 0, 128), OP.add)
+
+    def near_sums():
+        pick(X("PZ", 0, 256), X("NW"), X("LN"))
+        mm("Z", X("UQ"), X("PZ", 0, 128), True, False)
+        mm("Z", X("UQ"), X("PZ", 128, 256), False, False)
+
+    c05 = float(np.float32(0.05))
+    TINY = 2.0 ** -100
+    for t in range(R):
+        fw = (1024, 1152, 1280)[t]
+        z = X("ZS")
+        if t:
+            pick(X("PZ", 256, 384), X("FW", 0, fw), X("LF"))
+            mm("Z", X("UQ"), X("PZ", 256, 384), False, False)
+            mm("Z", X("VQ"), X("BBQ"), False, True)
+            tt(X("POS", 512, 768), X("POS", 512, 768), X("UG"), OP.max)
+            z = X("Z", 0, 128)
+        ts(X("NZ"), z, -1.0, OP.mult, TINY, OP.max)
+        tt(X("RW"), z, X("NZ"), OP.max)
+        tr(X("TR"), X("RW"))
+        for k in range(4):
+            act(X("SP", 32 * k, 32 * k + 32), X("CK"), FN.Identity, scale=X("TR", 32 * k, 32 * k + 1))
+        for k in range(4):
+            a, b, c = 32 * k, 32 * k + 32, 128 * k
+            val = X("TR", a, a + 1)
+            if b < P:
+                ts(X("CM", c + b, c + P), X("RW", b, P), val, OP.is_gt)
+            if a:
+                ts(X("CM", c, c + a), X("RW", 0, a), val, OP.is_ge)
+            tt(X("CM", c + a, c + b), X("RW", a, b), X("SP", a, b), OP.is_gt)
+            if k < 3:
+                act(X("JK4", c, c + P), X("CM", c, c + P), FN.Identity, acc=X("CT", k, k + 1))
+            else:
+                red(X("CT", k, k + 1), X("CM", c, c + P))
+        for k in range(4):
+            ts(X("MM", 32 * k, 32 * k + 32), X("IO16"), X("CT", k, k + 1), OP.is_equal, X("LAB", k, k + 1), OP.mult)
+        tr(X("MT"), X("MM"))
+        red(X("IX"), X("MT"))
+        ts(X("OFF8"), X("OFFC"), X("IX"), OP.add)
+        if t < R - 1:
+            gl = "GL%d" % t
+            ts(X(gl, 0, 1), X("IX"), 256.0 * me, OP.add)
+            spread(T[gl][:, 0:1], [T["RI%d" % t][:, slot_at(s):slot_at(s) + 1] for s in peers], "li%d" % t, [X(gl, 0, 1)])
+        gat(X("GP"), X("POS"), X("OFF8"))
+        tr(X("GPT"), X("GP"))
+        tc(X("PL"), X("GPT", 0, 128, 32))
+        j4 = X("GPT", 96, 97)
+        pick(X("PX", 0, 32), X("NW", 0, 128 * (t + 1)), X("PL", 0, 2))
+        if t == 0:
+            for b in range(4):
+                mm("S%d" % b, X("AQ", 128 * b, 128 * b + 128), X("PX", 0, 128), True, False)
+                mm("S%d" % b, X("AQ", 128 * b, 128 * b + 128), X("PX", 16, 144), False, False)
+        else:
+            pick(X("PX", 32, 48), X("FW", 0, fw), X("PL", 2, 3))
+            for b in range(4):
+                mm("S%d" % b, X("AQ", 128 * b, 128 * b + 128), X("PX", 0, 128))
+        ts(X("BO", 0, 8, 2), X("JT", 0, 4), j4, OP.add)
+        for b in range(4):
+            act(X("BG", b, 64, 4), X("bbb"), FN.Copy, off=X("BO", 2 * b, 2 * b + 1))
+        if t < R - 1:
+            ts(X("JU", 0, 1), j4, 0.25, OP.mult)
+            sct(X("NP"), X("JU", 0, 1), X("JT", P * (t + 1), P * (t + 1) + K))
+        else:
+            for d in range(2):
+                ts(X("JL", d, d + 1), X("IX"), 16.0 * d, OP.add)
+            sct(X("FPD"), X("JL"), X("VAL"))
+        if t == 0:
+            tr(X("PT"), X("POS", 0, 512))
+            tc(X("NLD"), X("PT", 0, 512, 16))
+            tr(X("FT"), X("POS", 512, 768))
+            act(X("POS", 0, 512), X("NP"), FN.Copy, off=X("NLD"))
+            pick(X("PX", 32, 48), X("FW", 0, fw), X("PL", 2, 3))
+            for b in range(4):
+                mm("S%d" % b, X("AQ", 128 * b, 128 * b + 128), X("PX", 32, 160), False, True)
+            for b in range(4):
+                ts(X("T3", b, 64, 4), X("S%d" % b, 0, 16), c05, OP.mult)
+        else:
+            def one(b):
+                tt(X("T1", b, 64, 4), X("S%d" % b, 0, 16), X("CC", 32 * b, 32 * b + 16), OP.add)
+
+            def two(b):
+                tt(X("T2", b, 64, 4), X("T1", b, 64, 4), X("CC", 32 * b + 16, 32 * b + 32), OP.add)
+            for b in range(4):
+                act(X("CC", 32 * b, 32 * b + 32), X("S%d" % b, 16, 48), FN.Copy)
+            if t < R - 1:
+                act(X("POS", 0, 512), X("NP"), FN.Copy, off=X("NLD"))
+            one(0)
+            one(1)
+            two(0)
+            if t == R - 1:
+                tr(X("FPT"), X("FPD"))
+                tc(X("LFIN"), X("FPT", 0, 256, 32))
+            one(2)
+            two(1)
+            one(3)
+            two(2)
+            two(3)
+            ts(X("T3"), X("T2"), c05, OP.mult)
+        tt(X("XT", 0, 64), X("T3"), X("BG"), OP.add)
+        new = P * (t + 1)
+        quant(X("NW", new, new + 128), X("XT"))
+        if t < R - 1:
+            spread(T.NW[:, new:new + K].bitcast(u8),
+                   [T.FW[:, fw + K * slot_at(s):fw + K * slot_at(s) + K].bitcast(u8) for s in peers], "cd%d" % t, [X("NW", new, new + K)])
+            spread(T.NWS[:, new:new + K],
+                   [T.FWS[:, fw + K * slot_at(s):fw + K * slot_at(s) + K] for s in peers], "sc%d" % t, [X("NWS", new, new + K)])
+            if t == 0:
+                act(X("LBI"), X("LABT"), FN.Copy, off=X("FOU"))
+                act(X("D3"), X("LBI"), FN.Copy, off=X("CIO"))
+            tr(X("PT"), X("POS", 0, 512))
+            tc(X("LN"), X("PT", 0, 512, 32))
+            near_sums()
+            if t == 0:
+                tr(X("LT"), X("D3"))
+                tc(X("FLD"), X("LT", 0, 256, 16))
+            arrive("li%d" % t, (n - 1) * bits(shared), [X("RI%d" % t, 0, 7)])
+            sct(X("UPD"), X("RI%d" % t, 0, 7), X("VL", fw - 1024, fw - 1024 + 112))
+            gat(X("UG"), X("UPD"), X("FLD"))
+            tr(X("UGT"), X("UG"))
+            tt(X("LD"), X("FT", 0, 256, 32), X("UGT", 0, 256, 32), OP.max)
+            tc(X("LF"), X("LD"))
+            emit("v", lambda: g.vector.tensor_scalar(T.NDB[0:1, K * t:K * t + K], T.GP[0:1, 96:112], 0.25, None, OP.mult),
+                 [X("GP")], [X("NDB", K * t, K * t + K)])
+            if t == 0:
+                quant(X("WQ"), X("wb"))
+            else:
+                for d in range(2):
+                    tc(X("IDD", d, 16, 2), X("CI"))
+                gat(X("FPD"), X("NP"), X("IDD"))
+                ts(X("VAL"), X("IO16"), float(P * R), OP.add)
+            arrive("cd%d" % t, (n - 1) * bits(shared), [X("FW", fw, fw + 112)])
+            arrive("sc%d" % t, (n - 1) * bits(shared), [X("FWS", fw, fw + 112)])
+        else:
+            pick(X("FIN"), X("NW"), X("LFIN"))
+            mm("Y", X("WQ"), X("FIN"))
+            dma("y", "oc", [(T.oc[:], T.FIN[:].bitcast(u8))], [X("FIN")], [])
+            dma("y", "os", [(T.osc[4 * k:4 * k + 4, :], T.FINS[32 * k:32 * k + 4, :]) for k in range(4)], [X("FINS")], [])
+            tc(X("YS"), X("Y", 0, 128))
+            dma("s", "oy", [(T.y[:], T.YS[:])], [X("YS")], [])
+            emit("v", lambda: g.vector.tensor_scalar(T.NDB[0:1, K * t:K * t + K], T.GP[0:1, 96:112], 0.25, None, OP.mult),
+                 [X("GP")], [X("NDB", K * t, K * t + K)])
+            dma("s", "on", [(T.nd[:], T.NDB[0:1, :])], [X("NDB")], [])
+    for s in total:
+        if clock["p"].get(s, 0) < total[s]:
+            g.wait_ge(T.sem[s], total[s])

@@ -31,25 +31,85 @@ _sb(I32, NB=24, SF=144, SFL=144, AB=136, VL=256)
 _sb(F32, JT=1024, PLK=128, FRF=128, GR=128, JKA=768, JKB=896, CMR=256, NEQ=128, ABF=128, KAP=128, CMP=512, RLD=352, RLT=352, LABT=1024,
     LBI=128, PIO=128, NBR=384, D3=256, POS=1024, PT=512, FT=256, UGT=256, NP=128, UPD=2048, UG=256, LT=256,
     ETR=128, EXP=1024, ETAB=1024, E3=384, E01=128, E2=128, ZS=128,
-    NZ=128, RW=128, TR=128, SP=128, CM=512, JK4=512, MM=128, MT=128, GP=128, GPT=128, CC=128, T1=64, T2=64, T3=64,
+    RW=128, TR=128, SP=128, CM=512, JK4=512, MM=128, MT=128, GP=128, GPT=128, CC=128, T1=64, T2=64, T3=64,
     NDB=48, FPD=256, FPT=256, YS=128)
-_sb(F32, ET=32)
+_sb(F32, ET=32, HE=4)
 _sb(U16, RQ=12, RQIN=14, GL0=2, GL1=2, RI0=8, RI1=8)
 _sb(B16, xb=512, bbb=512, ub=16, vb=16, ab=2048, wb=512, UT=512, VT=512, XT=512, BG=64)
-for _n, _w in (("XQ", 128), ("NW", 512), ("BBQ", 128), ("UQ", 128), ("VQ", 128), ("AQ", 512), ("WQ", 128), ("SL", 224), ("FW", 1280),
-               ("PZ", 384), ("PX", 256), ("FIN", 128)):
+for _n, _w in (("NW", 512), ("BBQ", 128), ("UQ", 128), ("VQ", 128), ("AQ", 512), ("WQ", 128), ("SL", 224), ("FW", 1280),
+               ("PZ", 384), ("PX", 256), ("FIN", 128), ("H1", 224), ("H2", 16), ("H3", 16)):
     SCRATCH[_n] = ("sbuf", [128, _w], Q8)
     SCRATCH[_n + "S"] = ("sbuf", [128, _w], U8)
 BANKS = ("Z", "S0", "S1", "S2", "S3", "Y", "EB", "FB0")
 for _n in BANKS:
     SCRATCH[_n] = ("psum", [128, 512], F32)
 SEMAPHORES = ["cv", "cs", "ct", "cp", "ln0", "ln1", "lx", "lb", "lu", "lv", "la", "lw", "ee", "rq", "rc", "rs", "loc",
-              "li0", "li1", "cd0", "cd1", "sc0", "sc1", "on", "oc", "os", "oy"]
+              "li0", "li1", "cd0", "cd1", "sc0", "sc1", "on", "oc", "os", "oy", "h0", "h1", "h2", "h3"]
+FAR = (1024, 1152, 1280)
+LANDS = (("ee", "ee"), ("rc", "rs"), ("cd0", "sc0"), ("cd1", "sc1"))
+
+
+def ways(T, topo, r):
+    n, c = len(T.cores), T.cores[r]
+    others = [(r + 1 + i) % n for i in range(n - 1)]
+    order = [s for s in others if topo.same_plane(c, T.cores[s])] + [s for s in others if not topo.same_plane(c, T.cores[s])]
+    mine = [h for h in topo.cores_of(c) if h != c]
+    full = [h for h in mine if all(topo.may_write(h, T.cores[s]) for s in others)]
+    rest = [h for h in mine if h not in full]
+    return order, [(rest[0], 0, 0, 2), (rest[1], 0, 2, 1), (full[0], 0, 3, 2), (full[1], 0, 5, 2), (rest[2], 1, 0, 3), (full[2], 1, 3, 2)]
+
+
+def view(T, name, half, a, b):
+    return T[name + "S"][:, a:b] if half else T[name][:, a:b].bitcast(dt.uint8)
+
+
+def serve(g, core, T, topo, r, order, stage, half, lo, cnt, home):
+    n = len(T.cores)
+    sem = T.sem[LANDS[stage][half]]
+    jobs = []
+    for i in range(lo, lo + cnt):
+        s = order[i]
+        slot = (r - s - 1) % n
+        if stage == 0:
+            a = 4 * r + 2 * half
+            src, to = (T.ET[:, a:a + 2] if home else T.HE[:, 2 * half:2 * half + 2]), T.ET[:, a:a + 2]
+        elif stage == 1:
+            a = 32 * i + (8 if slot % 2 else 0)
+            src, to = view(T, "SL" if home else "H1", half, a, a + LC), view(T, "FW", half, P * r, P * r + LC)
+        else:
+            a, b = P * (stage - 1), FAR[stage - 2] + K * slot
+            src = view(T, "NW", half, a, a + K) if home else view(T, "H%d" % stage, half, 0, K)
+            to = view(T, "FW", half, b, b + K)
+        rid, pid = topo.addr(T.cores[s], core)
+        jobs.append((DstId(rid=rid, pnc=pid), src, to))
+    m = topo.mask(core, T.cores[order[lo]])
+    calls = [[j] for j in jobs] if stage == 1 else [jobs]
+    for call in calls:
+        g.remote_dma_fused([RemoteDMATransfer(dst_ids=[j[0] for j in call], dma_engine_mask=m, remote_sem=sem,
+                                              srcs=[call[0][1]], dsts=[j[2] for j in call])], local_sem=T.sem.loc)
+    return len(calls) * bin(m).count("1")
+
+
+def helper(g, core, T, topo):
+    for r in range(len(T.cores)):
+        if core not in topo.cores_of(T.cores[r]):
+            continue
+        order, plan = ways(T, topo, r)
+        for (h, half, lo, cnt) in plan:
+            if h != core:
+                continue
+            share = len(topo.engines(T.cores[r], h)) // len([1 for w in plan if w[1] == half])
+            sent = 0
+            for stage in range(4):
+                g.wait_ge(T.sem["h%d" % stage], share)
+                sent += serve(g, core, T, topo, r, order, stage, half, lo, cnt, False)
+            g.wait_ge(T.sem.loc, sent)
 
 
 def rank_program(g, core, T, topo):
     me = T.rank_of(core)
     if me is None:
+        helper(g, core, T, topo)
         return
     n = len(T.cores)
     OP, FN, AX = AluOpType, ActivationFunctionType, AxisListType.X
@@ -199,12 +259,13 @@ def rank_program(g, core, T, topo):
         emit("p", lambda: g.iota(ap(o), pattern, base, 0, allow_small_or_imprecise_dtypes=True), [], [o])
 
     peers = [(me + 1 + i) % n for i in range(n - 1)]
+    order, plan = ways(T, topo, me)
 
     def slot_at(s):
         return (me - s - 1) % n
 
-    def dst(s):
-        rid, pid = topo.addr(T.cores[s], core)
+    def dst(c):
+        rid, pid = topo.addr(c, core)
         return DstId(rid=rid, pnc=pid)
 
     shared = topo.mask(core, T.cores[peers[0]])
@@ -214,30 +275,37 @@ def rank_program(g, core, T, topo):
     def bits(m):
         return bin(m).count("1")
 
-    def each(plan, srcs, dsts, sem, reads):
-        sync("p", reads, [])
-        for call in plan:
-            trs = []
-            for i, es in call:
-                have = topo.engines(core, T.cores[peers[i]])
-                m = 0
-                for k in es:
-                    m |= 1 << have[k]
-                trs.append(RemoteDMATransfer(dst_ids=[dst(peers[i])], dma_engine_mask=m, remote_sem=T.sem[sem], src=srcs[i], dst=dsts[i]))
-                total["loc"] = total.get("loc", 0) + len(es)
-            g.remote_dma_fused(trs, local_sem=T.sem.loc)
-
     def spread(src, dsts, sem, reads):
         sync("p", reads, [])
         total["loc"] = total.get("loc", 0) + bits(shared)
-        g.remote_dma_fused([RemoteDMATransfer(dst_ids=[dst(s) for s in peers], dma_engine_mask=shared, remote_sem=T.sem[sem],
+        g.remote_dma_fused([RemoteDMATransfer(dst_ids=[dst(T.cores[s]) for s in peers], dma_engine_mask=shared, remote_sem=T.sem[sem],
                                               srcs=[src], dsts=dsts)], local_sem=T.sem.loc)
 
-    ONE = [[(i, [i]) for i in range(7)]]
-    FOUR = [(i, [2 * i, 2 * i + 1]) for i in range(4)]
-    CODES = [FOUR, [(4, [0, 1]), (5, [2, 3]), (6, [4, 5, 6, 7])]]
-    SCALES = [FOUR, [(4, [4, 5]), (5, [6, 7]), (6, [0, 1, 2, 3])]]
+    def hand(stage, reads):
+        for half in (1, 0):
+            sync("p", [reads[half]], [])
+            jobs = [w for w in plan if w[1] == half]
+            wide = 32 * max(w[3] for w in jobs)
+            trs = []
+            for k, (h, hf, lo, cnt) in enumerate(jobs):
+                have = topo.engines(core, h)
+                per = len(have) // len(jobs)
+                m = 0
+                for e in have[per * k:per * k + per]:
+                    m |= 1 << e
+                if stage == 0:
+                    src, to = T.ET[:, 4 * me + 2 * half:4 * me + 2 * half + 2], T.HE[:, 2 * half:2 * half + 2]
+                elif stage == 1:
+                    src, to = view(T, "SL", half, 32 * lo, 32 * lo + wide), view(T, "H1", half, 32 * lo, 32 * lo + wide)
+                else:
+                    src, to = view(T, "NW", half, P * (stage - 1), P * (stage - 1) + K), view(T, "H%d" % stage, half, 0, K)
+                trs.append(RemoteDMATransfer(dst_ids=[dst(h)], dma_engine_mask=m, remote_sem=T.sem["h%d" % stage], src=src, dst=to))
+                total["loc"] = total.get("loc", 0) + per
+            g.remote_dma_fused(trs, local_sem=T.sem.loc)
+        total["loc"] += serve(g, core, T, topo, me, order, stage, 1, n - 3, 2, True)
+
     u8 = dt.uint8
+    ALL = (n - 1) * bits(shared)
 
     for q, s, lo in (("y", "ln0", 0), ("s", "ln1", 4)):
         for k in range(lo, lo + 4):
@@ -268,6 +336,8 @@ def rank_program(g, core, T, topo):
     iota(X("MJB"), [[48, 8], [0, 2]], 0, 2)
     fiota(X("OFFC"), [[256, 4], [0, 2]])
     fiota(X("KJ"), [[1, 32]])
+    fiota(X("POS", 768, 1024), [[64, 8], [0, 2], [4, 16]])
+    iota(X("VL"), [[1, 256]], 0, 1024)
     fill(X("SF", 0, 8), -1)
     fill(X("SF", 8, 144), 0)
     ts(X("PM16i"), X("PID"), 15, OP.bitwise_and)
@@ -307,9 +377,9 @@ def rank_program(g, core, T, topo):
     NS = 6
     for t in range(NS):
         act(X("JKA", 128 * t, 128 * t + 128), X("GR"), FN.Sign, bias=X("NGO", t, t + 1), acc=X("RS", t, t + 1))
-    quant(X("XQ"), X("xb"))
+    quant(X("NW", 0, 128), X("xb"))
     quant(X("UQ"), X("UT"))
-    mm("EB", X("UQ"), X("XQ"))
+    mm("EB", X("UQ"), X("NW", 0, 128))
     for t in range(NS, 8):
         ts(X("CMR", 128 * (t - NS), 128 * (t - NS) + 128), X("GR"), X("GO", t, t + 1), OP.is_lt)
     tr(X("ETR"), X("EB", 0, 128))
@@ -317,12 +387,10 @@ def rank_program(g, core, T, topo):
         red(X("RV", t, t + 1), X("CMR", 128 * (t - NS), 128 * (t - NS) + 128))
     own = X("ET", 4 * me, 4 * me + 4)
     tc(own, X("ETR", 0, 128, 32))
-    spread(ap(own), [ap(own) for s in peers], "ee", [own])
+    hand(0, [own, own])
     for lo, hi in ((0, 4 * me), (4 * me + 4, 32)):
         if lo < hi:
-            arrive("ee", (n - 1) * bits(shared), [X("ET", lo, hi)])
-    fiota(X("LABT"), [[32, 64], [1, 16]])
-    fiota(X("POS", 768, 1024), [[64, 8], [0, 2], [4, 16]])
+            arrive("ee", 2 * ALL, [X("ET", lo, hi)])
     tc(X("RU", NS, 8), X("RV", NS, 8))
     ts(X("RU", 0, NS), X("RS", 0, NS), -0.5, OP.mult, 63.5, OP.add)
     ts(X("NPM"), X("PM16"), -1.0, OP.mult, 0.5, OP.add)
@@ -349,16 +417,21 @@ def rank_program(g, core, T, topo):
     gat(X("RLD"), X("SFL", 8, 144), X("PU", 0, 22))
     tr(X("RLT"), X("RLD"))
     tc(X("RQ", 0, 11), X("RLT", 0, 352, 32))
-    first = [3 * (i // 2) + i % 2 for i in range(n - 1)]
-    each(ONE, [T.RQ[:, c:c + 2] for c in first],
-         [T.RQIN[:, 2 * slot_at(s):2 * slot_at(s) + 2] for s in peers], "rq", [X("RQ")])
-    fiota(X("UPD"), [[0, 2048]])
-    iota(X("VL"), [[1, 256]], 0, 1024)
+    sync("p", [X("RQ")], [])
+    trs = []
+    for i, s in enumerate(peers):
+        c, at = 3 * (i // 2) + i % 2, 2 * ways(T, topo, s)[0].index(me)
+        trs.append(RemoteDMATransfer(dst_ids=[dst(T.cores[s])], dma_engine_mask=1 << topo.engines(core, T.cores[s])[i],
+                                     remote_sem=T.sem.rq, src=T.RQ[:, c:c + 2], dst=T.RQIN[:, at:at + 2]))
+    g.remote_dma_fused(trs, local_sem=T.sem.loc)
+    total["loc"] += n - 1
+    fiota(X("LABT"), [[32, 64], [1, 16]])
+    fiota(X("UPD", 0, 512), [[0, 512]])
 
     tc(X("NBU"), X("NB"))
     tc(X("OX"), X("OXF"))
     ts(X("R3"), X("PM16"), 3.0, OP.mult)
-    for i, c in enumerate((2.0 ** -25, 1.0, float(-P * me))):
+    for i, c in enumerate((2.0 ** -25, 1.0, float(-P * me), 2.0 ** -124)):
         fill(X("BC", i, i + 1), c)
     ts(X("CN"), X("CNB"), X("R3"), OP.add)
     ts(X("NVC"), X("vb", 0, 4), -1.0, OP.mult)
@@ -367,29 +440,27 @@ def rank_program(g, core, T, topo):
     gat(X("NBR"), X("JT"), X("NBU"))
     act(X("POS", 0, 512), X("NBR"), FN.Identity, bias=X("BC", 2, 3), off=X("CN"))
     ts(X("MJ"), X("MJB"), X("R3"), OP.add)
-    quant(X("NW", 0, 128), X("xb"))
+    quant(X("BBQ"), X("bbb"))
     ts(X("MJ2"), X("MJ"), 4, OP.arith_shift_right)
     quant(X("VQ"), X("VT"))
     ts(X("MJ3"), X("MJ2"), 171, OP.mult)
-    quant(X("BBQ"), X("bbb"))
     mm("FB0", X("VQ"), X("BBQ"))
+    tc(X("PM32"), X("PM32i"))
     ts(X("MJ4"), X("MJ3"), 9, OP.arith_shift_right)
     ts(X("MJ2"), X("MJ"), 15, OP.bitwise_and)
     ts(X("MJ5"), X("MJ4"), 16, OP.mult)
+    ts(X("PMH"), X("PM32"), -0.5, OP.add)
     tt(X("MJ3"), X("MJ2"), X("MJ5"), OP.add)
+    ts(X("LA1"), X("PM32"), 16.0, OP.is_ge, 16.0, OP.mult)
     tc(X("CIO"), X("MJ3"))
     act(X("PIO"), X("KAP"), FN.Copy, off=X("RU"))
     act(X("POS", 512, 768), X("PIO"), FN.Copy, off=X("CIO"))
-    tc(X("PM32"), X("PM32i"))
-    ts(X("PMH"), X("PM32"), -0.5, OP.add)
     act(X("CKA"), X("KJ"), FN.Sign, bias=X("PMH"), scale=-1.0)
     act(X("CKB"), X("CKA"), FN.Identity, bias=X("BC", 0, 1), scale=2.0 ** -25)
     act(X("CK"), X("CKB"), FN.Identity, bias=X("BC", 1, 2), scale=-1.0)
-    ts(X("LA1"), X("PM32"), 16.0, OP.is_ge, 16.0, OP.mult)
     ts(X("IO16"), X("II"), 15, OP.bitwise_and)
     tt(X("LA2"), X("LA1"), X("PM32"), OP.add)
-    for b in range(4):
-        quant(X("AQ", 128 * b, 128 * b + 128), X("ab", 512 * b, 512 * b + 512))
+    quant(X("AQ"), X("ab"))
     ts(X("LAB"), X("JT", 0, 256, 64), X("LA2"), OP.add)
     for b in range(2):
         quant(X("PX", 128 * b, 128 * b + 128), X("xb"))
@@ -401,18 +472,15 @@ def rank_program(g, core, T, topo):
         tr(X("ETAB", 512 * h, 512 * h + 512), X("EXP", 512 * h, 512 * h + 512))
 
     arrive("rq", n - 1, [X("RQIN")])
-    pick(X("SL"), X("XQ"), X("RQIN"))
-    blocks = []
-    for i in range(n - 1):
-        skip = 8 if slot_at(peers[i]) % 2 else 0
-        blocks.append((32 * i + skip, 32 * i + skip + LC))
-    land = (P * me, P * me + LC)
-    each(CODES, [T.SL[:, a:b].bitcast(u8) for a, b in blocks], [T.FW[:, land[0]:land[1]].bitcast(u8) for s in peers], "rc", [X("SL")])
-    each(SCALES, [T.SLS[:, a:b] for a, b in blocks], [T.FWS[:, land[0]:land[1]] for s in peers], "rs", [X("SLS")])
+    pick(X("SL"), X("NW", 0, 128), X("RQIN"))
+    hand(1, [X("SL"), X("SLS")])
+    fiota(X("UPD", 512, 2048), [[0, 1536]])
     for s, w in (("rc", "FW"), ("rs", "FWS")):
-        arrive(s, sum(len(es) for call in CODES for i, es in call), [X(w, 0, 1024)])
+        arrive(s, ALL, [X(w, 0, 1024)])
 
     gat(X("E3"), X("ETAB"), X("NBU"))
+    act(X("LBI"), X("LABT"), FN.Copy, off=X("FOU"))
+    act(X("D3"), X("LBI"), FN.Copy, off=X("CIO"))
     tt(X("E01"), X("E3", 0, 384, 3), X("E3", 1, 384, 3), OP.add)
     tt(X("E2"), X("E01"), X("E3", 2, 384, 3), OP.add)
     tt(X("ZS"), X("E2"), X("FB0", 0, 128), OP.add)
@@ -423,9 +491,8 @@ def rank_program(g, core, T, topo):
         mm("Z", X("UQ"), X("PZ", 128, 256), False, False)
 
     c05 = float(np.float32(0.05))
-    TINY = 2.0 ** -100
     for t in range(R):
-        fw = (1024, 1152, 1280)[t]
+        fw = FAR[t]
         z = X("ZS")
         if t:
             pick(X("PZ", 256, 384), X("FW", 0, fw), X("LF"))
@@ -433,8 +500,9 @@ def rank_program(g, core, T, topo):
             mm("Z", X("VQ"), X("BBQ"), False, True)
             tt(X("POS", 512, 768), X("POS", 512, 768), X("UG"), OP.max)
             z = X("Z", 0, 128)
-        ts(X("NZ"), z, -1.0, OP.mult, TINY, OP.max)
-        tt(X("RW"), z, X("NZ"), OP.max)
+        act(X("RW"), z, FN.Abs, bias=X("BC", 3, 4))
+        if t == 0:
+            tr(X("LT"), X("D3"))
         tr(X("TR"), X("RW"))
         for k in range(4):
             act(X("SP", 32 * k, 32 * k + 32), X("CK"), FN.Identity, scale=X("TR", 32 * k, 32 * k + 1))
@@ -482,14 +550,22 @@ def rank_program(g, core, T, topo):
             for d in range(2):
                 ts(X("JL", d, d + 1), X("IX"), 16.0 * d, OP.add)
             sct(X("FPD"), X("JL"), X("VAL"))
+
+        def numbers():
+            emit("s", lambda: g.scalar.activation(T.NDB[0:1, K * t:K * t + K], T.GP[0:1, 96:112], FN.Identity, scale=0.25),
+                 [X("GP")], [X("NDB", K * t, K * t + K)])
         if t == 0:
             tr(X("PT"), X("POS", 0, 512))
             tc(X("NLD"), X("PT", 0, 512, 16))
             tr(X("FT"), X("POS", 512, 768))
-            act(X("POS", 0, 512), X("NP"), FN.Copy, off=X("NLD"))
             pick(X("PX", 32, 48), X("FW", 0, fw), X("PL", 2, 3))
+            act(X("POS", 0, 512), X("NP"), FN.Copy, off=X("NLD"))
+            numbers()
             for b in range(4):
                 mm("S%d" % b, X("AQ", 128 * b, 128 * b + 128), X("PX", 32, 160), False, True)
+            tc(X("FLD"), X("LT", 0, 256, 16))
+            for d in range(2):
+                tc(X("IDD", d, 16, 2), X("CI"))
             for b in range(4):
                 ts(X("T3", b, 64, 4), X("S%d" % b, 0, 16), c05, OP.mult)
         else:
@@ -502,12 +578,17 @@ def rank_program(g, core, T, topo):
                 act(X("CC", 32 * b, 32 * b + 32), X("S%d" % b, 16, 48), FN.Copy)
             if t < R - 1:
                 act(X("POS", 0, 512), X("NP"), FN.Copy, off=X("NLD"))
+                quant(X("WQ"), X("wb"))
+                ts(X("VAL"), X("IO16"), float(P * R), OP.add)
+            else:
+                tr(X("FPT"), X("FPD"))
+                tc(X("LFIN"), X("FPT", 0, 256, 32))
+            numbers()
+            if t == R - 1:
+                dma("y", "on", [(T.nd[:], T.NDB[0:1, :])], [X("NDB")], [])
             one(0)
             one(1)
             two(0)
-            if t == R - 1:
-                tr(X("FPT"), X("FPD"))
-                tc(X("LFIN"), X("FPT", 0, 256, 32))
             one(2)
             two(1)
             one(3)
@@ -518,36 +599,20 @@ def rank_program(g, core, T, topo):
         new = P * (t + 1)
         quant(X("NW", new, new + 128), X("XT"))
         if t < R - 1:
-            spread(T.NW[:, new:new + K].bitcast(u8),
-                   [T.FW[:, fw + K * slot_at(s):fw + K * slot_at(s) + K].bitcast(u8) for s in peers], "cd%d" % t, [X("NW", new, new + K)])
-            spread(T.NWS[:, new:new + K],
-                   [T.FWS[:, fw + K * slot_at(s):fw + K * slot_at(s) + K] for s in peers], "sc%d" % t, [X("NWS", new, new + K)])
-            if t == 0:
-                act(X("LBI"), X("LABT"), FN.Copy, off=X("FOU"))
-                act(X("D3"), X("LBI"), FN.Copy, off=X("CIO"))
+            hand(2 + t, [X("NW", new, new + K), X("NWS", new, new + K)])
+            arrive("li%d" % t, ALL, [X("RI%d" % t, 0, 7)])
             tr(X("PT"), X("POS", 0, 512))
-            tc(X("LN"), X("PT", 0, 512, 32))
-            near_sums()
-            if t == 0:
-                tr(X("LT"), X("D3"))
-                tc(X("FLD"), X("LT", 0, 256, 16))
-            arrive("li%d" % t, (n - 1) * bits(shared), [X("RI%d" % t, 0, 7)])
             sct(X("UPD"), X("RI%d" % t, 0, 7), X("VL", fw - 1024, fw - 1024 + 112))
-            gat(X("UG"), X("UPD"), X("FLD"))
+            tc(X("LN"), X("PT", 0, 512, 32))
+            act(X("UG"), X("UPD"), FN.Copy, off=X("FLD"))
+            near_sums()
             tr(X("UGT"), X("UG"))
             tt(X("LD"), X("FT", 0, 256, 32), X("UGT", 0, 256, 32), OP.max)
             tc(X("LF"), X("LD"))
-            emit("v", lambda: g.vector.tensor_scalar(T.NDB[0:1, K * t:K * t + K], T.GP[0:1, 96:112], 0.25, None, OP.mult),
-                 [X("GP")], [X("NDB", K * t, K * t + K)])
-            if t == 0:
-                quant(X("WQ"), X("wb"))
-            else:
-                for d in range(2):
-                    tc(X("IDD", d, 16, 2), X("CI"))
-                gat(X("FPD"), X("NP"), X("IDD"))
-                ts(X("VAL"), X("IO16"), float(P * R), OP.add)
-            arrive("cd%d" % t, (n - 1) * bits(shared), [X("FW", fw, fw + 112)])
-            arrive("sc%d" % t, (n - 1) * bits(shared), [X("FWS", fw, fw + 112)])
+            if t:
+                act(X("FPD"), X("NP"), FN.Copy, off=X("IDD"))
+            arrive("cd%d" % t, ALL, [X("FW", fw, fw + 112)])
+            arrive("sc%d" % t, ALL, [X("FWS", fw, fw + 112)])
         else:
             pick(X("FIN"), X("NW"), X("LFIN"))
             mm("Y", X("WQ"), X("FIN"))
@@ -555,9 +620,6 @@ def rank_program(g, core, T, topo):
             dma("y", "os", [(T.osc[4 * k:4 * k + 4, :], T.FINS[32 * k:32 * k + 4, :]) for k in range(4)], [X("FINS")], [])
             tc(X("YS"), X("Y", 0, 128))
             dma("s", "oy", [(T.y[:], T.YS[:])], [X("YS")], [])
-            emit("v", lambda: g.vector.tensor_scalar(T.NDB[0:1, K * t:K * t + K], T.GP[0:1, 96:112], 0.25, None, OP.mult),
-                 [X("GP")], [X("NDB", K * t, K * t + K)])
-            dma("s", "on", [(T.nd[:], T.NDB[0:1, :])], [X("NDB")], [])
     for s in total:
         if clock["p"].get(s, 0) < total[s]:
             g.wait_ge(T.sem[s], total[s])

@@ -1,6 +1,6 @@
 import numpy as np
 from concourse.bass import DstId, RemoteDMATransfer
-from concourse.mybir import dt, AluOpType, AxisListType, ActivationFunctionType
+from concourse.mybir import dt, AluOpType, ActivationFunctionType
 
 F32, I32, U16, B16, Q8, U8 = "float32", "int32", "uint16", "bfloat16", "float8_e4m3fn_x4", "uint8"
 P, K, R, LC = 128, 16, 3, 24
@@ -17,36 +17,33 @@ def _pack(kind, big, **names):
     at = 0
     for k in names:
         ALIAS[k] = (big, at, names[k])
-        at += (names[k] + 7) // 8 * 8
+        at += (names[k] + 15) // 16 * 16
     SCRATCH[big] = ("sbuf", [128, at], kind)
 
 
-_pack(I32, "KI", PID=1, PM16i=1, PM32i=1, W1=1, W2=1, II=32, IO16=32, MJ=16, MJ2=16, MJ3=16, MJ4=16, MJ5=16, CNB=32, MJB=16)
-_pack(F32, "KF", PM16=1, PM32=1, PMR=3, MH=3, CI=8, CI128=8, NCI=8, FA=8, FB=8, FC=8, FD0=8, FO=8, GO=8, NGO=8, RS=8, RV=8,
-      G8=1, TSH=3, NTAU=8, NPM=1, BASE=8, PC=11, PVC=8, R3=1, LA1=1, LA2=1, LAB=4, CT=4, IX=1, LD=8, PMH=1, BC=4, NVC=4, OFFC=8,
-      KJ=32, CKA=32, CKB=32, CK=32, OXF=64, VAL=32)
-_pack(U16, "KU", FOU=8, RU=8, PU=24, NBU=24, CN=32, CIO=16, LN=16, NLD=32, FLD=16, LF=8, IDD=16, OFF8=8, PL=4, BO=8, JU=2, OX=64,
-      LFIN=8, JL=2)
-_sb(I32, NB=24, SF=144, SFL=144, AB=136, VL=256)
-_sb(F32, JT=1024, PLK=128, FRF=128, GR=128, JKA=768, JKB=896, CMR=256, NEQ=128, ABF=128, KAP=128, CMP=512, RLD=352, RLT=352, LABT=1024,
-    LBI=128, PIO=128, NBR=384, D3=256, POS=1024, PT=512, FT=256, UGT=256, NP=128, UPD=2048, UG=256, LT=256,
-    ETR=128, EXP=1024, ETAB=1024, E3=384, E01=128, E2=128, ZS=128,
-    RW=128, TR=128, SP=128, CM=512, JK4=512, MM=128, MT=128, GP=128, GPT=128, CC=128, T1=64, T2=64, T3=64,
-    NDB=48, FPD=256, FPT=256, YS=128)
-_sb(F32, ET=32, HE=4)
-_sb(U16, RQ=12, RQIN=14, GL0=2, GL1=2, RI0=8, RI1=8)
-_sb(B16, xb=512, bbb=512, ub=16, vb=16, ab=2048, wb=512, UT=512, VT=512, XT=512, BG=64)
-for _n, _w in (("NW", 512), ("BBQ", 128), ("UQ", 128), ("VQ", 128), ("AQ", 512), ("WQ", 128), ("SL", 224), ("FW", 1280),
-               ("PZ", 384), ("PX", 256), ("FIN", 128), ("H1", 224), ("H2", 16), ("H3", 16)):
+_pack(I32, "KI", PID=1, PM16i=1, PM32i=1, W3=1, P3=1, P3i=1, NO=24, COI=8, QOI=8)
+_pack(F32, "KF", PM16=1, PM32=1, PMH=1, R3=1, P3f=1, M3=1, C3=24, MASK=24, RST=24, A24=24, FS=24, NCI=8, NGO=8, GO=8, TAU=8, NTAU=8,
+      CNB=24, DUP=16, IO16=32, CK0=32, CK=32, ID32=32, LAB=4, Q4=4, O4=4, TINY=1, CT=4, ZA=4, ZT=4, GP=32, GPT=32)
+_pack(U16, "KU", FOU=8, RU=8, PU=14, NBU=24, CN=24, LN=16, CO=8, QO=8, FG=8, SO=8, LABD=8, EXO=8, BO=4, OF=4, PL=2, LF=8, LCU=8)
+_sb(I32, NB=24)
+_sb(F32, JT=1024, PLK=128, FRF=128, GR=128, CMR=384, RS1=512, RS2=448, SF=144, AB1=128, AB=128, NEQ=128, KAP=128, BROW=224, RLD=224,
+    RLT=224, NBR=384, ND=384, NT=384, FT=128, PIO=128, PN=128, PD0=128, PD1=128, PD2=128, PT=128, MSK=128, EG=128, EGT=128, ES=128,
+    E1T=128, NFT=128, ETR=128, RW=256, TR=128, SP=128, CM=512, CW=64, IW=64, T3=512, T4=64, BG=64, BGR=64, NDB=48, YS=128)
+_sb(F32, ET=32, HE=4, NVC=4)
+_sb(U16, RQ=14, RQIN=14, GL0=2, GL1=2, HL0=2, HL1=2, RI0=8, RI1=8)
+_sb(B16, xb=512, bbb=512, ub=16, vb=16, ab=2048, wb=512, UT=512, VT=512, XT=512, JK1=896, JK2=640, JK3=384, MM=128, MT=128, R32=128,
+    UPD=1024, NPB=384, CD=128, CDT=128)
+for _n, _w in (("NW0", 256), ("NW1", 256), ("NW2", 256), ("BBQ", 128), ("UQ", 128), ("VQ", 128), ("AQ", 512), ("WQ", 128), ("SL", 224),
+               ("FW", 1280), ("PZ", 384), ("PX", 160), ("FIN", 128), ("H1", 224), ("H2", 16), ("H3", 16)):
     SCRATCH[_n] = ("sbuf", [128, _w], Q8)
     SCRATCH[_n + "S"] = ("sbuf", [128, _w], U8)
 BANKS = ("Z", "S0", "S1", "S2", "S3", "Y", "EB", "FB0")
 for _n in BANKS:
     SCRATCH[_n] = ("psum", [128, 512], F32)
 SEMAPHORES = ["cv", "cs", "ct", "cp", "ln0", "ln1", "lx", "lb", "lu", "lv", "la", "lw", "ee", "rq", "rc", "rs", "loc",
-              "li0", "li1", "cd0", "cd1", "sc0", "sc1", "on", "oc", "os", "oy", "h0", "h1", "h2", "h3"]
-FAR = (1024, 1152, 1280)
-LANDS = (("ee", "ee"), ("rc", "rs"), ("cd0", "sc0"), ("cd1", "sc1"))
+              "li0", "li1", "cd0", "cd1", "sc0", "sc1", "on", "oc", "os", "oy", "h0", "h1", "h2", "h3", "h4", "h5"]
+FAR = (1024, 1136, 1248)
+LANDS = (("ee", "ee"), ("rc", "rs"), ("cd0", "sc0"), ("cd1", "sc1"), ("li0",), ("li1",))
 
 
 def ways(T, topo, r):
@@ -74,12 +71,13 @@ def serve(g, core, T, topo, r, order, stage, half, lo, cnt, home):
             a = 4 * r + 2 * half
             src, to = (T.ET[:, a:a + 2] if home else T.HE[:, 2 * half:2 * half + 2]), T.ET[:, a:a + 2]
         elif stage == 1:
-            a = 32 * i + (8 if slot % 2 else 0)
-            src, to = view(T, "SL" if home else "H1", half, a, a + LC), view(T, "FW", half, P * r, P * r + LC)
-        else:
-            a, b = P * (stage - 1), FAR[stage - 2] + K * slot
-            src = view(T, "NW", half, a, a + K) if home else view(T, "H%d" % stage, half, 0, K)
+            src, to = view(T, "SL" if home else "H1", half, 32 * i, 32 * i + LC), view(T, "FW", half, P * r, P * r + LC)
+        elif stage < 4:
+            b = FAR[stage - 2] + K * slot
+            src = view(T, "NW%d" % (stage - 2), half, P, P + K) if home else view(T, "H%d" % stage, half, 0, K)
             to = view(T, "FW", half, b, b + K)
+        else:
+            src, to = T["HL%d" % (stage - 4)][:, 0:1], T["RI%d" % (stage - 4)][:, slot:slot + 1]
         rid, pid = topo.addr(T.cores[s], core)
         jobs.append((DstId(rid=rid, pnc=pid), src, to))
     m = topo.mask(core, T.cores[order[lo]])
@@ -100,9 +98,10 @@ def helper(g, core, T, topo):
                 continue
             share = len(topo.engines(T.cores[r], h)) // len([1 for w in plan if w[1] == half])
             sent = 0
-            for stage in range(4):
-                g.wait_ge(T.sem["h%d" % stage], share)
-                sent += serve(g, core, T, topo, r, order, stage, half, lo, cnt, False)
+            for stage in (0, 1, 4, 2, 5, 3):
+                if half < len(LANDS[stage]):
+                    g.wait_ge(T.sem["h%d" % stage], share if stage else share // 2)
+                    sent += serve(g, core, T, topo, r, order, stage, half, lo, cnt, False)
             g.wait_ge(T.sem.loc, sent)
 
 
@@ -112,7 +111,7 @@ def rank_program(g, core, T, topo):
         helper(g, core, T, topo)
         return
     n = len(T.cores)
-    OP, FN, AX = AluOpType, ActivationFunctionType, AxisListType.X
+    OP, FN = AluOpType, ActivationFunctionType
     E = {"v": g.vector, "s": g.scalar, "t": g.tensor, "p": g, "y": g.sync}
     SEM = {"v": "cv", "s": "cs", "t": "ct", "p": "cp"}
     clock = {e: {} for e in E}
@@ -132,10 +131,10 @@ def rank_program(g, core, T, topo):
             for x in xs:
                 x = norm(x)
                 bank = x[0] in BANKS
-                for (y, k, tok, by) in recs.get(x[0], []):
-                    if bank and by == e == "t":
+                for (y, k, tok, who) in recs.get(x[0], []):
+                    if bank and who == e == "t":
                         continue
-                    if (kind == "w" or k == "w" or (bank and by != e)) and meet(x, y):
+                    if (kind == "w" or k == "w" or (bank and who != e)) and meet(x, y):
                         toks.append(tok)
         best = {}
         for t in toks:
@@ -196,11 +195,14 @@ def rank_program(g, core, T, topo):
             return x
         return T[x[0]][:, x[1]:x[2]] if x[3] == 1 else T[x[0]][:, x[1]:x[2]:x[3]]
 
+    def by(x, off):
+        return ap(x) if off is None else ap(x).indirect(ap(off))
+
     def sc(x):
         return (x[0] + "S", x[1], x[2], x[3])
 
-    def tt(o, a, b, op):
-        emit("v", lambda: g.vector.tensor_tensor(ap(o), ap(a), ap(b), op), [a, b], [o])
+    def tt(o, a, b, op, off=None):
+        emit("v", lambda: g.vector.tensor_tensor(ap(o), by(a, off), ap(b), op), [a, b, off], [o])
 
     def ts(o, a, s1, op0, s2=None, op1=None):
         if op1 is None:
@@ -208,20 +210,20 @@ def rank_program(g, core, T, topo):
         else:
             emit("v", lambda: g.vector.tensor_scalar(ap(o), ap(a), ap(s1), ap(s2), op0, op1), [a, s1, s2], [o])
 
-    def tc(o, a):
-        emit("v", lambda: g.vector.tensor_copy(ap(o), ap(a)), [a], [o])
+    def tc(o, a, off=None):
+        emit("v", lambda: g.vector.tensor_copy(ap(o), by(a, off)), [a, off], [o])
 
     def tr(o, a):
         emit("v", lambda: g.vector.transpose(ap(o), ap(a)), [a], [o])
 
-    def red(o, a):
-        emit("v", lambda: g.vector.tensor_reduce(ap(o), ap(a), AX, OP.add), [a], [o])
+    def scan(o, a, b, first, op0, op1):
+        emit("v", lambda: g.vector.tensor_tensor_scan(ap(o), ap(a), ap(b), first, op0, op1), [a, b], [o])
+
+    def add_up(o, a, first):
+        scan(o, (a[0], a[1], a[1] + 64, 1), (a[0], a[1] + 64, a[2], 1), first, OP.add, OP.add)
 
     def fill(o, c):
         emit("v", lambda: g.vector.memset(ap(o), c), [], [o])
-
-    def gat(o, win, off):
-        emit("v", lambda: g.vector.tensor_copy(ap(o), ap(win).indirect(ap(off))), [win, off], [o])
 
     def sct(win, off, a):
         emit("v", lambda: g.vector.tensor_copy(ap(win).indirect(ap(off)), ap(a)), [a, off], [win])
@@ -234,10 +236,7 @@ def rank_program(g, core, T, topo):
             kw["scale"] = ap(scale)
         if acc is not None:
             kw["accum_out"] = ap(acc)
-
-        def go():
-            return g.scalar.activation(ap(o), ap(a) if off is None else ap(a).indirect(ap(off)), f, **kw)
-        emit("s", go, [a, bias, scale, off], [o] + ([acc] if acc is not None else []))
+        emit("s", lambda: g.scalar.activation(ap(o), by(a, off), f, **kw), [a, bias, scale, off], [o] + ([acc] if acc is not None else []))
 
     def quant(o, tile):
         emit("v", lambda: g.vector.quantize_mx(ap(o), ap(sc(o)), ap(tile)), [tile], [o, sc(o)])
@@ -258,11 +257,11 @@ def rank_program(g, core, T, topo):
     def fiota(o, pattern, base=0):
         emit("p", lambda: g.iota(ap(o), pattern, base, 0, allow_small_or_imprecise_dtypes=True), [], [o])
 
-    peers = [(me + 1 + i) % n for i in range(n - 1)]
-    order, plan = ways(T, topo, me)
+    def A(b):
+        return X("AQ", P * b, P * b + P)
 
-    def slot_at(s):
-        return (me - s - 1) % n
+    peers = [s for s in range(n) if s != me]
+    order, plan = ways(T, topo, me)
 
     def dst(c):
         rid, pid = topo.addr(c, core)
@@ -271,18 +270,10 @@ def rank_program(g, core, T, topo):
     shared = topo.mask(core, T.cores[peers[0]])
     for s in peers:
         shared &= topo.mask(core, T.cores[s])
-
-    def bits(m):
-        return bin(m).count("1")
-
-    def spread(src, dsts, sem, reads):
-        sync("p", reads, [])
-        total["loc"] = total.get("loc", 0) + bits(shared)
-        g.remote_dma_fused([RemoteDMATransfer(dst_ids=[dst(T.cores[s]) for s in peers], dma_engine_mask=shared, remote_sem=T.sem[sem],
-                                              srcs=[src], dsts=dsts)], local_sem=T.sem.loc)
+    ALL = (n - 1) * bin(shared).count("1")
 
     def hand(stage, reads):
-        for half in (1, 0):
+        for half in range(len(LANDS[stage]) - 1, -1, -1):
             sync("p", [reads[half]], [])
             jobs = [w for w in plan if w[1] == half]
             wide = 32 * max(w[3] for w in jobs)
@@ -290,335 +281,289 @@ def rank_program(g, core, T, topo):
             for k, (h, hf, lo, cnt) in enumerate(jobs):
                 have = topo.engines(core, h)
                 per = len(have) // len(jobs)
-                m = 0
-                for e in have[per * k:per * k + per]:
-                    m |= 1 << e
-                if stage == 0:
-                    src, to = T.ET[:, 4 * me + 2 * half:4 * me + 2 * half + 2], T.HE[:, 2 * half:2 * half + 2]
-                elif stage == 1:
+                if stage == 1:
                     src, to = view(T, "SL", half, 32 * lo, 32 * lo + wide), view(T, "H1", half, 32 * lo, 32 * lo + wide)
+                elif stage < 4:
+                    src, to = view(T, "NW%d" % (stage - 2), half, P, P + K), view(T, "H%d" % stage, half, 0, K)
                 else:
-                    src, to = view(T, "NW", half, P * (stage - 1), P * (stage - 1) + K), view(T, "H%d" % stage, half, 0, K)
-                trs.append(RemoteDMATransfer(dst_ids=[dst(h)], dma_engine_mask=m, remote_sem=T.sem["h%d" % stage], src=src, dst=to))
-                total["loc"] = total.get("loc", 0) + per
+                    src, to = T["GL%d" % (stage - 4)][:, 0:1], T["HL%d" % (stage - 4)][:, 0:1]
+                trs.append(RemoteDMATransfer(dst_ids=[dst(h)], dma_engine_mask=sum(1 << e for e in have[per * k:per * k + per]),
+                                             remote_sem=T.sem["h%d" % stage], src=src, dst=to))
+                total["loc"] += per
             g.remote_dma_fused(trs, local_sem=T.sem.loc)
-        total["loc"] += serve(g, core, T, topo, me, order, stage, 1, n - 3, 2, True)
+        if stage < 4:
+            total["loc"] += serve(g, core, T, topo, me, order, stage, 1, n - 3, 2, True)
 
     u8 = dt.uint8
-    ALL = (n - 1) * bits(shared)
 
+    dma("s", "lu", [(T.ub[:], T.u[:, 0:16])], [], [X("ub")])
     for q, s, lo in (("y", "ln0", 0), ("s", "ln1", 4)):
         for k in range(lo, lo + 4):
             E[q].dma_start(T.NB[16 * k:16 * k + 16, :], T.nb[:]).then_inc(T.sem[s], 16)
         total[s] = 64
     recs["NB"] = [(X("NB"), "w", (s, 64, {s: 64}), "d") for s in ("ln0", "ln1")]
-    dma("s", "lu", [(T.ub[:], T.u[:, 0:16])], [], [X("ub")])
     dma("y", "lx", [(T.xb[:], T.x[:])], [], [X("xb")])
     dma("s", "lv", [(T.vb[:], T.v[:, 0:16])], [], [X("vb")])
     dma("y", "lb", [(T.bbb[:], T.bb[:])], [], [X("bbb")])
     dma("y", "la", [(T.ab[:], T.a[:])], [], [X("ab")])
-    dma("y", "lw", [(T.wb[:], T.w[:])], [], [X("wb")])
 
     iota(X("PID"), [[0, 1]], 1)
     fiota(X("JT", 0, 256), [[1, 256]])
-    iota(X("II"), [[1, 32]])
-    fiota(X("OXF"), [[1, 32], [0, 2]])
-    wrap = n - 1 - me
-    for lo, hi, base in ((0, wrap, -P * (me + 1)), (wrap, 8, 0)):
-        if lo < hi and lo % 2:
-            fiota(X("BASE", lo, lo + 1), [[0, 1]], base - 8)
-            lo, base = lo + 1, base - P
-        if hi - lo > 1:
-            fiota(X("BASE", lo, hi - hi % 2), [[-2 * P, (hi - lo) // 2], [-P - 8, 2]], base)
-        if hi % 2 and lo < hi:
-            fiota(X("BASE", hi - 1, hi), [[0, 1]], base - P * (hi - 1 - lo))
-    iota(X("CNB"), [[1, 2], [48, 8], [0, 2]])
-    iota(X("MJB"), [[48, 8], [0, 2]], 0, 2)
-    fiota(X("OFFC"), [[256, 4], [0, 2]])
-    fiota(X("KJ"), [[1, 32]])
-    fiota(X("POS", 768, 1024), [[64, 8], [0, 2], [4, 16]])
-    iota(X("VL"), [[1, 256]], 0, 1024)
-    fill(X("SF", 0, 8), -1)
-    fill(X("SF", 8, 144), 0)
+    fiota(X("C3"), [[0, 8], [1, 3]])
+    for lo, hi in ((0, me), (me, n - 1)):
+        if lo < hi:
+            fiota(X("BROW", 32 * lo, 32 * hi), [[P, hi - lo], [0, 32]], P * peers[lo])
+    fiota(X("CNB"), [[1, 3], [96, 4], [0, 2]])
+    fiota(X("DUP"), [[1, 8], [0, 2]])
+    fiota(X("IO16"), [[0, 2], [1, 16]])
+    fill(X("SF"), -1000.0)
     ts(X("PM16i"), X("PID"), 15, OP.bitwise_and)
     ts(X("PM32i"), X("PID"), 31, OP.bitwise_and)
-    ts(X("W1"), X("PM16i"), 11, OP.mult)
+    fill(X("TINY"), 2.0 ** -124)
     tc(X("PM16"), X("PM16i"))
-    for h in range(3):
-        ts(X("PMR", h, h + 1), X("PM16i"), float(h - 2), OP.add)
-    ts(X("W2"), X("W1"), 5, OP.arith_shift_right)
-    ts(X("G8"), X("PM16"), 7.5, OP.is_gt)
-    for h in range(3):
-        ts(X("MH", h, h + 1), X("W2"), 3.0, OP.mult, X("PMR", h, h + 1), OP.is_equal)
-    ts(X("JT", 256, 512), X("JT", 0, 256), 256.0, OP.add)
-    ts(X("CI"), X("JT", 0, 128, 16), X("PM16"), OP.add)
-    ts(X("PLK"), X("JT", 0, 128), 1.0 / P, OP.mult)
-    ts(X("CI128"), X("CI"), 1.0 / P, OP.mult)
-    ts(X("NCI"), X("CI"), -1.0 / P, OP.mult)
-    ts(X("JT", 512, 1024), X("JT", 0, 512), 512.0, OP.add)
+    ts(X("W3"), X("PM16i"), 1.0 / 3, OP.mult, -1.0 / 3, OP.add)
+    tc(X("PM32"), X("PM32i"))
+    ts(X("PMH"), X("PM32i"), -0.5, OP.add)
+    ts(X("R3"), X("W3"), -3.0, OP.mult, X("PM16"), OP.add)
+    act(X("JT", 256, 512), X("JT", 0, 256), FN.Identity, bias=256.0)
+    act(X("JT", 512, 768), X("JT", 0, 256), FN.Identity, bias=512.0)
+    ts(X("JT", 768, 1024), X("JT", 0, 256), 768.0, OP.add)
+    ts(X("PLK"), X("JT", 0, P), 1.0 / P, OP.mult)
+    ts(X("NCI"), X("JT", 0, P, 16), X("PM16"), OP.add, -1.0 / P, OP.mult)
+    ts(X("MASK"), X("C3"), X("R3"), OP.add, 2.0, OP.is_equal)
+    ts(X("RST"), X("C3"), 0.5, OP.is_gt)
     for b in range(4):
-        act(X("UT", b, 512, 4), X("JT", 0, 128), FN.Identity, bias=X("ub", b, b + 1), scale=0.0)
+        act(X("UT", b, 512, 4), X("JT", 0, P), FN.Identity, bias=X("ub", b, b + 1), scale=0.0)
 
-    def shared_column(m):
-        ts(X("TSH", m, m + 1), X("G8"), float(P * (peers[2 * m + 1] - peers[2 * m]) - LC), OP.mult, X("PM16"), OP.add)
-
-    for h, o in enumerate(("FA", "FB", "FC")):
-        ts(X(o), X("NB", h, 24, 3), X("MH", h, h + 1), OP.mult)
-    tt(X("FD0"), X("FA"), X("FB"), OP.add)
-    shared_column(0)
-    tt(X("FO"), X("FD0"), X("FC"), OP.add)
-    shared_column(1)
-    tc(X("FOU"), X("FO"))
-    tt(X("GO"), X("FO"), X("CI128"), OP.add)
-    tt(X("NGO"), X("NCI"), X("FO"), OP.subtract)
-    emit("v", lambda: g.vector.tensor_tensor(ap(X("GR")), ap(X("JT")).indirect(ap(X("FOU"))), ap(X("PLK")), OP.add),
-         [X("JT"), X("FOU"), X("PLK")], [X("GR")])
-    act(X("FRF"), X("JT"), FN.Copy, off=X("FOU"))
+    FO = X("FS", 2, 24, 3)
+    tt(X("A24"), X("NB"), X("MASK"), OP.mult)
+    ts(X("P3"), X("PID"), 3.0, OP.mult, 2.0, OP.add)
+    scan(X("FS"), X("RST"), X("A24"), 0.0, OP.mult, OP.add)
+    ts(X("P3i"), X("P3"), 15, OP.bitwise_and)
+    tc(X("FOU"), FO)
+    tt(X("NGO"), X("NCI"), FO, OP.subtract)
+    tt(X("GR"), X("JT"), X("PLK"), OP.add, off=X("FOU"))
+    act(X("FRF"), X("JT"), FN.Identity, bias=-63.5, off=X("FOU"))
     NS = 6
     for t in range(NS):
-        act(X("JKA", 128 * t, 128 * t + 128), X("GR"), FN.Sign, bias=X("NGO", t, t + 1), acc=X("RS", t, t + 1))
-    quant(X("NW", 0, 128), X("xb"))
+        act(X("JK1", P * t, P * t + P), X("GR"), FN.Sign, bias=X("NGO", t, t + 1), acc=X("RS1", 64 * t + 63, 64 * t + 64))
+    quant(X("NW0", 0, P), X("xb"))
     quant(X("UQ"), X("UT"))
-    mm("EB", X("UQ"), X("NW", 0, 128))
-    for t in range(NS, 8):
-        ts(X("CMR", 128 * (t - NS), 128 * (t - NS) + 128), X("GR"), X("GO", t, t + 1), OP.is_lt)
-    tr(X("ETR"), X("EB", 0, 128))
-    for t in range(NS, 8):
-        red(X("RV", t, t + 1), X("CMR", 128 * (t - NS), 128 * (t - NS) + 128))
+    mm("EB", X("UQ"), X("NW0", 0, P))
+    ts(X("GO"), X("NGO"), -1.0, OP.mult)
+    tr(X("ETR"), X("EB", 0, P))
     own = X("ET", 4 * me, 4 * me + 4)
-    tc(own, X("ETR", 0, 128, 32))
-    hand(0, [own, own])
+    ts(X("CMR", 0, P), X("GR"), X("GO", NS, NS + 1), OP.is_lt, -2.0, OP.mult)
+    tc(own, X("ETR", 0, P, 32))
+    sync("p", [own], [])
+    trs, at = [], 0
+    for (h, half, lo, cnt) in sorted(plan, key=lambda w: -w[1]):
+        have = topo.engines(core, h)
+        per = len(have) // 2 // len([1 for w in plan if w[1] == half])
+        trs.append(RemoteDMATransfer(dst_ids=[dst(h)], dma_engine_mask=sum(1 << e for e in have[at:at + per]), remote_sem=T.sem.h0,
+                                     src=T.ET[:, 4 * me + 2 * half:4 * me + 2 * half + 2], dst=T.HE[:, 2 * half:2 * half + 2]))
+        at += per
+    g.remote_dma_fused(trs, local_sem=T.sem.loc)
+    total["loc"] = at
     for lo, hi in ((0, 4 * me), (4 * me + 4, 32)):
         if lo < hi:
             arrive("ee", 2 * ALL, [X("ET", lo, hi)])
-    tc(X("RU", NS, 8), X("RV", NS, 8))
-    ts(X("RU", 0, NS), X("RS", 0, NS), -0.5, OP.mult, 63.5, OP.add)
-    ts(X("NPM"), X("PM16"), -1.0, OP.mult, 0.5, OP.add)
+    for t in range(NS + 1, 8):
+        ts(X("CMR", P * (t - NS), P * (t - NS) + P), X("GR"), X("GO", t, t + 1), OP.is_lt, -2.0, OP.mult)
+    for t in range(NS, 8):
+        add_up(X("RS1", 64 * t, 64 * t + 64), X("CMR", P * (t - NS), P * (t - NS) + P), P - 1.0)
+    ts(X("RU"), X("RS1", 63, 512, 64), -0.5, OP.mult, 63.5, OP.add)
+    ts(X("TAU", 0, 7), X("BROW", 0, 224, 32), X("PMH"), OP.add)
     sct(X("SF", 8, 136), X("RU"), X("FRF"))
-    ts(X("NTAU"), X("BASE"), X("NPM"), OP.add)
-    ts(X("AB"), X("SF", 8, 144), 896, OP.bitwise_and)
+    ts(X("NTAU", 0, 7), X("TAU", 0, 7), -1.0, OP.mult)
+    BIG = 1.5 * 2.0 ** 30
+    act(X("AB1"), X("SF", 8, 136), FN.Identity, bias=BIG)
+    act(X("AB"), X("AB1"), FN.Identity, bias=-BIG)
     tt(X("NEQ"), X("SF", 8, 136), X("SF", 7, 135), OP.not_equal)
-    tc(X("ABF"), X("AB", 0, 128))
-    shared_column(2)
-    emit("v", lambda: g.vector.tensor_tensor_scan(ap(X("KAP")), ap(X("NEQ")), ap(X("ABF")), -1.0, OP.add, OP.max),
-         [X("NEQ"), X("ABF")], [X("KAP")])
-    for i in range(n - 1):
-        c = 3 * (i // 2) + 2 * (i % 2)
-        act(X("JKB", 128 * i, 128 * i + 128), X("KAP"), FN.Sign, bias=X("NTAU", i, i + 1), acc=X("PC", c, c + 1))
-    for m in range(4):
-        than = X("TSH", m, m + 1) if m < 3 else X("PM16")
-        ts(X("CMP", 128 * m, 128 * m + 128), X("KAP"), P * peers[2 * m] + 16.0, OP.subtract, than, OP.is_lt)
-    for m in range(4):
-        red(X("PVC", m, m + 1), X("CMP", 128 * m, 128 * m + 128))
-    ts(X("SFL", 8, 144), X("SF", 8, 144), 127, OP.bitwise_and)
-    ts(X("PC", 1, 11, 3), X("PVC", 0, 4), -2.0, OP.mult, float(P), OP.add)
+    tc(X("NBU"), X("NB"))
+    scan(X("KAP"), X("NEQ"), X("AB"), -1.0, OP.add, OP.max)
+    NS = 4
+    for i in range(NS):
+        act(X("JK2", P * i, P * i + P), X("KAP"), FN.Sign, bias=X("NTAU", i, i + 1), acc=X("RS2", 64 * i + 63, 64 * i + 64))
+    for i in range(NS, n - 1):
+        ts(X("CMR", P * (i - NS), P * (i - NS) + P), X("KAP"), X("TAU", i, i + 1), OP.is_lt, -2.0, OP.mult)
+    for i in range(NS, n - 1):
+        add_up(X("RS2", 64 * i, 64 * i + 64), X("CMR", P * (i - NS), P * (i - NS) + P), float(P))
     for d in range(2):
-        ts(X("PU", d, 22, 2), X("PC"), -0.5, OP.mult, 64.0, OP.add)
-    gat(X("RLD"), X("SFL", 8, 144), X("PU", 0, 22))
+        ts(X("PU", d, 14, 2), X("RS2", 63, 448, 64), -0.5, OP.mult, 64.0, OP.add)
+    tt(X("RLD"), X("SF", 8, 144), X("BROW"), OP.subtract, off=X("PU"))
     tr(X("RLT"), X("RLD"))
-    tc(X("RQ", 0, 11), X("RLT", 0, 352, 32))
+    ts(X("RQ"), X("RLT", 0, 224, 16), 63.5, OP.add, P - 1.0, OP.min)
     sync("p", [X("RQ")], [])
     trs = []
     for i, s in enumerate(peers):
-        c, at = 3 * (i // 2) + i % 2, 2 * ways(T, topo, s)[0].index(me)
+        at = 2 * ways(T, topo, s)[0].index(me)
         trs.append(RemoteDMATransfer(dst_ids=[dst(T.cores[s])], dma_engine_mask=1 << topo.engines(core, T.cores[s])[i],
-                                     remote_sem=T.sem.rq, src=T.RQ[:, c:c + 2], dst=T.RQIN[:, at:at + 2]))
+                                     remote_sem=T.sem.rq, src=T.RQ[:, 2 * i:2 * i + 2], dst=T.RQIN[:, at:at + 2]))
     g.remote_dma_fused(trs, local_sem=T.sem.loc)
     total["loc"] += n - 1
-    fiota(X("LABT"), [[32, 64], [1, 16]])
-    fiota(X("UPD", 0, 512), [[0, 512]])
+    total["loc"] += serve(g, core, T, topo, me, order, 0, 1, n - 3, 2, True)
+    fiota(X("NPB"), [[0, R], [1, P]])
 
-    tc(X("NBU"), X("NB"))
-    tc(X("OX"), X("OXF"))
-    ts(X("R3"), X("PM16"), 3.0, OP.mult)
-    for i, c in enumerate((2.0 ** -25, 1.0, float(-P * me), 2.0 ** -124)):
-        fill(X("BC", i, i + 1), c)
-    ts(X("CN"), X("CNB"), X("R3"), OP.add)
+    act(X("NBR"), X("JT"), FN.Copy, off=X("NBU"))
+    ts(X("M3"), X("PM32"), 3.0, OP.mult)
     ts(X("NVC"), X("vb", 0, 4), -1.0, OP.mult)
+    ts(X("CN"), X("CNB"), X("M3"), OP.add)
+    tc(X("P3f"), X("P3i"))
+    act(X("ND"), X("NBR"), FN.Copy, off=X("CN"))
     for b in range(4):
-        act(X("VT", b, 512, 4), X("JT", 0, 128), FN.Identity, bias=X("NVC", b, b + 1), scale=0.0)
-    gat(X("NBR"), X("JT"), X("NBU"))
-    act(X("POS", 0, 512), X("NBR"), FN.Identity, bias=X("BC", 2, 3), off=X("CN"))
-    ts(X("MJ"), X("MJB"), X("R3"), OP.add)
-    quant(X("BBQ"), X("bbb"))
-    ts(X("MJ2"), X("MJ"), 4, OP.arith_shift_right)
-    quant(X("VQ"), X("VT"))
-    ts(X("MJ3"), X("MJ2"), 171, OP.mult)
-    mm("FB0", X("VQ"), X("BBQ"))
-    tc(X("PM32"), X("PM32i"))
-    ts(X("MJ4"), X("MJ3"), 9, OP.arith_shift_right)
-    ts(X("MJ2"), X("MJ"), 15, OP.bitwise_and)
-    ts(X("MJ5"), X("MJ4"), 16, OP.mult)
-    ts(X("PMH"), X("PM32"), -0.5, OP.add)
-    tt(X("MJ3"), X("MJ2"), X("MJ5"), OP.add)
-    ts(X("LA1"), X("PM32"), 16.0, OP.is_ge, 16.0, OP.mult)
-    tc(X("CIO"), X("MJ3"))
-    act(X("PIO"), X("KAP"), FN.Copy, off=X("RU"))
-    act(X("POS", 512, 768), X("PIO"), FN.Copy, off=X("CIO"))
-    act(X("CKA"), X("KJ"), FN.Sign, bias=X("PMH"), scale=-1.0)
-    act(X("CKB"), X("CKA"), FN.Identity, bias=X("BC", 0, 1), scale=2.0 ** -25)
-    act(X("CK"), X("CKB"), FN.Identity, bias=X("BC", 1, 2), scale=-1.0)
-    ts(X("IO16"), X("II"), 15, OP.bitwise_and)
-    tt(X("LA2"), X("LA1"), X("PM32"), OP.add)
+        act(X("VT", b, 512, 4), X("JT", 0, P), FN.Identity, bias=X("NVC", b, b + 1), scale=0.0)
     quant(X("AQ"), X("ab"))
-    ts(X("LAB"), X("JT", 0, 256, 64), X("LA2"), OP.add)
-    for b in range(2):
-        quant(X("PX", 128 * b, 128 * b + 128), X("xb"))
-    fill(X("XT"), 0.0)
-    tc(X("NP"), X("JT", 0, 128))
-
-    for h in range(2):
-        act(X("EXP", 512 * h, 512 * h + 512), X("ET"), FN.Copy, off=X("OX", 32 * h, 32 * h + 32))
-        tr(X("ETAB", 512 * h, 512 * h + 512), X("EXP", 512 * h, 512 * h + 512))
+    quant(X("BBQ"), X("bbb"))
+    ts(X("ID32"), X("JT", 0, 32), X("PM32"), OP.is_equal)
+    ts(X("SO"), X("JT", 0, P, 16), X("P3f"), OP.add)
+    ts(X("LABD"), X("DUP", 0, 8), 32.0, OP.mult, X("PM32"), OP.add)
+    ts(X("EXO"), X("DUP", 0, 8), 1.0, OP.mult)
+    BELOW = 1.0 - 2.0 ** -24
+    ts(X("CK0"), X("JT", 0, 32), X("PMH"), OP.is_lt, -2.0 ** -24, OP.mult)
+    ts(X("LAB"), X("JT", 0, P, 32), X("PM32"), OP.add)
+    fill(X("R32"), 1.0)
+    ts(X("CK"), X("CK0"), 1.0, OP.add)
+    fill(X("R32", 0, P, 32), 0.0)
+    tr(X("NT"), X("ND"))
+    ts(X("Q4"), X("JT", 0, 4), 0.25, OP.mult)
+    tc(X("NO"), X("NT", 0, 384, 16))
+    ts(X("O4"), X("JT", 0, 4), 2.5, OP.is_gt, float(P), OP.mult)
+    ts(X("LN"), X("NO", 0, 16), float(-P * me), OP.add)
+    ts(X("QOI"), X("NO", 16, 24), 31, OP.bitwise_and)
+    ts(X("COI"), X("NO", 16, 24), 5, OP.arith_shift_right)
+    tc(X("QO"), X("QOI"))
+    tc(X("CO"), X("COI"))
+    act(X("MSK"), X("ID32"), FN.Copy, off=X("QO"))
+    quant(X("VQ"), X("VT"))
+    mm("FB0", X("VQ"), X("BBQ"))
+    pick(X("PZ", 0, 256), X("NW0", 0, P), X("LN"))
+    mm("Z", X("UQ"), X("PZ", 0, P), True, False)
+    mm("Z", X("UQ"), X("PZ", P, 256), False, True)
+    tr(X("NFT"), X("FB0", 0, P))
+    quant(X("PX", 32, 160), X("xb"))
+    fill(X("XT", 4 * K, 512), 0.0)
+    fill(X("UPD"), -2048.0)
+    tr(X("FT"), X("NBR", 2, 384, 3))
+    tr(X("E1T"), X("Z", 0, P))
+    tc(X("FG"), X("FT", 0, P, 16))
+    act(X("PIO"), X("KAP"), FN.Copy, off=X("RU"))
+    act(X("PN"), X("PIO"), FN.Copy, off=X("SO"))
+    act(X("PD0"), X("PN"), FN.Identity, bias=1.0 - FAR[0], off=X("LABD"))
 
     arrive("rq", n - 1, [X("RQIN")])
-    pick(X("SL"), X("NW", 0, 128), X("RQIN"))
+    pick(X("SL"), X("NW0", 0, P), X("RQIN"))
     hand(1, [X("SL"), X("SLS")])
-    fiota(X("UPD", 512, 2048), [[0, 1536]])
     for s, w in (("rc", "FW"), ("rs", "FWS")):
         arrive(s, ALL, [X(w, 0, 1024)])
 
-    gat(X("E3"), X("ETAB"), X("NBU"))
-    act(X("LBI"), X("LABT"), FN.Copy, off=X("FOU"))
-    act(X("D3"), X("LBI"), FN.Copy, off=X("CIO"))
-    tt(X("E01"), X("E3", 0, 384, 3), X("E3", 1, 384, 3), OP.add)
-    tt(X("E2"), X("E01"), X("E3", 2, 384, 3), OP.add)
-    tt(X("ZS"), X("E2"), X("FB0", 0, 128), OP.add)
-
-    def near_sums():
-        pick(X("PZ", 0, 256), X("NW"), X("LN"))
-        mm("Z", X("UQ"), X("PZ", 0, 128), True, False)
-        mm("Z", X("UQ"), X("PZ", 128, 256), False, False)
+    tt(X("EG"), X("ET"), X("MSK"), OP.mult, off=X("CO"))
+    tr(X("EGT"), X("EG"))
+    scan(X("ES"), X("R32"), X("EGT"), 0.0, OP.mult, OP.add)
+    tt(X("ZA"), X("E1T", 0, P, 32), X("ES", 31, P, 32), OP.add)
+    tt(X("ZT"), X("ZA"), X("NFT", 0, P, 32), OP.add)
 
     c05 = float(np.float32(0.05))
     for t in range(R):
-        fw = FAR[t]
-        z = X("ZS")
-        if t:
+        fw, NW = FAR[t], "NW%d" % t
+        row = X("RW", P, 256)
+        if t == 0:
+            act(X("TR"), X("ZT"), FN.Abs, bias=X("TINY"), off=X("EXO"))
+            tr(row, X("TR"))
+        else:
             pick(X("PZ", 256, 384), X("FW", 0, fw), X("LF"))
             mm("Z", X("UQ"), X("PZ", 256, 384), False, False)
             mm("Z", X("VQ"), X("BBQ"), False, True)
-            tt(X("POS", 512, 768), X("POS", 512, 768), X("UG"), OP.max)
-            z = X("Z", 0, 128)
-        act(X("RW"), z, FN.Abs, bias=X("BC", 3, 4))
-        if t == 0:
-            tr(X("LT"), X("D3"))
-        tr(X("TR"), X("RW"))
-        for k in range(4):
+            for b in range(4):
+                mm("S%d" % b, A(b), X("PZ", 256, 384), False, True)
+            act(row, X("Z", 0, P), FN.Abs, bias=X("TINY"))
+            tr(X("TR"), row)
+            act(X("RW", 32, P), X("Z", 32, P), FN.Abs, scale=BELOW)
+        for k in (3, 2, 1, 0):
             act(X("SP", 32 * k, 32 * k + 32), X("CK"), FN.Identity, scale=X("TR", 32 * k, 32 * k + 1))
-        for k in range(4):
-            a, b, c = 32 * k, 32 * k + 32, 128 * k
-            val = X("TR", a, a + 1)
-            if b < P:
-                ts(X("CM", c + b, c + P), X("RW", b, P), val, OP.is_gt)
-            if a:
-                ts(X("CM", c, c + a), X("RW", 0, a), val, OP.is_ge)
-            tt(X("CM", c + a, c + b), X("RW", a, b), X("SP", a, b), OP.is_gt)
-            if k < 3:
-                act(X("JK4", c, c + P), X("CM", c, c + P), FN.Identity, acc=X("CT", k, k + 1))
+            if t == 0 and k == 3:
+                act(X("RW", 32, P), X("RW", P + 32, 256), FN.Copy, scale=BELOW)
+        for k in (3, 2, 1, 0):
+            a, c = 32 * k, P * k
+            ts(X("CM", c, c + 96), X("RW", a + 32, a + P), X("TR", a, a + 1), OP.is_ge)
+            tt(X("CM", c + 96, c + P), X("RW", P + a, P + a + 32), X("SP", a, a + 32), OP.is_gt)
+            if k:
+                act(X("JK3", c - P, c), X("CM", c, c + P), FN.Identity, acc=X("CT", k, k + 1))
             else:
-                red(X("CT", k, k + 1), X("CM", c, c + P))
-        for k in range(4):
-            ts(X("MM", 32 * k, 32 * k + 32), X("IO16"), X("CT", k, k + 1), OP.is_equal, X("LAB", k, k + 1), OP.mult)
+                add_up(X("CW"), X("CM", 0, P), 0.0)
+        if t:
+            for b in range(4):
+                act(X("T3", P * b, P * b + P), X("S%d" % b, 0, P), FN.Copy, scale=c05)
+        for k in (3, 2, 1, 0):
+            ts(X("MM", 32 * k, 32 * k + 32), X("IO16"), X("CT", k, k + 1) if k else X("CW", 63, 64), OP.is_equal, X("LAB", k, k + 1), OP.mult)
         tr(X("MT"), X("MM"))
-        red(X("IX"), X("MT"))
-        ts(X("OFF8"), X("OFFC"), X("IX"), OP.add)
+        add_up(X("IW"), X("MT"), 0.0)
+        ix = X("IW", 63, 64)
+        ts(X("BO"), X("Q4"), ix, OP.add, 4.0, OP.mult)
+        act(X("BG"), X("bbb"), FN.Copy, off=X("BO"))
         if t < R - 1:
-            gl = "GL%d" % t
-            ts(X(gl, 0, 1), X("IX"), 256.0 * me, OP.add)
-            spread(T[gl][:, 0:1], [T["RI%d" % t][:, slot_at(s):slot_at(s) + 1] for s in peers], "li%d" % t, [X(gl, 0, 1)])
-        gat(X("GP"), X("POS"), X("OFF8"))
-        tr(X("GPT"), X("GP"))
-        tc(X("PL"), X("GPT", 0, 128, 32))
-        j4 = X("GPT", 96, 97)
-        pick(X("PX", 0, 32), X("NW", 0, 128 * (t + 1)), X("PL", 0, 2))
+            ts(X("GL%d" % t, 0, 1), ix, float(P * me), OP.add)
+            hand(4 + t, [X("GL%d" % t, 0, 1)])
+        ts(X("OF"), X("O4"), ix, OP.add)
+        mine = X("OF", 0, 1)
+        held = X("NPB", P * t, P * t + P)
+        sct(held, mine, X("JT", P, P + K))
         if t == 0:
+            pick(X("PX", 0, 32), X("PZ", 0, 256), X("OF", 2, 4))
             for b in range(4):
-                mm("S%d" % b, X("AQ", 128 * b, 128 * b + 128), X("PX", 0, 128), True, False)
-                mm("S%d" % b, X("AQ", 128 * b, 128 * b + 128), X("PX", 16, 144), False, False)
+                mm("S%d" % b, A(b), X("PX", 0, P), True, False)
+                mm("S%d" % b, A(b), X("PX", 16, 144), False, False)
+            tc(X("GP"), X("PN"), off=X("OF", 0, 2))
+            tr(X("GPT"), X("GP"))
+            tc(X("PL", 0, 1), X("GPT", 0, 1))
+            for b in range(4):
+                act(X("BGR", b, 64, 4), X("BG", K * b, K * b + K), FN.Copy)
+            act(X("CD"), held, FN.Copy, off=X("LABD"))
+            act(X("NDB", 0, K), X("JT", 0, P), FN.Copy, off=mine)
+            pick(X("PX", 32, 48), X("FW", 0, fw), X("PL", 0, 1))
+            for b in range(4):
+                mm("S%d" % b, A(b), X("PX", 32, 160), False, True)
+            for b in range(4):
+                ts(X("T4", b, 64, 4), X("S%d" % b, 0, K), c05, OP.mult)
+            tt(X("XT", 0, 64), X("T4"), X("BGR"), OP.add)
         else:
-            pick(X("PX", 32, 48), X("FW", 0, fw), X("PL", 2, 3))
-            for b in range(4):
-                mm("S%d" % b, X("AQ", 128 * b, 128 * b + 128), X("PX", 0, 128))
-        ts(X("BO", 0, 8, 2), X("JT", 0, 4), j4, OP.add)
-        for b in range(4):
-            act(X("BG", b, 64, 4), X("bbb"), FN.Copy, off=X("BO", 2 * b, 2 * b + 1))
-        if t < R - 1:
-            ts(X("JU", 0, 1), j4, 0.25, OP.mult)
-            sct(X("NP"), X("JU", 0, 1), X("JT", P * (t + 1), P * (t + 1) + K))
-        else:
-            for d in range(2):
-                ts(X("JL", d, d + 1), X("IX"), 16.0 * d, OP.add)
-            sct(X("FPD"), X("JL"), X("VAL"))
-
-        def numbers():
-            emit("s", lambda: g.scalar.activation(T.NDB[0:1, K * t:K * t + K], T.GP[0:1, 96:112], FN.Identity, scale=0.25),
-                 [X("GP")], [X("NDB", K * t, K * t + K)])
-        if t == 0:
-            tr(X("PT"), X("POS", 0, 512))
-            tc(X("NLD"), X("PT", 0, 512, 16))
-            tr(X("FT"), X("POS", 512, 768))
-            pick(X("PX", 32, 48), X("FW", 0, fw), X("PL", 2, 3))
-            act(X("POS", 0, 512), X("NP"), FN.Copy, off=X("NLD"))
-            numbers()
-            for b in range(4):
-                mm("S%d" % b, X("AQ", 128 * b, 128 * b + 128), X("PX", 32, 160), False, True)
-            tc(X("FLD"), X("LT", 0, 256, 16))
-            for d in range(2):
-                tc(X("IDD", d, 16, 2), X("CI"))
-            for b in range(4):
-                ts(X("T3", b, 64, 4), X("S%d" % b, 0, 16), c05, OP.mult)
-        else:
-            def one(b):
-                tt(X("T1", b, 64, 4), X("S%d" % b, 0, 16), X("CC", 32 * b, 32 * b + 16), OP.add)
-
-            def two(b):
-                tt(X("T2", b, 64, 4), X("T1", b, 64, 4), X("CC", 32 * b + 16, 32 * b + 32), OP.add)
-            for b in range(4):
-                act(X("CC", 32 * b, 32 * b + 32), X("S%d" % b, 16, 48), FN.Copy)
-            if t < R - 1:
-                act(X("POS", 0, 512), X("NP"), FN.Copy, off=X("NLD"))
-                quant(X("WQ"), X("wb"))
-                ts(X("VAL"), X("IO16"), float(P * R), OP.add)
-            else:
-                tr(X("FPT"), X("FPD"))
-                tc(X("LFIN"), X("FPT", 0, 256, 32))
-            numbers()
+            act(X("CD"), held, FN.Copy, off=X("LABD"))
+            act(X("NDB", K * t, K * t + K), X("JT", 0, P), FN.Copy, off=mine)
             if t == R - 1:
                 dma("y", "on", [(T.nd[:], T.NDB[0:1, :])], [X("NDB")], [])
-            one(0)
-            one(1)
-            two(0)
-            one(2)
-            two(1)
-            one(3)
-            two(2)
-            two(3)
-            ts(X("T3"), X("T2"), c05, OP.mult)
-        tt(X("XT", 0, 64), X("T3"), X("BG"), OP.add)
-        new = P * (t + 1)
-        quant(X("NW", new, new + 128), X("XT"))
+            for b in range(4):
+                tt(X("XT", b, 64, 4), X("T3", P * b, P * b + P), X("BG", K * b, K * b + K), OP.add, off=mine)
+        quant(X(NW, P, 256), X("XT"))
         if t < R - 1:
-            hand(2 + t, [X("NW", new, new + K), X("NWS", new, new + K)])
-            arrive("li%d" % t, ALL, [X("RI%d" % t, 0, 7)])
-            tr(X("PT"), X("POS", 0, 512))
-            sct(X("UPD"), X("RI%d" % t, 0, 7), X("VL", fw - 1024, fw - 1024 + 112))
-            tc(X("LN"), X("PT", 0, 512, 32))
-            act(X("UG"), X("UPD"), FN.Copy, off=X("FLD"))
-            near_sums()
-            tr(X("UGT"), X("UG"))
-            tt(X("LD"), X("FT", 0, 256, 32), X("UGT", 0, 256, 32), OP.max)
-            tc(X("LF"), X("LD"))
+            hand(2 + t, [X(NW, P, P + K), X(NW + "S", P, P + K)])
+        tr(X("CDT"), X("CD"))
+        tc(X("LCU"), X("CDT", 0, P, 16))
+        if t < R - 1:
+            nxt = X("NW%d" % (t + 1), 0, P)
+            pick(nxt, X(NW), X("LCU"))
+            pick(X("PZ", 0, 256), nxt, X("LN"))
+            for h in range(2):
+                mm("Z", X("UQ"), X("PZ", P * h, P * h + P), h == 0, False)
+            for b in range(4):
+                for h in range(2):
+                    mm("S%d" % b, A(b), X("PZ", P * h, P * h + P), h == 0, False)
             if t:
-                act(X("FPD"), X("NP"), FN.Copy, off=X("IDD"))
+                quant(X("WQ"), X("wb"))
+            arrive("li%d" % t, ALL, [X("RI%d" % t, 0, 7)])
+            sct(X("UPD"), X("RI%d" % t, 0, 7), X("JT", fw - FAR[0] + 1, fw - FAR[0] + 113))
+            tt(X("PD%d" % (t + 1)), X("UPD"), X("PD%d" % t), OP.max, off=X("FG"))
+            tr(X("PT"), X("PD%d" % (t + 1)))
+            ts(X("LF"), X("PT", 0, P, 16), FAR[0] - 1.0, OP.add)
             arrive("cd%d" % t, ALL, [X("FW", fw, fw + 112)])
             arrive("sc%d" % t, ALL, [X("FWS", fw, fw + 112)])
+            if t == 0:
+                dma("y", "lw", [(T.wb[:], T.w[:])], [X("FW", fw, fw + 112)], [X("wb")])
         else:
-            pick(X("FIN"), X("NW"), X("LFIN"))
+            pick(X("FIN"), X(NW), X("LCU"))
             mm("Y", X("WQ"), X("FIN"))
             dma("y", "oc", [(T.oc[:], T.FIN[:].bitcast(u8))], [X("FIN")], [])
             dma("y", "os", [(T.osc[4 * k:4 * k + 4, :], T.FINS[32 * k:32 * k + 4, :]) for k in range(4)], [X("FINS")], [])
-            tc(X("YS"), X("Y", 0, 128))
+            tc(X("YS"), X("Y", 0, P))
             dma("s", "oy", [(T.y[:], T.YS[:])], [X("YS")], [])
     for s in total:
         if clock["p"].get(s, 0) < total[s]:

@@ -21,71 +21,82 @@ def _pack(kind, big, **names):
     SCRATCH[big] = ("sbuf", [128, at], kind)
 
 
-_pack(I32, "KI", PID=1, PM16i=1, PM32i=1, W3=1, P3=1, P3i=1, NO=24, COI=8, QOI=8)
-_pack(F32, "KF", PM16=1, PM32=1, PMH=1, R3=1, P3f=1, M3=1, C3=24, MASK=24, RST=24, A24=24, FS=24, NCI=8, NGO=8, GO=8, TAU=8, NTAU=8,
-      CNB=24, DUP=16, IO16=32, CK0=32, CK=32, ID32=32, LAB=4, Q4=4, O4=4, TINY=1, CT=4, ZA=4, ZT=4, GP=32, GPT=32)
-_pack(U16, "KU", FOU=8, RU=8, PU=14, NBU=24, CN=24, LN=16, CO=8, QO=8, FG=8, SO=8, LABD=8, EXO=8, BO=4, OF=4, PL=2, LF=8, LCU=8)
+_pack(I32, "KI", PID=1, PM16i=1, PM32i=1, W3=1, P3=1, P3i=1, NO=8, COI=8, QOI=8)
+_pack(F32, "KF", PM16=1, PM32=1, PMK=1, R3=1, P3f=1, M3=1, C3=24, MASK=24, A24=24, FS=24, NCI=8, NGO=8, GO=8, TAU=8, NTAU=8,
+      CNB=24, DUP=16, IO16=32, CK0=32, CK=32, ID32=32, LAB=4, Q4=4, CT=4, ZA=4, ZT=4)
+_pack(U16, "KU", FOU=8, RU=8, PU=14, NBU=24, CN=24, LN=16, CO=8, QO=8, FG=8, SO=8, LABD=8, EXO=8, BO=4, OF=2, LF=8, LCU=8)
 _sb(I32, NB=24)
-_sb(F32, JT=1024, PLK=128, FRF=128, GR=128, CMR=384, RS1=512, RS2=448, SF=144, AB1=128, AB=128, NEQ=128, KAP=128, BROW=224, RLD=224,
-    RLT=224, NBR=384, ND=384, NT=384, FT=128, PIO=128, PN=128, PD0=128, PD1=128, PD2=128, PT=128, MSK=128, EG=128, EGT=128, ES=128,
-    E1T=128, NFT=128, ETR=128, RW=256, TR=128, SP=128, CM=512, CW=64, IW=64, T3=512, T4=64, BG=64, BGR=64, NDB=48, YS=128)
+_sb(F32, JT=1024, PLK=128, FRF=128, GR=128, CMR=384, RS1=512, RS2=448, SF=144, AB1=128, AB=128, NEQ=128, KAP=128, BROW=224,
+    NBR=384, ND=384, NT=384, FT=128, PIO=128, R0=128, PD0=128, PD1=128, PD2=128, PT=128, MSK=128, EG=128, EGT=128, ES=128,
+    E1T=128, NFT=128, ETR=128, RW=256, TR=128, SP=128, CM=512, CW=64, IW=64, T3=512, BG=64, NDB=48, YS=128)
 _sb(F32, ET=32, HE=4, NVC=4)
-_sb(U16, RQ=14, RQIN=14, GL0=2, GL1=2, HL0=2, HL1=2, RI0=8, RI1=8)
-_sb(B16, xb=512, bbb=512, ub=16, vb=16, ab=2048, wb=512, UT=512, VT=512, XT=512, JK1=896, JK2=640, JK3=384, MM=128, MT=128, R32=128,
-    UPD=1024, NPB=384, CD=128, CDT=128)
+_sb(U16, RQ=14, RQA=8, RQB=6, GL0=2, GL1=2, HL0=2, HL1=2, RI0=8, RI1=8)
+_sb(B16, xb=512, bbb=512, ub=16, vb=16, ab=2048, wb=512, UT=512, VT=512, JK1=896, JK2=640, JK3=384, MM=128, MT=128, R32=128,
+    UPD=1024, NPB=384, CD=128, CDT=128, RLD=224, RLT=224)
 for _n, _w in (("NW0", 256), ("NW1", 256), ("NW2", 256), ("BBQ", 128), ("UQ", 128), ("VQ", 128), ("AQ", 512), ("WQ", 128), ("SL", 224),
-               ("FW", 1280), ("PZ", 384), ("PX", 160), ("FIN", 128), ("H1", 224), ("H2", 16), ("H3", 16)):
+               ("FW", 1280), ("PZ", 384), ("FIN", 128), ("H1", 224), ("H2", 64), ("H3", 64)):
     SCRATCH[_n] = ("sbuf", [128, _w], Q8)
     SCRATCH[_n + "S"] = ("sbuf", [128, _w], U8)
 BANKS = ("Z", "S0", "S1", "S2", "S3", "Y", "EB", "FB0")
 for _n in BANKS:
     SCRATCH[_n] = ("psum", [128, 512], F32)
-SEMAPHORES = ["cv", "cs", "ct", "cp", "ln0", "ln1", "lx", "lb", "lu", "lv", "la", "lw", "ee", "rq", "rc", "rs", "loc",
+SEMAPHORES = ["cv", "cs", "ct", "cp", "ln0", "ln1", "lx", "lb", "lu", "lv", "la", "lw", "ee", "rqa", "rqb", "rc", "rs", "loc",
               "li0", "li1", "cd0", "cd1", "sc0", "sc1", "on", "oc", "os", "oy", "h0", "h1", "h2", "h3", "h4", "h5"]
 FAR = (1024, 1136, 1248)
-LANDS = (("ee", "ee"), ("rc", "rs"), ("cd0", "sc0"), ("cd1", "sc1"), ("li0",), ("li1",))
+LANDS = (("ee",), ("rc", "rs"), ("cd0", "sc0"), ("cd1", "sc1"), ("li0",), ("li1",))
 
 
 def ways(T, topo, r):
     n, c = len(T.cores), T.cores[r]
     others = [(r + 1 + i) % n for i in range(n - 1)]
     order = [s for s in others if topo.same_plane(c, T.cores[s])] + [s for s in others if not topo.same_plane(c, T.cores[s])]
+    order.sort(key=lambda s: topo.mates(c, T.cores[s]))
     mine = [h for h in topo.cores_of(c) if h != c]
     full = [h for h in mine if all(topo.may_write(h, T.cores[s]) for s in others)]
-    rest = [h for h in mine if h not in full]
-    return order, [(rest[0], 0, 0, 2), (rest[1], 0, 2, 1), (full[0], 0, 3, 2), (full[1], 0, 5, 2), (rest[2], 1, 0, 3), (full[2], 1, 3, 2)]
+    a = [h for h in mine if h not in full and topo.die(h) == topo.die(c)][0]
+    b, d = [h for h in full if topo.die(h) != topo.die(c)]
+    e = [h for h in full if topo.die(h) == topo.die(c)][0]
+    numbers = [(a, 0, 0, 2, 4), (d, 0, 2, 1, 4), (b, 0, 3, 2, 4), (e, 0, 5, 2, 4)]
+    asked = [(b, 0, 3, 2, 4), (e, 0, 5, 2, 4), (d, 1, 3, 4, 2)]
+    made = [(a, 0, 0, 3, 2), (b, 0, 3, 3, 2), (e, 1, 5, 2, 2), (d, 1, 0, 1, 2)]
+    labels = [(e, 0, 0, 3, 2), (d, 0, 3, 3, 2)]
+    return order, (numbers, asked, made, made, labels, labels)
 
 
 def view(T, name, half, a, b):
     return T[name + "S"][:, a:b] if half else T[name][:, a:b].bitcast(dt.uint8)
 
 
-def serve(g, core, T, topo, r, order, stage, half, lo, cnt, home):
+def bits(engines):
+    return sum(1 << e for e in engines)
+
+
+def writes(T, topo, core, r, order, stage, half, lo, cnt, home):
     n = len(T.cores)
-    sem = T.sem[LANDS[stage][half]]
     jobs = []
     for i in range(lo, lo + cnt):
         s = order[i]
         slot = (r - s - 1) % n
         if stage == 0:
-            a = 4 * r + 2 * half
-            src, to = (T.ET[:, a:a + 2] if home else T.HE[:, 2 * half:2 * half + 2]), T.ET[:, a:a + 2]
+            src, to = T.HE[:], T.ET[:, 4 * r:4 * r + 4]
         elif stage == 1:
-            src, to = view(T, "SL" if home else "H1", half, 32 * i, 32 * i + LC), view(T, "FW", half, P * r, P * r + LC)
+            src, to = view(T, "H1", half, 32 * i, 32 * i + LC), view(T, "FW", half, P * r, P * r + LC)
         elif stage < 4:
             b = FAR[stage - 2] + K * slot
             src = view(T, "NW%d" % (stage - 2), half, P, P + K) if home else view(T, "H%d" % stage, half, 0, K)
             to = view(T, "FW", half, b, b + K)
         else:
-            src, to = T["HL%d" % (stage - 4)][:, 0:1], T["RI%d" % (stage - 4)][:, slot:slot + 1]
+            src, to = T[("GL%d" if home else "HL%d") % (stage - 4)][:, 0:1], T["RI%d" % (stage - 4)][:, slot:slot + 1]
         rid, pid = topo.addr(T.cores[s], core)
         jobs.append((DstId(rid=rid, pnc=pid), src, to))
-    m = topo.mask(core, T.cores[order[lo]])
-    calls = [[j] for j in jobs] if stage == 1 else [jobs]
-    for call in calls:
-        g.remote_dma_fused([RemoteDMATransfer(dst_ids=[j[0] for j in call], dma_engine_mask=m, remote_sem=sem,
-                                              srcs=[call[0][1]], dsts=[j[2] for j in call])], local_sem=T.sem.loc)
-    return len(calls) * bin(m).count("1")
+    sem = T.sem[LANDS[stage][half]]
+    have = topo.engines(core, T.cores[order[lo]])
+    if stage != 1:
+        return [RemoteDMATransfer(dst_ids=[j[0] for j in jobs], dma_engine_mask=bits(have), remote_sem=sem,
+                                  srcs=[jobs[0][1]], dsts=[j[2] for j in jobs])]
+    per = len(have) // cnt
+    return [RemoteDMATransfer(dst_ids=[j[0]], dma_engine_mask=bits(have[per * k:per * k + per]), remote_sem=sem, src=j[1], dst=j[2])
+            for k, j in enumerate(jobs)]
 
 
 def helper(g, core, T, topo):
@@ -93,15 +104,14 @@ def helper(g, core, T, topo):
         if core not in topo.cores_of(T.cores[r]):
             continue
         order, plan = ways(T, topo, r)
-        for (h, half, lo, cnt) in plan:
-            if h != core:
-                continue
-            share = len(topo.engines(T.cores[r], h)) // len([1 for w in plan if w[1] == half])
-            sent = 0
-            for stage in (0, 1, 4, 2, 5, 3):
-                if half < len(LANDS[stage]):
-                    g.wait_ge(T.sem["h%d" % stage], share if stage else share // 2)
-                    sent += serve(g, core, T, topo, r, order, stage, half, lo, cnt, False)
+        sent = 0
+        for stage in (0, 1, 4, 2, 5, 3):
+            for (h, half, lo, cnt, part) in plan[stage]:
+                if h == core:
+                    g.wait_ge(T.sem["h%d" % stage], len(topo.engines(T.cores[r], h)) // part)
+                    g.remote_dma_fused(writes(T, topo, core, r, order, stage, half, lo, cnt, False), local_sem=T.sem.loc)
+                    sent += len(topo.engines(core, T.cores[order[lo]]))
+        if sent:
             g.wait_ge(T.sem.loc, sent)
 
 
@@ -216,14 +226,11 @@ def rank_program(g, core, T, topo):
     def tr(o, a):
         emit("v", lambda: g.vector.transpose(ap(o), ap(a)), [a], [o])
 
-    def scan(o, a, b, first, op0, op1):
-        emit("v", lambda: g.vector.tensor_tensor_scan(ap(o), ap(a), ap(b), first, op0, op1), [a, b], [o])
+    def scan(o, a, b, start, op0, op1):
+        emit("v", lambda: g.vector.tensor_tensor_scan(ap(o), ap(a), ap(b), start, op0, op1), [a, b], [o])
 
-    def add_up(o, a, first):
-        scan(o, (a[0], a[1], a[1] + 64, 1), (a[0], a[1] + 64, a[2], 1), first, OP.add, OP.add)
-
-    def fill(o, c):
-        emit("v", lambda: g.vector.memset(ap(o), c), [], [o])
+    def add_up(o, a, start):
+        scan(o, (a[0], a[1], a[1] + 64, 1), (a[0], a[1] + 64, a[2], 1), start, OP.add, OP.add)
 
     def sct(win, off, a):
         emit("v", lambda: g.vector.tensor_copy(ap(win).indirect(ap(off)), ap(a)), [a, off], [win])
@@ -257,6 +264,10 @@ def rank_program(g, core, T, topo):
     def fiota(o, pattern, base=0):
         emit("p", lambda: g.iota(ap(o), pattern, base, 0, allow_small_or_imprecise_dtypes=True), [], [o])
 
+    def spread(o, cols):
+        for b in range(4):
+            act(X(o, b, 512, 4), X("JT", 0, P), FN.Identity, bias=X(cols, b, b + 1), scale=0.0)
+
     def A(b):
         return X("AQ", P * b, P * b + P)
 
@@ -267,120 +278,107 @@ def rank_program(g, core, T, topo):
         rid, pid = topo.addr(c, core)
         return DstId(rid=rid, pnc=pid)
 
-    shared = topo.mask(core, T.cores[peers[0]])
-    for s in peers:
-        shared &= topo.mask(core, T.cores[s])
-    ALL = (n - 1) * bin(shared).count("1")
+    have = topo.engines(core, plan[0][0][0])
+    leave = topo.engines(core, T.cores[order[0]])
+    stay = [e for e in have if e not in leave]
+    ALL = (n - 1) * len(leave)
+    total["loc"] = 0
 
-    def hand(stage, reads):
-        for half in range(len(LANDS[stage]) - 1, -1, -1):
-            sync("p", [reads[half]], [])
-            jobs = [w for w in plan if w[1] == half]
-            wide = 32 * max(w[3] for w in jobs)
-            trs = []
-            for k, (h, hf, lo, cnt) in enumerate(jobs):
-                have = topo.engines(core, h)
-                per = len(have) // len(jobs)
-                if stage == 1:
-                    src, to = view(T, "SL", half, 32 * lo, 32 * lo + wide), view(T, "H1", half, 32 * lo, 32 * lo + wide)
-                elif stage < 4:
-                    src, to = view(T, "NW%d" % (stage - 2), half, P, P + K), view(T, "H%d" % stage, half, 0, K)
-                else:
-                    src, to = T["GL%d" % (stage - 4)][:, 0:1], T["HL%d" % (stage - 4)][:, 0:1]
-                trs.append(RemoteDMATransfer(dst_ids=[dst(h)], dma_engine_mask=sum(1 << e for e in have[per * k:per * k + per]),
-                                             remote_sem=T.sem["h%d" % stage], src=src, dst=to))
-                total["loc"] += per
-            g.remote_dma_fused(trs, local_sem=T.sem.loc)
-        if stage < 4:
-            total["loc"] += serve(g, core, T, topo, me, order, stage, 1, n - 3, 2, True)
+    def call(reads, trs, engines):
+        sync("p", reads, [])
+        g.remote_dma_fused(trs, local_sem=T.sem.loc)
+        total["loc"] += engines
+
+    def deal(stage, jobs, engines, w=0):
+        per, trs = len(engines) // len(jobs), []
+        for k, (h, half, lo, cnt, part) in enumerate(jobs):
+            if stage == 0:
+                src, to = T.ET[:, 4 * me:4 * me + 4], T.HE[:]
+            elif stage == 1:
+                src, to = view(T, "SL", half, 32 * lo, 32 * lo + w), view(T, "H1", half, 32 * lo, 32 * lo + w)
+            elif stage < 4:
+                src, to = view(T, "NW%d" % (stage - 2), half, P, P + w), view(T, "H%d" % stage, half, 0, w)
+            else:
+                src, to = T["GL%d" % (stage - 4)][:, 0:1], T["HL%d" % (stage - 4)][:, 0:1]
+            trs.append(RemoteDMATransfer(dst_ids=[dst(h)], dma_engine_mask=bits(engines[per * k:per * k + per]),
+                                         remote_sem=T.sem["h%d" % stage], src=src, dst=to))
+        return trs
+
+    def own_writes(stage, half, lo, cnt):
+        return writes(T, topo, core, me, order, stage, half, lo, cnt, True)
 
     u8 = dt.uint8
 
-    dma("s", "lu", [(T.ub[:], T.u[:, 0:16])], [], [X("ub")])
     for q, s, lo in (("y", "ln0", 0), ("s", "ln1", 4)):
         for k in range(lo, lo + 4):
             E[q].dma_start(T.NB[16 * k:16 * k + 16, :], T.nb[:]).then_inc(T.sem[s], 16)
         total[s] = 64
     recs["NB"] = [(X("NB"), "w", (s, 64, {s: 64}), "d") for s in ("ln0", "ln1")]
+    dma("s", "lu", [(T.ub[:], T.u[:, 0:16])], [], [X("ub")])
     dma("y", "lx", [(T.xb[:], T.x[:])], [], [X("xb")])
     dma("s", "lv", [(T.vb[:], T.v[:, 0:16])], [], [X("vb")])
     dma("y", "lb", [(T.bbb[:], T.bb[:])], [], [X("bbb")])
     dma("y", "la", [(T.ab[:], T.a[:])], [], [X("ab")])
 
+    BIG3 = 2048
     iota(X("PID"), [[0, 1]], 1)
-    fiota(X("JT", 0, 256), [[1, 256]])
-    fiota(X("C3"), [[0, 8], [1, 3]])
+    fiota(X("JT", 0, P), [[1, P]])
+    fiota(X("C3"), [[0, 8], [BIG3, 3]])
+    fiota(X("SF"), [[0, 144]], -1000)
     for lo, hi in ((0, me), (me, n - 1)):
         if lo < hi:
             fiota(X("BROW", 32 * lo, 32 * hi), [[P, hi - lo], [0, 32]], P * peers[lo])
     fiota(X("CNB"), [[1, 3], [96, 4], [0, 2]])
     fiota(X("DUP"), [[1, 8], [0, 2]])
-    fiota(X("IO16"), [[0, 2], [1, 16]])
-    fill(X("SF"), -1000.0)
     ts(X("PM16i"), X("PID"), 15, OP.bitwise_and)
     ts(X("PM32i"), X("PID"), 31, OP.bitwise_and)
-    fill(X("TINY"), 2.0 ** -124)
-    tc(X("PM16"), X("PM16i"))
     ts(X("W3"), X("PM16i"), 1.0 / 3, OP.mult, -1.0 / 3, OP.add)
+    ts(X("PMK"), X("PM16i"), float(BIG3), OP.mult)
+    tc(X("PM16"), X("PM16i"))
+    ts(X("R3"), X("W3"), -3.0 * BIG3, OP.mult, X("PMK"), OP.add)
     tc(X("PM32"), X("PM32i"))
-    ts(X("PMH"), X("PM32i"), -0.5, OP.add)
-    ts(X("R3"), X("W3"), -3.0, OP.mult, X("PM16"), OP.add)
-    act(X("JT", 256, 512), X("JT", 0, 256), FN.Identity, bias=256.0)
-    act(X("JT", 512, 768), X("JT", 0, 256), FN.Identity, bias=512.0)
-    ts(X("JT", 768, 1024), X("JT", 0, 256), 768.0, OP.add)
-    ts(X("PLK"), X("JT", 0, P), 1.0 / P, OP.mult)
-    ts(X("NCI"), X("JT", 0, P, 16), X("PM16"), OP.add, -1.0 / P, OP.mult)
-    ts(X("MASK"), X("C3"), X("R3"), OP.add, 2.0, OP.is_equal)
-    ts(X("RST"), X("C3"), 0.5, OP.is_gt)
-    for b in range(4):
-        act(X("UT", b, 512, 4), X("JT", 0, P), FN.Identity, bias=X("ub", b, b + 1), scale=0.0)
+    ts(X("MASK"), X("C3"), X("R3"), OP.add, 2.0 * BIG3, OP.is_equal)
+    ts(X("P3"), X("PID"), 3.0, OP.mult, 2.0, OP.add)
+    for w in (P, 2 * P, 4 * P):
+        act(X("JT", w, 2 * w), X("JT", 0, w), FN.Identity, bias=float(w))
+    spread("UT", "ub")
 
     FO = X("FS", 2, 24, 3)
     tt(X("A24"), X("NB"), X("MASK"), OP.mult)
-    ts(X("P3"), X("PID"), 3.0, OP.mult, 2.0, OP.add)
-    scan(X("FS"), X("RST"), X("A24"), 0.0, OP.mult, OP.add)
-    ts(X("P3i"), X("P3"), 15, OP.bitwise_and)
+    ts(X("NCI"), X("JT", 0, P, 16), X("PM16"), OP.add, -1.0 / P, OP.mult)
+    scan(X("FS"), X("C3"), X("A24"), 0.0, OP.min, OP.add)
+    ts(X("PLK"), X("JT", 0, P), 1.0 / P, OP.mult)
     tc(X("FOU"), FO)
     tt(X("NGO"), X("NCI"), FO, OP.subtract)
+    ts(X("P3i"), X("P3"), 15, OP.bitwise_and)
+    tc(X("NBU"), X("NB"))
     tt(X("GR"), X("JT"), X("PLK"), OP.add, off=X("FOU"))
-    act(X("FRF"), X("JT"), FN.Identity, bias=-63.5, off=X("FOU"))
-    NS = 6
-    for t in range(NS):
+    for t in range(7):
         act(X("JK1", P * t, P * t + P), X("GR"), FN.Sign, bias=X("NGO", t, t + 1), acc=X("RS1", 64 * t + 63, 64 * t + 64))
+    act(X("FRF"), X("JT"), FN.Identity, bias=-63.5, off=X("FOU"))
     quant(X("NW0", 0, P), X("xb"))
     quant(X("UQ"), X("UT"))
     mm("EB", X("UQ"), X("NW0", 0, P))
-    ts(X("GO"), X("NGO"), -1.0, OP.mult)
+    ts(X("GO", 7, 8), X("NGO", 7, 8), -1.0, OP.mult)
     tr(X("ETR"), X("EB", 0, P))
+    ts(X("CMR", 0, P), X("GR"), X("GO", 7, 8), OP.is_lt, -2.0, OP.mult)
     own = X("ET", 4 * me, 4 * me + 4)
-    ts(X("CMR", 0, P), X("GR"), X("GO", NS, NS + 1), OP.is_lt, -2.0, OP.mult)
     tc(own, X("ETR", 0, P, 32))
-    sync("p", [own], [])
-    trs, at = [], 0
-    for (h, half, lo, cnt) in sorted(plan, key=lambda w: -w[1]):
-        have = topo.engines(core, h)
-        per = len(have) // 2 // len([1 for w in plan if w[1] == half])
-        trs.append(RemoteDMATransfer(dst_ids=[dst(h)], dma_engine_mask=sum(1 << e for e in have[at:at + per]), remote_sem=T.sem.h0,
-                                     src=T.ET[:, 4 * me + 2 * half:4 * me + 2 * half + 2], dst=T.HE[:, 2 * half:2 * half + 2]))
-        at += per
-    g.remote_dma_fused(trs, local_sem=T.sem.loc)
-    total["loc"] = at
+    call([own], deal(0, plan[0], have), len(have))
     for lo, hi in ((0, 4 * me), (4 * me + 4, 32)):
         if lo < hi:
-            arrive("ee", 2 * ALL, [X("ET", lo, hi)])
-    for t in range(NS + 1, 8):
-        ts(X("CMR", P * (t - NS), P * (t - NS) + P), X("GR"), X("GO", t, t + 1), OP.is_lt, -2.0, OP.mult)
-    for t in range(NS, 8):
-        add_up(X("RS1", 64 * t, 64 * t + 64), X("CMR", P * (t - NS), P * (t - NS) + P), P - 1.0)
+            arrive("ee", ALL, [X("ET", lo, hi)])
+    add_up(X("RS1", 448, 512), X("CMR", 0, P), P - 1.0)
+    ts(X("TAU", 0, 7), X("BROW", 0, 224, 32), X("PM32"), OP.add, -0.5, OP.add)
     ts(X("RU"), X("RS1", 63, 512, 64), -0.5, OP.mult, 63.5, OP.add)
-    ts(X("TAU", 0, 7), X("BROW", 0, 224, 32), X("PMH"), OP.add)
-    sct(X("SF", 8, 136), X("RU"), X("FRF"))
     ts(X("NTAU", 0, 7), X("TAU", 0, 7), -1.0, OP.mult)
+    sct(X("SF", 8, 136), X("RU"), X("FRF"))
+    ts(X("P3f"), X("P3i"), X("PM32"), OP.add, X("PM16"), OP.subtract)
     BIG = 1.5 * 2.0 ** 30
     act(X("AB1"), X("SF", 8, 136), FN.Identity, bias=BIG)
     act(X("AB"), X("AB1"), FN.Identity, bias=-BIG)
     tt(X("NEQ"), X("SF", 8, 136), X("SF", 7, 135), OP.not_equal)
-    tc(X("NBU"), X("NB"))
+    ts(X("EXO"), X("DUP", 0, 8), 1.0, OP.mult)
     scan(X("KAP"), X("NEQ"), X("AB"), -1.0, OP.add, OP.max)
     NS = 4
     for i in range(NS):
@@ -389,171 +387,188 @@ def rank_program(g, core, T, topo):
         ts(X("CMR", P * (i - NS), P * (i - NS) + P), X("KAP"), X("TAU", i, i + 1), OP.is_lt, -2.0, OP.mult)
     for i in range(NS, n - 1):
         add_up(X("RS2", 64 * i, 64 * i + 64), X("CMR", P * (i - NS), P * (i - NS) + P), float(P))
+    act(X("M3"), X("PM32"), FN.Copy, scale=3.0)
+    act(X("NBR"), X("JT"), FN.Copy, off=X("NBU"))
     for d in range(2):
         ts(X("PU", d, 14, 2), X("RS2", 63, 448, 64), -0.5, OP.mult, 64.0, OP.add)
+    ts(X("LABD"), X("DUP", 0, 8), 32.0, OP.mult, X("PM32"), OP.add)
     tt(X("RLD"), X("SF", 8, 144), X("BROW"), OP.subtract, off=X("PU"))
+    ts(X("SO"), X("DUP", 0, 8), 32.0, OP.mult, X("P3f"), OP.add)
     tr(X("RLT"), X("RLD"))
-    ts(X("RQ"), X("RLT", 0, 224, 16), 63.5, OP.add, P - 1.0, OP.min)
-    sync("p", [X("RQ")], [])
-    trs = []
-    for i, s in enumerate(peers):
-        at = 2 * ways(T, topo, s)[0].index(me)
-        trs.append(RemoteDMATransfer(dst_ids=[dst(T.cores[s])], dma_engine_mask=1 << topo.engines(core, T.cores[s])[i],
-                                     remote_sem=T.sem.rq, src=T.RQ[:, 2 * i:2 * i + 2], dst=T.RQIN[:, at:at + 2]))
-    g.remote_dma_fused(trs, local_sem=T.sem.loc)
-    total["loc"] += n - 1
-    total["loc"] += serve(g, core, T, topo, me, order, 0, 1, n - 3, 2, True)
-    fiota(X("NPB"), [[0, R], [1, P]])
-
-    act(X("NBR"), X("JT"), FN.Copy, off=X("NBU"))
-    ts(X("M3"), X("PM32"), 3.0, OP.mult)
-    ts(X("NVC"), X("vb", 0, 4), -1.0, OP.mult)
     ts(X("CN"), X("CNB"), X("M3"), OP.add)
-    tc(X("P3f"), X("P3i"))
+    ts(X("RQ"), X("RLT", 0, 224, 16), 63.5, OP.add, P - 1.0, OP.min)
+    two = len(leave) // 4
+    for sem, land, lo, hi in (("rqa", "RQA", 3, 7), ("rqb", "RQB", 0, 3)):
+        trs = []
+        for k, s in enumerate(order[lo:hi]):
+            i, at = peers.index(s), 2 * (ways(T, topo, s)[0].index(me) - lo)
+            trs.append(RemoteDMATransfer(dst_ids=[dst(T.cores[s])], dma_engine_mask=bits(leave[two * k:two * k + two]),
+                                         remote_sem=T.sem[sem], src=T.RQ[:, 2 * i:2 * i + 2], dst=T[land][:, at:at + 2]))
+        call([X("RQ")], trs, two * (hi - lo))
+        arrive(sem, two * (hi - lo), [X(land)])
+    fiota(X("IO16"), [[0, 2], [1, 16]])
+    fiota(X("R0"), [[0, 4], [1, 32]])
+
     act(X("ND"), X("NBR"), FN.Copy, off=X("CN"))
-    for b in range(4):
-        act(X("VT", b, 512, 4), X("JT", 0, P), FN.Identity, bias=X("NVC", b, b + 1), scale=0.0)
     quant(X("AQ"), X("ab"))
     quant(X("BBQ"), X("bbb"))
     ts(X("ID32"), X("JT", 0, 32), X("PM32"), OP.is_equal)
-    ts(X("SO"), X("JT", 0, P, 16), X("P3f"), OP.add)
-    ts(X("LABD"), X("DUP", 0, 8), 32.0, OP.mult, X("PM32"), OP.add)
-    ts(X("EXO"), X("DUP", 0, 8), 1.0, OP.mult)
     BELOW = 1.0 - 2.0 ** -24
-    ts(X("CK0"), X("JT", 0, 32), X("PMH"), OP.is_lt, -2.0 ** -24, OP.mult)
-    ts(X("LAB"), X("JT", 0, P, 32), X("PM32"), OP.add)
-    fill(X("R32"), 1.0)
-    ts(X("CK"), X("CK0"), 1.0, OP.add)
-    fill(X("R32", 0, P, 32), 0.0)
+    ts(X("CK0"), X("JT", 0, 32), X("PM32"), OP.is_lt, -2.0 ** -24, OP.mult)
+    act(X("NVC"), X("vb", 0, 4), FN.Copy, scale=-1.0)
+    spread("VT", "NVC")
     tr(X("NT"), X("ND"))
-    ts(X("Q4"), X("JT", 0, 4), 0.25, OP.mult)
-    tc(X("NO"), X("NT", 0, 384, 16))
-    ts(X("O4"), X("JT", 0, 4), 2.5, OP.is_gt, float(P), OP.mult)
-    ts(X("LN"), X("NO", 0, 16), float(-P * me), OP.add)
-    ts(X("QOI"), X("NO", 16, 24), 31, OP.bitwise_and)
-    ts(X("COI"), X("NO", 16, 24), 5, OP.arith_shift_right)
+    tr(X("FT"), X("NBR", 2, 384, 3))
+    tc(X("NO"), X("NT", 256, 384, 16))
+    ts(X("LN"), X("NT", 0, 256, 16), float(-P * me), OP.add)
+    ts(X("QOI"), X("NO"), 31, OP.bitwise_and)
+    ts(X("COI"), X("NO"), 5, OP.arith_shift_right)
     tc(X("QO"), X("QOI"))
     tc(X("CO"), X("COI"))
     act(X("MSK"), X("ID32"), FN.Copy, off=X("QO"))
+
+    def near(win, close):
+        pick(X("PZ", 0, 256), win, X("LN"))
+        for h in range(2):
+            mm("Z", X("UQ"), X("PZ", P * h, P * h + P), h == 0, close and h == 1)
+        for b in range(4):
+            for h in range(2):
+                mm("S%d" % b, A(b), X("PZ", P * h, P * h + P), h == 0, False)
+
+    def answer(half, i, engines):
+        return RemoteDMATransfer(dst_ids=[dst(T.cores[order[i]])], dma_engine_mask=bits(engines), remote_sem=T.sem[LANDS[1][half]],
+                                 src=view(T, "SL", half, 32 * i, 32 * i + LC), dst=view(T, "FW", half, P * me, P * me + LC))
+
+    pick(X("SL", 96, 224), X("NW0", 0, P), X("RQA"))
+    call([X("SL", 96, 224)], deal(1, plan[1][:2], stay, 32 + LC), len(stay))
+    call([X("SLS", 96, 224)], deal(1, plan[1][2:], leave, P), len(leave))
     quant(X("VQ"), X("VT"))
     mm("FB0", X("VQ"), X("BBQ"))
-    pick(X("PZ", 0, 256), X("NW0", 0, P), X("LN"))
-    mm("Z", X("UQ"), X("PZ", 0, P), True, False)
-    mm("Z", X("UQ"), X("PZ", P, 256), False, True)
-    tr(X("NFT"), X("FB0", 0, P))
-    quant(X("PX", 32, 160), X("xb"))
-    fill(X("XT", 4 * K, 512), 0.0)
-    fill(X("UPD"), -2048.0)
-    tr(X("FT"), X("NBR", 2, 384, 3))
-    tr(X("E1T"), X("Z", 0, P))
+    near(X("NW0", 0, P), True)
     tc(X("FG"), X("FT", 0, P, 16))
+    tr(X("NFT"), X("FB0", 0, P))
+    pick(X("SL", 0, 96), X("NW0", 0, P), X("RQB"))
+    for half, w in enumerate(("SL", "SLS")):
+        call([X(w, 0, 96)], [answer(half, 0, leave[:2 * two]), answer(half, 1, leave[2 * two:])], len(leave))
+        call([], [answer(half, 2, leave)], len(leave))
+    arrive("rc", 2 * len(leave) + 4 * 2 * two, [X("FW", 0, 1024)])
+    arrive("rs", 2 * len(leave) + 4 * two, [X("FWS", 0, 1024)])
+    fiota(X("NPB"), [[0, R], [1, P]])
+    fiota(X("UPD"), [[0, 1024]], -2048)
+    tr(X("E1T"), X("Z", 0, P))
+
     act(X("PIO"), X("KAP"), FN.Copy, off=X("RU"))
-    act(X("PN"), X("PIO"), FN.Copy, off=X("SO"))
-    act(X("PD0"), X("PN"), FN.Identity, bias=1.0 - FAR[0], off=X("LABD"))
-
-    arrive("rq", n - 1, [X("RQIN")])
-    pick(X("SL"), X("NW0", 0, P), X("RQIN"))
-    hand(1, [X("SL"), X("SLS")])
-    for s, w in (("rc", "FW"), ("rs", "FWS")):
-        arrive(s, ALL, [X(w, 0, 1024)])
-
+    act(X("R32"), X("R0"), FN.Sign)
+    act(X("PD0"), X("PIO"), FN.Identity, bias=1.0 - FAR[0], off=X("SO"))
+    act(X("CK"), X("CK0"), FN.Identity, bias=1.0)
+    act(X("LAB"), X("JT", 0, P, 32), FN.Identity, bias=X("PM32"))
+    act(X("Q4"), X("JT", 0, 4), FN.Copy, scale=0.25)
     tt(X("EG"), X("ET"), X("MSK"), OP.mult, off=X("CO"))
     tr(X("EGT"), X("EG"))
     scan(X("ES"), X("R32"), X("EGT"), 0.0, OP.mult, OP.add)
     tt(X("ZA"), X("E1T", 0, P, 32), X("ES", 31, P, 32), OP.add)
     tt(X("ZT"), X("ZA"), X("NFT", 0, P, 32), OP.add)
 
+    def far_list(t):
+        tr(X("PT"), X("PD%d" % t))
+        ts(X("LF"), X("PT", 0, P, 16), FAR[0] - 1.0, OP.add)
+
+    def outside(k):
+        ts(X("CM", P * k, P * k + 96), X("RW", 32 * k + 32, 32 * k + P), X("TR", 32 * k, 32 * k + 1), OP.is_ge)
+
+    def label(k):
+        ts(X("MM", 32 * k, 32 * k + 32), X("IO16"), X("CT", k, k + 1) if k else X("CW", 63, 64), OP.is_equal, X("LAB", k, k + 1), OP.mult)
+
+    def scaled(b):
+        act(X("T3", P * b, P * b + P), X("S%d" % b, 0, P), FN.Copy, scale=c05)
+
+    def far_sums():
+        for b in range(4):
+            mm("S%d" % b, A(b), X("PZ", 256, 384), False, True)
+
+    TINY = 2.0 ** -124
     c05 = float(np.float32(0.05))
     for t in range(R):
         fw, NW = FAR[t], "NW%d" % t
-        row = X("RW", P, 256)
+        row, far = X("RW", P, 256), X("PZ", 256, 384)
         if t == 0:
-            act(X("TR"), X("ZT"), FN.Abs, bias=X("TINY"), off=X("EXO"))
+            act(X("TR"), X("ZT"), FN.Abs, bias=TINY, off=X("EXO"))
+            far_list(0)
             tr(row, X("TR"))
         else:
-            pick(X("PZ", 256, 384), X("FW", 0, fw), X("LF"))
-            mm("Z", X("UQ"), X("PZ", 256, 384), False, False)
+            pick(far, X("FW", 0, fw), X("LF"))
+            mm("Z", X("UQ"), far, False, False)
             mm("Z", X("VQ"), X("BBQ"), False, True)
-            for b in range(4):
-                mm("S%d" % b, A(b), X("PZ", 256, 384), False, True)
-            act(row, X("Z", 0, P), FN.Abs, bias=X("TINY"))
+            far_sums()
+            act(row, X("Z", 0, P), FN.Abs, bias=TINY)
             tr(X("TR"), row)
             act(X("RW", 32, P), X("Z", 32, P), FN.Abs, scale=BELOW)
         for k in (3, 2, 1, 0):
             act(X("SP", 32 * k, 32 * k + 32), X("CK"), FN.Identity, scale=X("TR", 32 * k, 32 * k + 1))
             if t == 0 and k == 3:
                 act(X("RW", 32, P), X("RW", P + 32, 256), FN.Copy, scale=BELOW)
+        outside(3)
         for k in (3, 2, 1, 0):
             a, c = 32 * k, P * k
-            ts(X("CM", c, c + 96), X("RW", a + 32, a + P), X("TR", a, a + 1), OP.is_ge)
+            if k:
+                outside(k - 1)
             tt(X("CM", c + 96, c + P), X("RW", P + a, P + a + 32), X("SP", a, a + 32), OP.is_gt)
             if k:
                 act(X("JK3", c - P, c), X("CM", c, c + P), FN.Identity, acc=X("CT", k, k + 1))
-            else:
-                add_up(X("CW"), X("CM", 0, P), 0.0)
+        label(3)
+        add_up(X("CW"), X("CM", 0, P), 0.0)
         if t:
             for b in range(4):
-                act(X("T3", P * b, P * b + P), X("S%d" % b, 0, P), FN.Copy, scale=c05)
-        for k in (3, 2, 1, 0):
-            ts(X("MM", 32 * k, 32 * k + 32), X("IO16"), X("CT", k, k + 1) if k else X("CW", 63, 64), OP.is_equal, X("LAB", k, k + 1), OP.mult)
+                scaled(b)
+        for k in (2, 1, 0):
+            label(k)
+        if t == 0:
+            pick(far, X("FW", 0, fw), X("LF"))
+            far_sums()
         tr(X("MT"), X("MM"))
         add_up(X("IW"), X("MT"), 0.0)
-        ix = X("IW", 63, 64)
-        ts(X("BO"), X("Q4"), ix, OP.add, 4.0, OP.mult)
-        act(X("BG"), X("bbb"), FN.Copy, off=X("BO"))
+        ix, mine, held = X("IW", 63, 64), X("OF", 0, 1), X("NPB", P * t, P * t + P)
         if t < R - 1:
             ts(X("GL%d" % t, 0, 1), ix, float(P * me), OP.add)
-            hand(4 + t, [X("GL%d" % t, 0, 1)])
-        ts(X("OF"), X("O4"), ix, OP.add)
-        mine = X("OF", 0, 1)
-        held = X("NPB", P * t, P * t + P)
+            call([X("GL%d" % t, 0, 1)], deal(4 + t, plan[4 + t], have), len(have))
+            call([], own_writes(4 + t, 0, n - 2, 1), len(leave))
+        ts(X("BO"), X("Q4"), ix, OP.add, 4.0, OP.mult)
+        if t == 0:
+            scaled(0)
+        act(X("BG"), X("bbb"), FN.Copy, off=X("BO"))
+        tc(mine, ix)
+        if t == 0:
+            ts(X("T3", P, 2 * P), X("S1", 0, P), c05, OP.mult)
+            scaled(2)
         sct(held, mine, X("JT", P, P + K))
         if t == 0:
-            pick(X("PX", 0, 32), X("PZ", 0, 256), X("OF", 2, 4))
-            for b in range(4):
-                mm("S%d" % b, A(b), X("PX", 0, P), True, False)
-                mm("S%d" % b, A(b), X("PX", 16, 144), False, False)
-            tc(X("GP"), X("PN"), off=X("OF", 0, 2))
-            tr(X("GPT"), X("GP"))
-            tc(X("PL", 0, 1), X("GPT", 0, 1))
-            for b in range(4):
-                act(X("BGR", b, 64, 4), X("BG", K * b, K * b + K), FN.Copy)
-            act(X("CD"), held, FN.Copy, off=X("LABD"))
-            act(X("NDB", 0, K), X("JT", 0, P), FN.Copy, off=mine)
-            pick(X("PX", 32, 48), X("FW", 0, fw), X("PL", 0, 1))
-            for b in range(4):
-                mm("S%d" % b, A(b), X("PX", 32, 160), False, True)
-            for b in range(4):
-                ts(X("T4", b, 64, 4), X("S%d" % b, 0, K), c05, OP.mult)
-            tt(X("XT", 0, 64), X("T4"), X("BGR"), OP.add)
-        else:
-            act(X("CD"), held, FN.Copy, off=X("LABD"))
-            act(X("NDB", K * t, K * t + K), X("JT", 0, P), FN.Copy, off=mine)
-            if t == R - 1:
-                dma("y", "on", [(T.nd[:], T.NDB[0:1, :])], [X("NDB")], [])
-            for b in range(4):
-                tt(X("XT", b, 64, 4), X("T3", P * b, P * b + P), X("BG", K * b, K * b + K), OP.add, off=mine)
-        quant(X(NW, P, 256), X("XT"))
+            ts(X("T3", 3 * P, 4 * P), X("S3", 0, P), c05, OP.mult)
+        act(X("CD"), held, FN.Copy, off=X("LABD"))
+        act(X("NDB", K * t, K * t + K), X("JT", 0, P), FN.Copy, off=mine)
+        if t == R - 1:
+            dma("y", "on", [(T.nd[:], T.NDB[0:1, :])], [X("NDB")], [])
+        for b in range(4):
+            tt(X("xb", b, 64, 4), X("T3", P * b, P * b + P), X("BG", K * b, K * b + K), OP.add, off=mine)
+        if t == R - 1:
+            tr(X("CDT"), X("CD"))
+        quant(X(NW, P, 256), X("xb"))
         if t < R - 1:
-            hand(2 + t, [X(NW, P, P + K), X(NW + "S", P, P + K)])
-        tr(X("CDT"), X("CD"))
+            jobs = plan[2 + t]
+            call([X(NW, P, P + K)], deal(2 + t, jobs[:2], have, K), len(have))
+            call([X(NW + "S", P, P + 4 * K)], own_writes(2 + t, 0, n - 2, 1) + deal(2 + t, jobs[2:3], stay, 4 * K), len(have))
+            call([], own_writes(2 + t, 1, 1, 4) + deal(2 + t, jobs[3:], stay, K), len(have))
+            tr(X("CDT"), X("CD"))
         tc(X("LCU"), X("CDT", 0, P, 16))
         if t < R - 1:
             nxt = X("NW%d" % (t + 1), 0, P)
             pick(nxt, X(NW), X("LCU"))
-            pick(X("PZ", 0, 256), nxt, X("LN"))
-            for h in range(2):
-                mm("Z", X("UQ"), X("PZ", P * h, P * h + P), h == 0, False)
-            for b in range(4):
-                for h in range(2):
-                    mm("S%d" % b, A(b), X("PZ", P * h, P * h + P), h == 0, False)
+            near(nxt, False)
             if t:
                 quant(X("WQ"), X("wb"))
             arrive("li%d" % t, ALL, [X("RI%d" % t, 0, 7)])
             sct(X("UPD"), X("RI%d" % t, 0, 7), X("JT", fw - FAR[0] + 1, fw - FAR[0] + 113))
             tt(X("PD%d" % (t + 1)), X("UPD"), X("PD%d" % t), OP.max, off=X("FG"))
-            tr(X("PT"), X("PD%d" % (t + 1)))
-            ts(X("LF"), X("PT", 0, P, 16), FAR[0] - 1.0, OP.add)
+            far_list(t + 1)
             arrive("cd%d" % t, ALL, [X("FW", fw, fw + 112)])
             arrive("sc%d" % t, ALL, [X("FWS", fw, fw + 112)])
             if t == 0:

import numpy as np
from concourse.bass import DstId, RemoteDMATransfer
from concourse.mybir import dt, AluOpType, ActivationFunctionType

F32, I32, U16, B16, Q8, U8 = "float32", "int32", "uint16", "bfloat16", "float8_e4m3fn_x4", "uint8"
P, K, R, LC = 128, 16, 3, 24
SCRATCH = {}
ALIAS = {}


def _sb(kind, **names):
    for k in names:
        SCRATCH[k] = ("sbuf", [128, names[k]], kind)


def _pack(kind, big, **names):
    at = 0
    for k in names:
        ALIAS[k] = (big, at, names[k])
        at += (names[k] + 15) // 16 * 16
    SCRATCH[big] = ("sbuf", [128, at], kind)


_pack(I32, "KI", PID=1, PM16i=1, PM32i=1, W3=1, P3=1, P3i=1, NO=8, COI=8, QOI=8)
_pack(F32, "KF", PM16=1, PM32=1, PMK=1, R3=1, P3f=1, M3=1, C3=24, MASK=24, A24=24, FS=24, NCI=8, NGO=8, GO=8, TAU=8, NTAU=8,
      CNB=24, DUP=16, IO16=32, CK0=32, CK=32, ID32=32, LAB=4, Q4=4, CT=4, ZA=4, ZT=4)
_pack(U16, "KU", FOU=8, RU=8, PU=14, NBU=24, CN=24, LN=16, CO=8, QO=8, FG=8, SO=8, LABD=8, EXO=8, BO=4, OF=2, LF=8, LCU=8)
_sb(I32, NB=24)
_sb(F32, JT=1024, PLK=128, FRF=128, GR=128, CMR=384, RS1=512, RS2=448, SF=144, AB1=128, AB=128, NEQ=128, KAP=128, BROW=224,
    NBR=384, ND=384, NT=384, FT=128, PIO=128, R0=128, PD0=128, PD1=128, PD2=128, PT=128, MSK=128, EG=128, EGT=128, ES=128,
    E1T=128, NFT=128, ETR=128, RW=256, TR=128, SP=128, CM=512, CW=64, IW=64, T3=512, BG=64, NDB=48, YS=128)
_sb(F32, ET=32, HE=4, NVC=4)
_sb(U16, RQ=14, RQA=8, RQB=6, GL0=2, GL1=2, HL0=2, HL1=2, RI0=8, RI1=8)
_sb(B16, xb=512, bbb=512, ub=16, vb=16, ab=2048, wb=512, UT=512, VT=512, JK1=896, JK2=640, JK3=384, MM=128, MT=128, R32=128,
    UPD=1024, NPB=384, CD=128, CDT=128, RLD=224, RLT=224)
for _n, _w in (("NW0", 256), ("NW1", 256), ("NW2", 256), ("BBQ", 128), ("UQ", 128), ("VQ", 128), ("AQ", 512), ("WQ", 128), ("SL", 224),
               ("FW", 1280), ("PZ", 384), ("FIN", 128), ("H1", 224), ("H2", 64), ("H3", 64)):
    SCRATCH[_n] = ("sbuf", [128, _w], Q8)
    SCRATCH[_n + "S"] = ("sbuf", [128, _w], U8)
BANKS = ("Z", "S0", "S1", "S2", "S3", "Y", "EB", "FB0")
for _n in BANKS:
    SCRATCH[_n] = ("psum", [128, 512], F32)
SEMAPHORES = ["cv", "cs", "ct", "cp", "ln0", "ln1", "lx", "lb", "lu", "lv", "la", "lw", "ee", "rqa", "rqb", "rc", "rs", "loc",
              "li0", "li1", "cd0", "cd1", "sc0", "sc1", "on", "oc", "os", "oy", "h0", "h1", "h2", "h3", "h4", "h5"]
FAR = (1024, 1136, 1248)
LANDS = (("ee",), ("rc", "rs"), ("cd0", "sc0"), ("cd1", "sc1"), ("li0",), ("li1",))


def ways(T, topo, r):
    n, c = len(T.cores), T.cores[r]
    others = [(r + 1 + i) % n for i in range(n - 1)]
    order = [s for s in others if topo.same_plane(c, T.cores[s])] + [s for s in others if not topo.same_plane(c, T.cores[s])]
    order.sort(key=lambda s: topo.mates(c, T.cores[s]))
    mine = [h for h in topo.cores_of(c) if h != c]
    full = [h for h in mine if all(topo.may_write(h, T.cores[s]) for s in others)]
    a = [h for h in mine if h not in full and topo.die(h) == topo.die(c)][0]
    b, d = [h for h in full if topo.die(h) != topo.die(c)]
    e = [h for h in full if topo.die(h) == topo.die(c)][0]
    numbers = [(a, 0, 0, 2, 4), (d, 0, 2, 1, 4), (b, 0, 3, 2, 4), (e, 0, 5, 2, 4)]
    asked = [(b, 0, 3, 2, 4), (e, 0, 5, 2, 4), (d, 1, 3, 4, 2)]
    made = [(a, 0, 0, 3, 2), (b, 0, 3, 3, 2), (e, 1, 5, 2, 2), (d, 1, 0, 1, 2)]
    labels = [(e, 0, 0, 3, 2), (d, 0, 3, 3, 2)]
    return order, (numbers, asked, made, made, labels, labels)


def view(T, name, half, a, b):
    return T[name + "S"][:, a:b] if half else T[name][:, a:b].bitcast(dt.uint8)


def bits(engines):
    return sum(1 << e for e in engines)


def writes(T, topo, core, r, order, stage, half, lo, cnt, home):
    n = len(T.cores)
    jobs = []
    for i in range(lo, lo + cnt):
        s = order[i]
        slot = (r - s - 1) % n
        if stage == 0:
            src, to = T.HE[:], T.ET[:, 4 * r:4 * r + 4]
        elif stage == 1:
            src, to = view(T, "H1", half, 32 * i, 32 * i + LC), view(T, "FW", half, P * r, P * r + LC)
        elif stage < 4:
            b = FAR[stage - 2] + K * slot
            src = view(T, "NW%d" % (stage - 2), half, P, P + K) if home else view(T, "H%d" % stage, half, 0, K)
            to = view(T, "FW", half, b, b + K)
        else:
            src, to = T[("GL%d" if home else "HL%d") % (stage - 4)][:, 0:1], T["RI%d" % (stage - 4)][:, slot:slot + 1]
        rid, pid = topo.addr(T.cores[s], core)
        jobs.append((DstId(rid=rid, pnc=pid), src, to))
    sem = T.sem[LANDS[stage][half]]
    have = topo.engines(core, T.cores[order[lo]])
    if stage != 1:
        return [RemoteDMATransfer(dst_ids=[j[0] for j in jobs], dma_engine_mask=bits(have), remote_sem=sem,
                                  srcs=[jobs[0][1]], dsts=[j[2] for j in jobs])]
    per = len(have) // cnt
    return [RemoteDMATransfer(dst_ids=[j[0]], dma_engine_mask=bits(have[per * k:per * k + per]), remote_sem=sem, src=j[1], dst=j[2])
            for k, j in enumerate(jobs)]


def helper(g, core, T, topo):
    for r in range(len(T.cores)):
        if core not in topo.cores_of(T.cores[r]):
            continue
        order, plan = ways(T, topo, r)
        sent = 0
        for stage in (0, 1, 4, 2, 5, 3):
            for (h, half, lo, cnt, part) in plan[stage]:
                if h == core:
                    g.wait_ge(T.sem["h%d" % stage], len(topo.engines(T.cores[r], h)) // part)
                    g.remote_dma_fused(writes(T, topo, core, r, order, stage, half, lo, cnt, False), local_sem=T.sem.loc)
                    sent += len(topo.engines(core, T.cores[order[lo]]))
        if sent:
            g.wait_ge(T.sem.loc, sent)


def rank_program(g, core, T, topo):
    me = T.rank_of(core)
    if me is None:
        helper(g, core, T, topo)
        return
    n = len(T.cores)
    OP, FN = AluOpType, ActivationFunctionType
    E = {"v": g.vector, "s": g.scalar, "t": g.tensor, "p": g, "y": g.sync}
    SEM = {"v": "cv", "s": "cs", "t": "ct", "p": "cp"}
    clock = {e: {} for e in E}
    total, recs = {}, {}

    def norm(x):
        return (x[0], 0, 512, 1) if x[0] in BANKS else x

    def meet(a, b):
        if a[1] >= b[2] or b[1] >= a[2]:
            return False
        return not (a[3] == b[3] and a[3] > 1 and (a[1] - b[1]) % a[3])

    def sync(e, reads, writes):
        toks = []
        for kind, xs in (("r", reads), ("w", writes)):
            for x in xs:
                x = norm(x)
                bank = x[0] in BANKS
                for (y, k, tok, who) in recs.get(x[0], []):
                    if bank and who == e == "t":
                        continue
                    if (kind == "w" or k == "w" or (bank and who != e)) and meet(x, y):
                        toks.append(tok)
        best = {}
        for t in toks:
            if clock[e].get(t[0], 0) < t[1] and best.get(t[0], (0, 0))[1] < t[1]:
                best[t[0]] = t
        for s in sorted(best):
            t = best[s]
            if any(o != s and best[o][2].get(s, 0) >= t[1] for o in best):
                continue
            E[e].wait_ge(T.sem[s], t[1])
        for s in best:
            for k in best[s][2]:
                clock[e][k] = max(clock[e].get(k, 0), best[s][2][k])
            clock[e][s] = max(clock[e].get(s, 0), best[s][1])

    def note(e, tok, reads, writes):
        for x in writes:
            x = norm(x)
            old = recs.setdefault(x[0], [])
            if x[3] == 1 and x[0] not in BANKS:
                old[:] = [r for r in old if not (x[1] <= r[0][1] and r[0][2] <= x[2])]
            old.append((x, "w", tok, e))
        for x in reads:
            x = norm(x)
            recs.setdefault(x[0], []).append((x, "r", tok, e))

    def emit(e, fn, reads, writes):
        reads = [x for x in reads if isinstance(x, tuple)]
        sync(e, reads, writes)
        s = SEM[e]
        total[s] = total.get(s, 0) + 1
        fn().then_inc(T.sem[s], 1)
        snap = dict(clock[e])
        snap[s] = total[s]
        note(e, (s, total[s], snap), reads, writes)

    def dma(q, s, pairs, reads, writes):
        sync(q, reads, writes)
        for o, i in pairs:
            E[q].dma_start(o, i).then_inc(T.sem[s], 16)
        total[s] = 16 * len(pairs)
        snap = dict(clock[q])
        snap[s] = total[s]
        note("d", (s, total[s], snap), reads, writes)

    def arrive(s, val, writes):
        total[s] = val
        note("r", (s, val, {s: val}), [], writes)

    def X(name, lo=0, hi=None, st=1):
        if name in ALIAS:
            big, at, w = ALIAS[name]
            return (big, at + lo, at + (w if hi is None else hi), st)
        return (name, lo, SCRATCH[name][1][1] if hi is None else hi, st)

    def ap(x):
        if not isinstance(x, tuple):
            return x
        return T[x[0]][:, x[1]:x[2]] if x[3] == 1 else T[x[0]][:, x[1]:x[2]:x[3]]

    def by(x, off):
        return ap(x) if off is None else ap(x).indirect(ap(off))

    def sc(x):
        return (x[0] + "S", x[1], x[2], x[3])

    def tt(o, a, b, op, off=None):
        emit("v", lambda: g.vector.tensor_tensor(ap(o), by(a, off), ap(b), op), [a, b, off], [o])

    def ts(o, a, s1, op0, s2=None, op1=None):
        if op1 is None:
            emit("v", lambda: g.vector.tensor_scalar(ap(o), ap(a), ap(s1), None, op0), [a, s1], [o])
        else:
            emit("v", lambda: g.vector.tensor_scalar(ap(o), ap(a), ap(s1), ap(s2), op0, op1), [a, s1, s2], [o])

    def tc(o, a, off=None):
        emit("v", lambda: g.vector.tensor_copy(ap(o), by(a, off)), [a, off], [o])

    def tr(o, a):
        emit("v", lambda: g.vector.transpose(ap(o), ap(a)), [a], [o])

    def scan(o, a, b, start, op0, op1):
        emit("v", lambda: g.vector.tensor_tensor_scan(ap(o), ap(a), ap(b), start, op0, op1), [a, b], [o])

    def add_up(o, a, start):
        scan(o, (a[0], a[1], a[1] + 64, 1), (a[0], a[1] + 64, a[2], 1), start, OP.add, OP.add)

    def sct(win, off, a):
        emit("v", lambda: g.vector.tensor_copy(ap(win).indirect(ap(off)), ap(a)), [a, off], [win])

    def act(o, a, f, bias=None, scale=None, acc=None, off=None):
        kw = {}
        if bias is not None:
            kw["bias"] = ap(bias)
        if scale is not None:
            kw["scale"] = ap(scale)
        if acc is not None:
            kw["accum_out"] = ap(acc)
        emit("s", lambda: g.scalar.activation(ap(o), by(a, off), f, **kw), [a, bias, scale, off], [o] + ([acc] if acc is not None else []))

    def quant(o, tile):
        emit("v", lambda: g.vector.quantize_mx(ap(o), ap(sc(o)), ap(tile)), [tile], [o, sc(o)])

    def pick(o, win, off):
        emit("v", lambda: g.vector.tensor_copy(ap(o).bitcast(dt.uint32), ap(win).bitcast(dt.uint32).indirect(ap(off))),
             [win, off], [o])
        emit("s", lambda: g.scalar.activation(ap(sc(o)), ap(sc(win)).indirect(ap(off)), FN.Copy), [sc(win), off], [sc(o)])

    def mm(bank, a, b, start=True, stop=True):
        o = (bank, 0, b[2] - b[1], 1)
        emit("t", lambda: g.tensor.matmul_mx(ap(o), ap(a), ap(sc(a)), ap(b), ap(sc(b)), start, stop),
             [a, sc(a), b, sc(b)], [o])

    def iota(o, pattern, cm=0, base=0):
        emit("p", lambda: g.iota(ap(o), pattern, base, cm), [], [o])

    def fiota(o, pattern, base=0):
        emit("p", lambda: g.iota(ap(o), pattern, base, 0, allow_small_or_imprecise_dtypes=True), [], [o])

    def spread(o, cols):
        for b in range(4):
            act(X(o, b, 512, 4), X("JT", 0, P), FN.Identity, bias=X(cols, b, b + 1), scale=0.0)

    def A(b):
        return X("AQ", P * b, P * b + P)

    peers = [s for s in range(n) if s != me]
    order, plan = ways(T, topo, me)

    def dst(c):
        rid, pid = topo.addr(c, core)
        return DstId(rid=rid, pnc=pid)

    have = topo.engines(core, plan[0][0][0])
    leave = topo.engines(core, T.cores[order[0]])
    stay = [e for e in have if e not in leave]
    ALL = (n - 1) * len(leave)
    total["loc"] = 0

    def call(reads, trs, engines):
        sync("p", reads, [])
        g.remote_dma_fused(trs, local_sem=T.sem.loc)
        total["loc"] += engines

    def deal(stage, jobs, engines, w=0):
        per, trs = len(engines) // len(jobs), []
        for k, (h, half, lo, cnt, part) in enumerate(jobs):
            if stage == 0:
                src, to = T.ET[:, 4 * me:4 * me + 4], T.HE[:]
            elif stage == 1:
                src, to = view(T, "SL", half, 32 * lo, 32 * lo + w), view(T, "H1", half, 32 * lo, 32 * lo + w)
            elif stage < 4:
                src, to = view(T, "NW%d" % (stage - 2), half, P, P + w), view(T, "H%d" % stage, half, 0, w)
            else:
                src, to = T["GL%d" % (stage - 4)][:, 0:1], T["HL%d" % (stage - 4)][:, 0:1]
            trs.append(RemoteDMATransfer(dst_ids=[dst(h)], dma_engine_mask=bits(engines[per * k:per * k + per]),
                                         remote_sem=T.sem["h%d" % stage], src=src, dst=to))
        return trs

    def own_writes(stage, half, lo, cnt):
        return writes(T, topo, core, me, order, stage, half, lo, cnt, True)

    u8 = dt.uint8

    for q, s, lo in (("y", "ln0", 0), ("s", "ln1", 4)):
        for k in range(lo, lo + 4):
            E[q].dma_start(T.NB[16 * k:16 * k + 16, :], T.nb[:]).then_inc(T.sem[s], 16)
        total[s] = 64
    recs["NB"] = [(X("NB"), "w", (s, 64, {s: 64}), "d") for s in ("ln0", "ln1")]
    dma("s", "lu", [(T.ub[:], T.u[:, 0:16])], [], [X("ub")])
    dma("y", "lx", [(T.xb[:], T.x[:])], [], [X("xb")])
    dma("s", "lv", [(T.vb[:], T.v[:, 0:16])], [], [X("vb")])
    dma("y", "lb", [(T.bbb[:], T.bb[:])], [], [X("bbb")])
    dma("y", "la", [(T.ab[:], T.a[:])], [], [X("ab")])

    BIG3 = 2048
    iota(X("PID"), [[0, 1]], 1)
    fiota(X("JT", 0, P), [[1, P]])
    fiota(X("C3"), [[0, 8], [BIG3, 3]])
    fiota(X("SF"), [[0, 144]], -1000)
    for lo, hi in ((0, me), (me, n - 1)):
        if lo < hi:
            fiota(X("BROW", 32 * lo, 32 * hi), [[P, hi - lo], [0, 32]], P * peers[lo])
    fiota(X("CNB"), [[1, 3], [96, 4], [0, 2]])
    fiota(X("DUP"), [[1, 8], [0, 2]])
    ts(X("PM16i"), X("PID"), 15, OP.bitwise_and)
    ts(X("PM32i"), X("PID"), 31, OP.bitwise_and)
    ts(X("W3"), X("PM16i"), 1.0 / 3, OP.mult, -1.0 / 3, OP.add)
    ts(X("PMK"), X("PM16i"), float(BIG3), OP.mult)
    tc(X("PM16"), X("PM16i"))
    ts(X("R3"), X("W3"), -3.0 * BIG3, OP.mult, X("PMK"), OP.add)
    tc(X("PM32"), X("PM32i"))
    ts(X("MASK"), X("C3"), X("R3"), OP.add, 2.0 * BIG3, OP.is_equal)
    ts(X("P3"), X("PID"), 3.0, OP.mult, 2.0, OP.add)
    for w in (P, 2 * P, 4 * P):
        act(X("JT", w, 2 * w), X("JT", 0, w), FN.Identity, bias=float(w))
    spread("UT", "ub")

    FO = X("FS", 2, 24, 3)
    tt(X("A24"), X("NB"), X("MASK"), OP.mult)
    ts(X("NCI"), X("JT", 0, P, 16), X("PM16"), OP.add, -1.0 / P, OP.mult)
    scan(X("FS"), X("C3"), X("A24"), 0.0, OP.min, OP.add)
    ts(X("PLK"), X("JT", 0, P), 1.0 / P, OP.mult)
    tc(X("FOU"), FO)
    tt(X("NGO"), X("NCI"), FO, OP.subtract)
    ts(X("P3i"), X("P3"), 15, OP.bitwise_and)
    tc(X("NBU"), X("NB"))
    tt(X("GR"), X("JT"), X("PLK"), OP.add, off=X("FOU"))
    for t in range(7):
        act(X("JK1", P * t, P * t + P), X("GR"), FN.Sign, bias=X("NGO", t, t + 1), acc=X("RS1", 64 * t + 63, 64 * t + 64))
    act(X("FRF"), X("JT"), FN.Identity, bias=-63.5, off=X("FOU"))
    quant(X("NW0", 0, P), X("xb"))
    quant(X("UQ"), X("UT"))
    mm("EB", X("UQ"), X("NW0", 0, P))
    ts(X("GO", 7, 8), X("NGO", 7, 8), -1.0, OP.mult)
    tr(X("ETR"), X("EB", 0, P))
    ts(X("CMR", 0, P), X("GR"), X("GO", 7, 8), OP.is_lt, -2.0, OP.mult)
    own = X("ET", 4 * me, 4 * me + 4)
    tc(own, X("ETR", 0, P, 32))
    call([own], deal(0, plan[0], have), len(have))
    for lo, hi in ((0, 4 * me), (4 * me + 4, 32)):
        if lo < hi:
            arrive("ee", ALL, [X("ET", lo, hi)])
    add_up(X("RS1", 448, 512), X("CMR", 0, P), P - 1.0)
    ts(X("TAU", 0, 7), X("BROW", 0, 224, 32), X("PM32"), OP.add, -0.5, OP.add)
    ts(X("RU"), X("RS1", 63, 512, 64), -0.5, OP.mult, 63.5, OP.add)
    ts(X("NTAU", 0, 7), X("TAU", 0, 7), -1.0, OP.mult)
    sct(X("SF", 8, 136), X("RU"), X("FRF"))
    ts(X("P3f"), X("P3i"), X("PM32"), OP.add, X("PM16"), OP.subtract)
    BIG = 1.5 * 2.0 ** 30
    act(X("AB1"), X("SF", 8, 136), FN.Identity, bias=BIG)
    act(X("AB"), X("AB1"), FN.Identity, bias=-BIG)
    tt(X("NEQ"), X("SF", 8, 136), X("SF", 7, 135), OP.not_equal)
    ts(X("EXO"), X("DUP", 0, 8), 1.0, OP.mult)
    scan(X("KAP"), X("NEQ"), X("AB"), -1.0, OP.add, OP.max)
    NS = 4
    for i in range(NS):
        act(X("JK2", P * i, P * i + P), X("KAP"), FN.Sign, bias=X("NTAU", i, i + 1), acc=X("RS2", 64 * i + 63, 64 * i + 64))
    for i in range(NS, n - 1):
        ts(X("CMR", P * (i - NS), P * (i - NS) + P), X("KAP"), X("TAU", i, i + 1), OP.is_lt, -2.0, OP.mult)
    for i in range(NS, n - 1):
        add_up(X("RS2", 64 * i, 64 * i + 64), X("CMR", P * (i - NS), P * (i - NS) + P), float(P))
    act(X("M3"), X("PM32"), FN.Copy, scale=3.0)
    act(X("NBR"), X("JT"), FN.Copy, off=X("NBU"))
    for d in range(2):
        ts(X("PU", d, 14, 2), X("RS2", 63, 448, 64), -0.5, OP.mult, 64.0, OP.add)
    ts(X("LABD"), X("DUP", 0, 8), 32.0, OP.mult, X("PM32"), OP.add)
    tt(X("RLD"), X("SF", 8, 144), X("BROW"), OP.subtract, off=X("PU"))
    ts(X("SO"), X("DUP", 0, 8), 32.0, OP.mult, X("P3f"), OP.add)
    tr(X("RLT"), X("RLD"))
    ts(X("CN"), X("CNB"), X("M3"), OP.add)
    ts(X("RQ"), X("RLT", 0, 224, 16), 63.5, OP.add, P - 1.0, OP.min)
    two = len(leave) // 4
    for sem, land, lo, hi in (("rqa", "RQA", 3, 7), ("rqb", "RQB", 0, 3)):
        trs = []
        for k, s in enumerate(order[lo:hi]):
            i, at = peers.index(s), 2 * (ways(T, topo, s)[0].index(me) - lo)
            trs.append(RemoteDMATransfer(dst_ids=[dst(T.cores[s])], dma_engine_mask=bits(leave[two * k:two * k + two]),
                                         remote_sem=T.sem[sem], src=T.RQ[:, 2 * i:2 * i + 2], dst=T[land][:, at:at + 2]))
        call([X("RQ")], trs, two * (hi - lo))
        arrive(sem, two * (hi - lo), [X(land)])
    fiota(X("IO16"), [[0, 2], [1, 16]])
    fiota(X("R0"), [[0, 4], [1, 32]])

    act(X("ND"), X("NBR"), FN.Copy, off=X("CN"))
    quant(X("AQ"), X("ab"))
    quant(X("BBQ"), X("bbb"))
    ts(X("ID32"), X("JT", 0, 32), X("PM32"), OP.is_equal)
    BELOW = 1.0 - 2.0 ** -24
    ts(X("CK0"), X("JT", 0, 32), X("PM32"), OP.is_lt, -2.0 ** -24, OP.mult)
    act(X("NVC"), X("vb", 0, 4), FN.Copy, scale=-1.0)
    spread("VT", "NVC")
    tr(X("NT"), X("ND"))
    tr(X("FT"), X("NBR", 2, 384, 3))
    tc(X("NO"), X("NT", 256, 384, 16))
    ts(X("LN"), X("NT", 0, 256, 16), float(-P * me), OP.add)
    ts(X("QOI"), X("NO"), 31, OP.bitwise_and)
    ts(X("COI"), X("NO"), 5, OP.arith_shift_right)
    tc(X("QO"), X("QOI"))
    tc(X("CO"), X("COI"))
    act(X("MSK"), X("ID32"), FN.Copy, off=X("QO"))

    def near(win, close):
        pick(X("PZ", 0, 256), win, X("LN"))
        for h in range(2):
            mm("Z", X("UQ"), X("PZ", P * h, P * h + P), h == 0, close and h == 1)
        for b in range(4):
            for h in range(2):
                mm("S%d" % b, A(b), X("PZ", P * h, P * h + P), h == 0, False)

    def answer(half, i, engines):
        return RemoteDMATransfer(dst_ids=[dst(T.cores[order[i]])], dma_engine_mask=bits(engines), remote_sem=T.sem[LANDS[1][half]],
                                 src=view(T, "SL", half, 32 * i, 32 * i + LC), dst=view(T, "FW", half, P * me, P * me + LC))

    pick(X("SL", 96, 224), X("NW0", 0, P), X("RQA"))
    call([X("SL", 96, 224)], deal(1, plan[1][:2], stay, 32 + LC), len(stay))
    call([X("SLS", 96, 224)], deal(1, plan[1][2:], leave, P), len(leave))
    quant(X("VQ"), X("VT"))
    mm("FB0", X("VQ"), X("BBQ"))
    near(X("NW0", 0, P), True)
    tc(X("FG"), X("FT", 0, P, 16))
    tr(X("NFT"), X("FB0", 0, P))
    pick(X("SL", 0, 96), X("NW0", 0, P), X("RQB"))
    for half, w in enumerate(("SL", "SLS")):
        call([X(w, 0, 96)], [answer(half, 0, leave[:2 * two]), answer(half, 1, leave[2 * two:])], len(leave))
        call([], [answer(half, 2, leave)], len(leave))
    arrive("rc", 2 * len(leave) + 4 * 2 * two, [X("FW", 0, 1024)])
    arrive("rs", 2 * len(leave) + 4 * two, [X("FWS", 0, 1024)])
    fiota(X("NPB"), [[0, R], [1, P]])
    fiota(X("UPD"), [[0, 1024]], -2048)
    tr(X("E1T"), X("Z", 0, P))

    act(X("PIO"), X("KAP"), FN.Copy, off=X("RU"))
    act(X("R32"), X("R0"), FN.Sign)
    act(X("PD0"), X("PIO"), FN.Identity, bias=1.0 - FAR[0], off=X("SO"))
    act(X("CK"), X("CK0"), FN.Identity, bias=1.0)
    act(X("LAB"), X("JT", 0, P, 32), FN.Identity, bias=X("PM32"))
    act(X("Q4"), X("JT", 0, 4), FN.Copy, scale=0.25)
    tt(X("EG"), X("ET"), X("MSK"), OP.mult, off=X("CO"))
    tr(X("EGT"), X("EG"))
    scan(X("ES"), X("R32"), X("EGT"), 0.0, OP.mult, OP.add)
    tt(X("ZA"), X("E1T", 0, P, 32), X("ES", 31, P, 32), OP.add)
    tt(X("ZT"), X("ZA"), X("NFT", 0, P, 32), OP.add)

    def far_list(t):
        tr(X("PT"), X("PD%d" % t))
        ts(X("LF"), X("PT", 0, P, 16), FAR[0] - 1.0, OP.add)

    def outside(k):
        ts(X("CM", P * k, P * k + 96), X("RW", 32 * k + 32, 32 * k + P), X("TR", 32 * k, 32 * k + 1), OP.is_ge)

    def label(k):
        ts(X("MM", 32 * k, 32 * k + 32), X("IO16"), X("CT", k, k + 1) if k else X("CW", 63, 64), OP.is_equal, X("LAB", k, k + 1), OP.mult)

    def scaled(b):
        act(X("T3", P * b, P * b + P), X("S%d" % b, 0, P), FN.Copy, scale=c05)

    def far_sums():
        for b in range(4):
            mm("S%d" % b, A(b), X("PZ", 256, 384), False, True)

    TINY = 2.0 ** -124
    c05 = float(np.float32(0.05))
    for t in range(R):
        fw, NW = FAR[t], "NW%d" % t
        row, far = X("RW", P, 256), X("PZ", 256, 384)
        if t == 0:
            act(X("TR"), X("ZT"), FN.Abs, bias=TINY, off=X("EXO"))
            far_list(0)
            tr(row, X("TR"))
        else:
            pick(far, X("FW", 0, fw), X("LF"))
            mm("Z", X("UQ"), far, False, False)
            mm("Z", X("VQ"), X("BBQ"), False, True)
            far_sums()
            act(row, X("Z", 0, P), FN.Abs, bias=TINY)
            tr(X("TR"), row)
            act(X("RW", 32, P), X("Z", 32, P), FN.Abs, scale=BELOW)
        for k in (3, 2, 1, 0):
            act(X("SP", 32 * k, 32 * k + 32), X("CK"), FN.Identity, scale=X("TR", 32 * k, 32 * k + 1))
            if t == 0 and k == 3:
                act(X("RW", 32, P), X("RW", P + 32, 256), FN.Copy, scale=BELOW)
        outside(3)
        for k in (3, 2, 1, 0):
            a, c = 32 * k, P * k
            if k:
                outside(k - 1)
            tt(X("CM", c + 96, c + P), X("RW", P + a, P + a + 32), X("SP", a, a + 32), OP.is_gt)
            if k:
                act(X("JK3", c - P, c), X("CM", c, c + P), FN.Identity, acc=X("CT", k, k + 1))
        label(3)
        add_up(X("CW"), X("CM", 0, P), 0.0)
        if t:
            for b in range(4):
                scaled(b)
        for k in (2, 1, 0):
            label(k)
        if t == 0:
            pick(far, X("FW", 0, fw), X("LF"))
            far_sums()
        tr(X("MT"), X("MM"))
        add_up(X("IW"), X("MT"), 0.0)
        ix, mine, held = X("IW", 63, 64), X("OF", 0, 1), X("NPB", P * t, P * t + P)
        if t < R - 1:
            ts(X("GL%d" % t, 0, 1), ix, float(P * me), OP.add)
            call([X("GL%d" % t, 0, 1)], deal(4 + t, plan[4 + t], have), len(have))
            call([], own_writes(4 + t, 0, n - 2, 1), len(leave))
        ts(X("BO"), X("Q4"), ix, OP.add, 4.0, OP.mult)
        if t == 0:
            scaled(0)
        act(X("BG"), X("bbb"), FN.Copy, off=X("BO"))
        tc(mine, ix)
        if t == 0:
            ts(X("T3", P, 2 * P), X("S1", 0, P), c05, OP.mult)
            scaled(2)
        sct(held, mine, X("JT", P, P + K))
        if t == 0:
            ts(X("T3", 3 * P, 4 * P), X("S3", 0, P), c05, OP.mult)
        act(X("CD"), held, FN.Copy, off=X("LABD"))
        act(X("NDB", K * t, K * t + K), X("JT", 0, P), FN.Copy, off=mine)
        if t == R - 1:
            dma("y", "on", [(T.nd[:], T.NDB[0:1, :])], [X("NDB")], [])
        for b in range(4):
            tt(X("xb", b, 64, 4), X("T3", P * b, P * b + P), X("BG", K * b, K * b + K), OP.add, off=mine)
        if t == R - 1:
            tr(X("CDT"), X("CD"))
        quant(X(NW, P, 256), X("xb"))
        if t < R - 1:
            jobs = plan[2 + t]
            call([X(NW, P, P + K)], deal(2 + t, jobs[:2], have, K), len(have))
            call([X(NW + "S", P, P + 4 * K)], own_writes(2 + t, 0, n - 2, 1) + deal(2 + t, jobs[2:3], stay, 4 * K), len(have))
            call([], own_writes(2 + t, 1, 1, 4) + deal(2 + t, jobs[3:], stay, K), len(have))
            tr(X("CDT"), X("CD"))
        tc(X("LCU"), X("CDT", 0, P, 16))
        if t < R - 1:
            nxt = X("NW%d" % (t + 1), 0, P)
            pick(nxt, X(NW), X("LCU"))
            near(nxt, False)
            if t:
                quant(X("WQ"), X("wb"))
            arrive("li%d" % t, ALL, [X("RI%d" % t, 0, 7)])
            sct(X("UPD"), X("RI%d" % t, 0, 7), X("JT", fw - FAR[0] + 1, fw - FAR[0] + 113))
            tt(X("PD%d" % (t + 1)), X("UPD"), X("PD%d" % t), OP.max, off=X("FG"))
            far_list(t + 1)
            arrive("cd%d" % t, ALL, [X("FW", fw, fw + 112)])
            arrive("sc%d" % t, ALL, [X("FWS", fw, fw + 112)])
            if t == 0:
                dma("y", "lw", [(T.wb[:], T.w[:])], [X("FW", fw, fw + 112)], [X("wb")])
        else:
            pick(X("FIN"), X(NW), X("LCU"))
            mm("Y", X("WQ"), X("FIN"))
            dma("y", "oc", [(T.oc[:], T.FIN[:].bitcast(u8))], [X("FIN")], [])
            dma("y", "os", [(T.osc[4 * k:4 * k + 4, :], T.FINS[32 * k:32 * k + 4, :]) for k in range(4)], [X("FINS")], [])
            tc(X("YS"), X("Y", 0, P))
            dma("s", "oy", [(T.y[:], T.YS[:])], [X("YS")], [])
    for s in total:
        if clock["p"].get(s, 0) < total[s]:
            g.wait_ge(T.sem[s], total[s])
